import numpy as np, ml_dtypes
CORES = [10,34,74,98]
N = 4
import mx_ref
BF = ml_dtypes.bfloat16
def gcols(t, e):
    v = np.concatenate([t.reshape(8, 16, -1, 4), np.zeros((8, 16, 1, 4), BF)], axis=2)
    return np.ascontiguousarray(np.stack([v[g][:, e[g]] for g in range(8)])).reshape(128, -1)
def tile(rs):
    return np.stack(rs, axis=2).reshape(128, -1).astype(BF)
def pick(q, e):
    c = np.concatenate([q[0].reshape(128, -1, 4), np.zeros((128, 1, 4), np.uint8)], axis=1); s = np.concatenate([q[1], np.ones((16, 1), np.uint8)], axis=1)
    return (np.ascontiguousarray(c[:, e].reshape(128, -1)), np.ascontiguousarray(s[:, e]))
def join(*qs):
    return (np.concatenate([q[0] for q in qs], axis=1), np.concatenate([q[1] for q in qs], axis=1))
def put(q, e, v):
    c, s = q[0].reshape(128, -1, 4).copy(), q[1].copy(); c[:, e] = v[0].reshape(128, -1, 4); s[:, e] = v[1]
    return (c.reshape(128, -1), s)
def pk(c, s):
    return (np.ascontiguousarray(c), mx_ref.live(s))
def emit(q):
    return q[0], q[1]
def packed(v, rng):
    q = [mx_ref.quantize(np.ascontiguousarray(v[r])) for r in range(N)]
    return np.stack([a for a, b in q]), np.stack([mx_ref.plane(b, rng) for a, b in q])
def f(rng, *shape):
    return mx_ref.flush((rng.standard_normal(shape, dtype=np.float32) * np.exp2(rng.integers(-2, 3, shape[:-1] + (1,)))).astype(BF))
def wide(rng, *shape, cols=0):
    v = rng.standard_normal(shape, dtype=np.float32) * np.exp2(rng.integers(-12, 13, shape)).astype(np.float32)
    if cols: v *= np.repeat(np.exp2(rng.integers(-cols, cols + 1, shape[:-2] + (1, shape[-1] // 4))) * (rng.random(shape[:-2] + (1, shape[-1] // 4)) > 0.0625), 4, axis=-1).astype(np.float32)
    return mx_ref.flush(v.astype(BF))
C, K, R = 512, 160, 3
def lowest(p):
    return np.argsort(p[::16] + np.float32(0.0), axis=1, kind="stable")[:, :K]
def gput(t, e, s):
    o, w = t.reshape(8, 16, -1, 4).copy(), s.reshape(8, 16, -1, 4)
    for g in range(8): o[g][:, e[g]] = w[g]
    return o.reshape(128, -1)
def numbers_of(rng):
    return {"x": np.array(f(rng, N, 128, 4 * C)), "a": np.array(f(rng, N, 128, 4 * K)), "u": np.array(f(rng, N, 128, 512)), "v": np.array(f(rng, N, 128, 512))}
def weights(rng, w):
    c, p = packed(w, rng)
    return {"wc": c, "ws": p}
def still(rng):
    w = np.zeros((N, 128, 4, 128, 4), np.float32)
    i = np.arange(128)
    for b in range(4): w[:, i, b, i, b] = 32
    return weights(rng, w.reshape(N, 128, 2048).astype(BF))
def signs(rng):
    return np.stack([rng.permutation(8) % 2 * 2.0 - 1.0 for r in range(N)])
def digits(rng, t, s):
    x = t.astype(np.float32).reshape(N, 8, 16, -1, 4)
    b = ((s[..., None] >> np.arange(8)) & 1) * np.exp2(np.arange(8) - 23.0)
    x[:, :, 0] = 0
    x[:, :, 0, :, 0] = 1
    x[:, :, 8] = b[..., :4]
    x[:, :, 9] = b[..., 4:]
    z = x[:, :, 10:].shape
    x[:, :, 10:] = rng.integers(4, 8, z) * rng.choice([-1.0, 1.0], z) * 2.0 ** -20
    return x.reshape(t.shape).astype(BF)
def setup_inputs(rng):
    return {**numbers_of(rng), **weights(rng, f(rng, N, 128, 2048))}
def setup_inputs_ties(rng):
    d = numbers_of(rng)
    e = rng.permutation(N)
    for n in ("x", "a"):
        x = d[n].reshape(N, 8, 16, -1, 4)
        for r in range(N):
            k = rng.permutation(x.shape[3]) % 3
            if n == "x" and r == e[0]: k = np.zeros(C, int)
            p = x[r][:, :8, :3].copy()
            p[:, :, 2] = 0
            x[r][:, :8] = p[:, :, k]
        if n == "x": x[e[1]] = 0
        d[n] = x.reshape(N, 128, -1)
    u = d["u"].reshape(N, 8, 16, 128, 4)
    u[:, :, 8:, ::16] = 0
    w = np.array(f(rng, N, 128, 2048)).reshape(N, 8, 16, 4, 8, 16, 4)
    w[:, :, 8:, :, :, :8] = 0
    return {"x": d["x"], "a": d["a"], "u": u.reshape(N, 128, 512), "v": d["v"], **weights(rng, w.reshape(N, 128, 2048))}
def setup_inputs_near(rng):
    d = numbers_of(rng)
    turn = (1.0 - 2.0 * (np.arange(N) % 2))[:, None]
    g = signs(rng)[:1] * turn
    h = rng.choice([-1.0, 1.0], 8)[None, :] * turn
    size = np.where(signs(rng) > 0, 1.0, 2.0 ** -28)
    shift = np.stack([2 + 2 * rng.permutation(C // 2 - K - 1)[:8] for r in range(N)])
    shift[np.arange(N), np.argmax(g, axis=1)] = 0
    q = (C - 1 - np.arange(C) - shift[:, :, None]) % C // 2
    k = K // 2 + (K - np.arange(K)) // 2 + np.zeros((N, 8, 1), int)
    up = h[:, :, None] > 0
    d["x"] = digits(rng, d["x"], np.where(up, q, C // 2 - 1 - q))
    d["a"] = digits(rng, d["a"], np.where(up, k, C // 2 - 1 - k))
    far = np.where(g > 0, np.argmax(q, axis=2), np.argmin(q, axis=2))
    x = d["x"].reshape(N, 8, 16, C, 4)
    x[np.arange(N)[:, None], np.arange(8)[None, :], 0, far, 0] = 4096
    g = (g * size).astype(np.float32).astype(BF)
    h = (h * size).astype(np.float32).astype(BF)
    u = d["u"].reshape(N, 128, 128, 4)
    u[:, :, ::16] = 0
    for i in range(8):
        u[:, 16 * i, 16 * i, 0] = g[:, i]
        u[:, 16 * i + 8:16 * i + 10, 16 * i] = h[:, i, None, None]
    return {"x": x.reshape(N, 128, 4 * C), "a": d["a"], "u": u.reshape(N, 128, 512), "v": d["v"], **still(rng)}
def setup_inputs_huge(rng):
    d = numbers_of(rng)
    both = rng.permutation(N) % 2 == 0
    k = np.stack([rng.permutation(C) % 2 for r in range(N)])
    k[~both] = -1
    x = 2.0 ** 30 * (0.6 + 0.4 * rng.random((N, 8, 16, C, 4)))
    x[:, :, :8] *= np.where(k == 1, 2.0 ** -6, 1.0)[:, None, None, :, None]
    x[:, :, 8:] *= np.where(k == 0, 2.0 ** -6, 1.0)[:, None, None, :, None]
    a = 2.0 ** 30 * (0.6 + 0.4 * rng.random((N, 128, 4 * K)))
    s = np.ones((N, 8, 16, 1, 1))
    s[both, :, 8:] = -1
    s = s * signs(rng)[:, None, None, :, None] * 2.0 ** 30 * (1 - 0.25 * rng.random((N, 8, 16, 8, 4)))
    u = d["u"].reshape(N, 8, 16, 128, 4)
    u[:, :, :, ::16] = s.astype(np.float32).astype(BF)
    return {"x": x.astype(np.float32).reshape(N, 128, 4 * C).astype(BF), "a": a.astype(np.float32).astype(BF), "u": u.reshape(N, 128, 512), "v": d["v"], **still(rng)}
def setup_inputs_spread(rng):
    d = setup_inputs(rng)
    d["x"] = wide(rng, N, 128, 4 * C, cols=6)
    d["a"] = wide(rng, N, 128, 4 * K, cols=6)
    return d
def check_inputs(d):
    b = []
    for k in ("x", "a", "u", "v"):
        z = np.abs(d[k].astype(np.float32))
        if not (np.isfinite(z).all() and ((z == 0) | (z >= 2.0 ** -30) & (z <= 2.0 ** 30)).all()): b.append("a value of " + k)
    top = np.max((d["wc"] & 127).reshape(N, 16, 8, -1, 4), axis=(2, 4))
    s = np.stack([mx_ref.live(p) for p in d["ws"]])
    if (top == 127).any(): b.append("a code of wc")
    if not ((top == 0) & (s == 1) | (top > 0) & (s >= 88) & (s <= 157)).all(): b.append("a scale of ws")
    return b
def reference(x, a, u, v, wc, ws):
    qu = [mx_ref.quantize(u[r]) for r in range(N)]
    lay = [pk(wc[r], ws[r]) for r in range(N)]
    now = [x[r] for r in range(N)]
    came = [mx_ref.quantize(a[r]) for r in range(N)]
    for t in range(R):
        o, gone = [], []
        for r in range(N):
            o.append(lowest(mx_ref.matmul(qu[r], mx_ref.quantize(now[r]))))
            gone.append(mx_ref.quantize(gcols(now[r], o[r])))
            e = tile([np.maximum(mx_ref.matmul(pick(lay[r], np.arange(128 * b, 128 * b + 128)), came[r]), np.float32(0.0)) * np.float32(0.03125) for b in range(4)])
            now[r] = gput(now[r], o[r], e)
        came = [gone[(r - 1) % N] for r in range(N)]
    y, ol = np.zeros((N, 128, C), np.float32), np.zeros((N, 8, K), np.float32)
    oc, osc = np.zeros((N, 128, 4 * C), np.uint8), np.zeros((N, 16, C), np.uint8)
    for r in range(N):
        q = mx_ref.quantize(now[r])
        y[r] = mx_ref.matmul(mx_ref.quantize(v[r]), q)
        ol[r] = o[r]
        oc[r], osc[r] = emit(q)
    return {"y": y, "ol": ol, "oc": oc, "osc": osc}

@@ -1,0 +1,399 @@
+from concourse.mybir import dt, AluOpType, ActivationFunctionType
+
+C, K, R, NR = 512, 160, 3, 4
+NV = 15
+RS = 4
+GV1, GV0 = 3, 0
+VG, QP = 9, 8
+EW = 4 * K
+H2 = C // 2
+SL = 18
+BIG = 2e29
+CHUNKS = ((240, 352), (352, 464), (464, 512), (128, 240), (32, 128), (0, 32))
+CST = 1088
+STAGES = ((256, 512, 256, 544), (32, 256, 64, 256), (0, 32, 0, 64))
+Q8 = "float8_e4m3fn_x4"
+
+SCRATCH = {
+    "ub": ("sbuf", [128, 512], "bfloat16"), "uq": ("sbuf", [128, 128], Q8), "us": ("sbuf", [128, 128], "uint8"),
+    "urq": ("sbuf", [128, 128], Q8), "urs": ("sbuf", [128, 128], "uint8"),
+    "vb": ("sbuf", [128, 512], "bfloat16"), "vq": ("sbuf", [128, 128], Q8), "vs": ("sbuf", [128, 128], "uint8"),
+    "ab": ("sbuf", [128, EW], "bfloat16"),
+    "wq": ("sbuf", [128, 512], Q8), "wp": ("sbuf", [128, 512], "uint8"),
+    "xfin": ("sbuf", [128, 4 * C], "bfloat16"),
+    "pcol": ("sbuf", [128, 1], "int32"), "pint": ("sbuf", [128, 4], "int32"), "pf": ("sbuf", [128, 6], "float32"),
+    "uoi": ("sbuf", [128, 8], "int32"), "uoff": ("sbuf", [128, 8], "uint16"),
+    "i16": ("sbuf", [128, C + 32], "bfloat16"), "i4": ("sbuf", [128, K], "bfloat16"), "places": ("sbuf", [128, C], "float32"),
+    "jb": ("sbuf", [128, 32], "float32"), "i3": ("sbuf", [128, 96], "float32"), "k3": ("sbuf", [128, 96], "float32"),
+    "nb": ("sbuf", [128, 32], "float32"), "nn": ("sbuf", [128, 32], "float32"),
+    "mh": ("sbuf", [128, H2], "bfloat16"), "mt": ("sbuf", [128, H2], "bfloat16"), "kt": ("sbuf", [128, H2], "bfloat16"),
+    "k0": ("sbuf", [128, C + 32], "bfloat16"),
+    "m4": ("sbuf", [128, K], "bfloat16"), "k4": ("sbuf", [128, K], "bfloat16"),
+    "msk": ("sbuf", [128, C], "float32"), "hh": ("sbuf", [128, C], "float32"),
+    "cb": ("sbuf", [128, SL * C], "bfloat16"), "sg": ("sbuf", [128, 20 * H2], "bfloat16"),
+    "jk": ("sbuf", [128, 8 * H2], "bfloat16"),
+    "ro": ("sbuf", [128, 16 * 128], "float16"), "ds": ("sbuf", [128, C], "float16"),
+    "co": ("sbuf", [128, CST * len(CHUNKS)], "float16"), "tin": ("sbuf", [128, C + 32], "bfloat16"),
+    "t1": ("sbuf", [128, C], "bfloat16"), "t2": ("sbuf", [128, C + 32], "bfloat16"),
+    "u1": ("sbuf", [128, C], "float16"), "u2": ("sbuf", [128, C + 32], "float16"),
+    "a1": ("sbuf", [128, 32], "float32"), "a2": ("sbuf", [128, 32], "float32"),
+    "dn": ("sbuf", [128, 32], "float32"), "b1": ("sbuf", [128, 32], "float32"),
+    "x3": ("sbuf", [128, 96], "float32"), "p3": ("sbuf", [128, 96], "float32"),
+    "z2": ("sbuf", [128, 64], "float32"), "d2": ("sbuf", [128, 64], "float32"), "i2": ("sbuf", [128, 64], "float32"),
+    "soff": ("sbuf", [128, 128], "uint16"), "roff": ("sbuf", [128, 32], "uint16"), "voff": ("sbuf", [128, 40], "uint16"),
+    "lst": ("sbuf", [128, C], "float32"), "lm": ("sbuf", [128, K], "float32"), "lz": ("sbuf", [128, K], "float32"),
+    "ysb": ("sbuf", [128, C], "float32"),
+    "ps1": ("psum", [128, 512], "float32"), "ps2": ("psum", [128, 1024], "float32"), "psa": ("psum", [128, 512], "float32"),
+}
+for _b in range(4):
+    SCRATCH["pr%d" % _b] = ("psum", [128, 512], "float32")
+for _t in range(R):
+    SCRATCH["win%d" % _t] = ("sbuf", [128, EW + 4 * C], "bfloat16")
+    SCRATCH["inq%d" % _t] = ("sbuf", [128, K], Q8)
+    SCRATCH["ins%d" % _t] = ("sbuf", [128, K], "uint8")
+for _t in range(R + 1):
+    SCRATCH["xq%d" % _t] = ("sbuf", [128, C], Q8)
+    SCRATCH["xs%d" % _t] = ("sbuf", [128, C], "uint8")
+for _t in range(R - 1):
+    SCRATCH["vic%d" % _t] = ("sbuf", [128, EW], "bfloat16")
+    SCRATCH["pq%d" % _t] = ("sbuf", [128, K], Q8)
+    SCRATCH["ps%dc" % _t] = ("sbuf", [128, K], "uint8")
+
+SEMAPHORES = ["lu", "lxa", "lxb", "la", "lw", "lv", "io1", "io2", "io3", "io4", "c0", "c1", "c2", "c3", "c3a", "c4", "c5", "c6",
+              "qa", "qb", "qin", "qv", "sa", "s1", "s2", "s2w", "rr", "mka", "mkb", "ha", "hb", "dd", "dsc", "dns",
+              "cma", "rsc", "sga", "sgb", "ac0", "ac1", "ac2", "ac3", "ac4", "ac5", "acr", "ee",
+              "ck0", "ck1", "ck2", "ck3", "ck4", "ck5", "df0", "df1", "df2", "tr0", "tr1", "tr2",
+              "us", "b1s", "la1", "l1", "l2", "l2r", "l3", "l40", "l41", "l42", "l43",
+              "ga", "gb", "sct", "lms", "lzs", "vo", "vg", "qp", "arr1", "arr2", "sent",
+              "ya", "yb", "yca", "ycb", "st1", "st2"]
+
+
+def rank_program(g, core, T, topo):
+    rank = T.rank_of(core)
+    if rank is None:
+        return
+    A, F = AluOpType, ActivationFunctionType
+    V, S, PE, SY = g.vector, g.scalar, g.tensor, g.sync
+    queues = {"g": g, "v": V, "s": S, "p": PE, "y": SY}
+    nxt = T.cores[(rank + 1) % NR]
+    prv = T.cores[(rank - 1) % NR]
+    rid, pid, _se = topo.addr(nxt)
+    emask = topo.mask(core, nxt)
+    n_out, n_in = len(topo.engines(core, nxt)), len(topo.engines(prv, core))
+    cnt, seen = {}, {}
+
+    def ev(name, ins, n=1):
+        ins.then_inc(T.sem[name], n)
+        cnt[name] = cnt.get(name, 0) + n
+
+    def w(q, *names):
+        for name in names:
+            if seen.get((q, name), 0) < cnt.get(name, 0):
+                queues[q].wait_ge(T.sem[name], cnt[name])
+                seen[(q, name)] = cnt[name]
+
+    def state(t):
+        return (T["win%d" % t], EW) if t < R else (T.xfin, 0)
+
+    def quant_half(t, h):
+        buf, o = state(t)
+        ev("qb" if h else "qa", V.quantize_mx(T["xq%d" % t][:, h * H2:(h + 1) * H2], T["xs%d" % t][:, h * H2:(h + 1) * H2],
+                                              buf[:, o + 4 * h * H2:o + 4 * (h + 1) * H2]))
+
+    def own_scores(h, src, wait):
+        lo, hi = h * H2, (h + 1) * H2
+        w("v", wait)
+        ev("mkb" if h else "mka", V.tensor_tensor(T.msk[:, lo:hi], src, T.mt[:], A.min))
+        w("v", "mkb" if h else "mka")
+        ev("hb" if h else "ha", V.tensor_tensor_scan(T.hh[:, lo:hi], T.kt[:], T.msk[:, lo:hi], 0.0, A.min, A.max))
+
+    def scores(t, out, lo, hi, name):
+        ev(name, PE.matmul_mx(out, T.urq[:], T.urs[:], T["xq%d" % t][:, lo:hi], T["xs%d" % t][:, lo:hi], True, True))
+
+    def gather_half(t, h, q, es):
+        buf, o = state(t + 1)
+        for e in es:
+            w(q, "l4%d" % e)
+            out = buf[:, o + 4 * h * H2 + e:o + 4 * (h + 1) * H2:4]
+            src = T["win%d" % t][:, 0:EW + 4 * C].indirect(T.soff[:, 32 * e + 16 * h:32 * e + 16 * h + 16])
+            ev("gb" if h else "ga", S.activation(out, src, F.Copy) if q == "s" else V.tensor_copy(out, src))
+
+    def listing():
+        w("v", "l2r", "io4")
+        ev("sct", V.tensor_copy(T.lst[:, 0:C].indirect(T.roff[:, 0:32]), T.places[:]))
+
+    def slot(c, lo, hi):
+        return T.cb[:, SL * lo + c % 16:SL * hi:SL]
+
+    def own(c):
+        return T.hh[:, 16 * c + 15:16 * c + 16]
+
+    ev("lu", SY.dma_start(T.ub[:], T.u[:]), 16)
+    ev("lxb", S.dma_start(T.win0[:, EW + 4 * H2:EW + 4 * C], T.x[:, 4 * H2:4 * C]), 16)
+    ev("lxa", SY.dma_start(T.win0[:, EW:EW + 4 * H2], T.x[:, 0:4 * H2]), 16)
+    w("y", "lxa")
+    ev("la", SY.dma_start(T.ab[:], T.a[:]), 16)
+    ev("lw", SY.dma_start(T.wq[:].bitcast(dt.uint8), T.wc[:]), 16)
+    ev("lw", SY.dma_start(T.wp[:], T.ws[:]), 16)
+    ev("lv", SY.dma_start(T.vb[:], T.v[:]), 16)
+
+    def count_up(name, out, pattern, base):
+        ev(name, g.iota(out, pattern, base, 0, allow_small_or_imprecise_dtypes=True))
+
+    ev("io1", g.iota(T.pcol[:], [[0, 1]], 0, 1))
+    ev("io1", g.iota(T.uoi[:], [[16, 8]], 0, 0))
+    count_up("io2", T.i16[:], [[0, 34], [1, 16]], 0)
+    count_up("io3", T.nb[:], [[16, 2], [0, 16]], 240)
+    count_up("io3", T.i4[:], [[0, K // 4], [1, 4]], 0)
+    count_up("io3", T.jb[:], [[16, 32]], K)
+    count_up("io3", T.i3[:], [[0, 32], [1, 3]], 0)
+    count_up("io4", T.places[:], [[1, C]], 0)
+    for q in range(8):
+        ev("c0", V.memset(slot(q, 16 * q, 16 * q + 16), 0.0))
+    w("v", "io1")
+    ev("c1", V.tensor_copy(T.uoff[:], T.uoi[:]))
+    ev("c1", V.tensor_scalar(T.pint[:, 0:1], T.pcol[:], 15, None, A.bitwise_and))
+    ev("c1", V.tensor_scalar(T.pint[:, 1:2], T.pcol[:], 3, None, A.bitwise_and))
+    ev("c1", V.tensor_scalar(T.pint[:, 2:3], T.pcol[:], 2, 3, A.arith_shift_right, A.bitwise_and))
+    ev("c1", V.tensor_scalar(T.pint[:, 3:4], T.pcol[:], 4, 1, A.arith_shift_right, A.bitwise_and))
+    for q in range(8, 16):
+        ev("c0", V.memset(slot(q, 16 * q, 16 * q + 16), 0.0))
+    w("v", "c1")
+    ev("c2", V.tensor_copy(T.pf[:, 0:4], T.pint[:]))
+    ev("c0", V.memset(T.a1[:], 0.0))
+    ev("c0", V.memset(T.a2[:], 0.0))
+    ev("c6", V.memset(T.tin[:, 0:16], 0.0))
+    ev("c6", V.memset(T.tin[:, 16 + C:32 + C], 0.0))
+    ev("c6", V.memset(T.z2[:, 0:64:2], 0.0))
+    ev("c0", V.memset(T.cb[:, SL - 1:SL * C:SL], 0.0))
+    w("v", "c2", "io2")
+    ev("c3a", V.tensor_scalar(T.mh[:], T.i16[:, 0:H2], T.pf[:, 0:1], 0.5, A.is_equal, A.subtract))
+    ev("c3", V.tensor_scalar(T.kt[:], T.i16[:, 0:H2], 0.5, BIG / 16, A.subtract, A.mult))
+    w("v", "c3a")
+    ev("c3", V.tensor_scalar(T.mt[:], T.mh[:], BIG, None, A.mult))
+    w("v", "lu")
+    ev("c4", V.quantize_mx(T.uq[:], T.us[:], T.ub[:]))
+    ev("c6", V.tensor_scalar(T.pf[:, 4:5], T.pf[:, 3:4], 1.0, None, A.subtract))
+    ev("c6", V.tensor_scalar(T.pf[:, 5:6], T.pf[:, 3:4], -1.0, None, A.mult))
+    w("v", "c4")
+    ev("c5", V.tensor_copy(T.urq[:].bitcast(dt.uint32), T.uq[:].bitcast(dt.uint32).indirect(T.uoff[:, 0:8])))
+    ev("c5", V.tensor_copy(T.urs[:], T.us[:].indirect(T.uoff[:, 0:8])))
+    w("v", "lxb")
+    quant_half(0, 1)
+    w("p", "c5", "qb")
+    scores(0, T.psa[:, 0:H2], H2, C, "sa")
+    w("v", "lxa")
+    quant_half(0, 0)
+    w("v", "c3")
+
+    for t in range(R):
+        win = T["win%d" % t]
+        w("p", "qa")
+        scores(t, T.ps2[:, 0:C], 0, C, "s2")
+        scores(t, T.ps1[:, 0:C], 0, C, "s1")
+        scores(t, T.ps2[:, C:C + H2], 0, H2, "s2w")
+        own_scores(1, T.psa[:, 0:H2], "sa")
+        if t == 0:
+            w("v", "io3")
+            ev("c6", V.tensor_scalar(T.k0[:], T.i16[:], 1.0, None, A.min))
+            ev("c6", V.tensor_scalar(T.co[:, 0:CST * len(CHUNKS):CST], T.i16[:, 0:len(CHUNKS)], 0.0, None, A.mult))
+            ev("c6", V.tensor_scalar(T.m4[:], T.i4[:], T.pf[:, 2:3], None, A.is_equal))
+            ev("c6", V.tensor_scalar(T.k4[:], T.i4[:], T.pf[:, 2:3], None, A.not_equal))
+            ev("c6", V.tensor_scalar(T.d2[:, 0:64:2], T.jb[:], T.pf[:, 0:1], 4.0, A.add, A.mult))
+            ev("c6", V.tensor_scalar(T.nn[:], T.nb[:], T.pf[:, 0:1], None, A.add))
+            ev("c6", V.tensor_scalar(T.k3[:], T.i3[:], 1.0, None, A.min))
+        own_scores(0, T.ps1[:, 0:H2], "s1")
+        if t > 0:
+            listing()
+            w("v", "sct")
+            ev("lms", V.tensor_tensor_scan(T.lm[:], T.lst[:, 0:K], T.m4[:], 0.0, A.max, A.mult))
+            w("v", "lms")
+            ev("lzs", V.tensor_tensor_scan(T.lz[:], T.k4[:], T.lm[:], 0.0, A.mult, A.add))
+            w("v", "lzs")
+            ev("vo", V.tensor_scalar(T.voff[:], T.lz[:, 3:K:4], 4.0, T.pf[:, 1:2], A.mult, A.add))
+
+        def signs(c, name):
+            o, n = H2 * (c - NV), (H2 if c < 16 else 240)
+            ev(name, S.activation(T.sg[:, o:o + n], T.ps2[:, 16 * c + 16:16 * c + 16 + n], F.Sign, bias=own(c), scale=-1.0))
+
+        def above(c, name):
+            o, lo, hi = H2 * (c - NV), 16 * c + 16, min(16 * c + 16 + H2, C)
+            ev(name, S.activation(slot(c, lo, hi), T.sg[:, o:o + hi - lo], F.Relu, accum_out=T.a1[:, c:c + 1]))
+
+        def below(c, name):
+            o, n = H2 * (c - NV) + C - 16 * c - 16, 16 * (c - 16)
+            ev(name, S.activation(slot(c, 0, n), T.sg[:, o:o + n], F.Sign, bias=1.0, accum_out=T.a2[:, c:c + 1]))
+
+        w("s", "s2", "hb")
+        signs(16, "sga")
+        w("s", "s2w")
+        for c in range(17, 31):
+            signs(c, "sga")
+            if t > 0 and c == 16 + VG:
+                w("s", "vo")
+                ev("vg", S.activation(T["vic%d" % (t - 1)][:],
+                                      T["win%d" % (t - 1)][:, EW:EW + 4 * C].indirect(T.voff[:, 0:40]), F.Copy))
+        w("s", "ha")
+        for c in range(NV, 16):
+            signs(c, "sga")
+        signs(31, "sgb")
+        w("s", "sga", "c0")
+        for c in range(NV, 31):
+            above(c, "ac0" if c <= 20 else "ac1" if c <= 27 else "ac2")
+        w("s", "sgb")
+        for c in range(31, 16, -1):
+            below(c, "ac3" if c >= 25 else "ac4" if c >= 19 else "ac5")
+
+        w("v", "ha", "hb", "c0")
+        for c in range(NV):
+            lo, hi = 16 * c + 16, 16 * c + 16 + H2
+            ev("cma", V.tensor_scalar(slot(c, lo, hi), T.ps1[:, lo:hi], own(c), None, A.is_lt))
+            if t > 0 and c == QP:
+                w("v", "vg")
+                pq, ps = T["pq%d" % (t - 1)], T["ps%dc" % (t - 1)]
+                ev("qp", V.quantize_mx(pq[:], ps[:], T["vic%d" % (t - 1)][:]))
+                w("g", "qp")
+                arr = T.sem["arr%d" % t]
+                g.remote_dma(T["inq%d" % t][:].bitcast(dt.uint8), pq[:].bitcast(dt.uint8), arr, T.sem.sent, pid, rid, emask)
+                g.remote_dma(T["ins%d" % t][:], ps[:], arr, T.sem.sent, pid, rid, emask)
+                cnt["sent"] = cnt.get("sent", 0) + 2 * n_out
+                cnt["arr%d" % t] = 2 * n_in
+        ev("dd", V.tensor_tensor(T.cb[:, 16:SL * C:SL], T.ps1[:], T.hh[:], A.is_lt))
+        if t == 0:
+            w("v", "la", "lv")
+            ev("qin", V.quantize_mx(T.inq0[:], T.ins0[:], T.ab[:]))
+            ev("qv", V.quantize_mx(T.vq[:], T.vs[:], T.vb[:]))
+            w("p", "qin", "lw")
+        else:
+            w("p", "arr%d" % t)
+        for b in range(4):
+            ev("rr", PE.matmul_mx(T["pr%d" % b][:, 0:K], T.wq[:, 128 * b:128 * b + 128], T.wp[:, 128 * b:128 * b + 128],
+                                  T["inq%d" % t][:], T["ins%d" % t][:], True, True))
+        nr = NV - RS
+        w("s", "cma")
+        for c in range(nr, NV):
+            o = H2 * (c - nr)
+            ev("acr", S.activation(T.jk[:, o:o + H2], slot(c, 16 * c + 16, 16 * c + 16 + H2), F.Identity, accum_out=T.a1[:, c:c + 1]))
+        w("s", "rr")
+        for b in range(4):
+            ev("ee", S.activation(win[:, b:EW:4], T["pr%d" % b][:, 0:K], F.Relu, scale=0.03125))
+        w("v", "cma")
+        for c in range(nr):
+            lo = 16 * c + 16
+            ev("rsc", V.tensor_tensor_scan(T.ro[:, 128 * c:128 * c + 128], slot(c, lo, lo + 128), slot(c, lo + 128, lo + H2),
+                                           0.0, A.add, A.add))
+        w("v", "dd", "c6")
+        ev("dsc", V.tensor_tensor_scan(T.ds[:], T.k0[:, 0:C], T.cb[:, 16:SL * C:SL], 0.0, A.mult, A.add))
+
+        def chunk(k):
+            lo, hi = CHUNKS[k]
+            w("v", "ac%d" % k)
+            ev("ck%d" % k, V.tensor_tensor_scan(T.co[:, CST * k + 1:CST * k + 1 + 9 * (hi - lo)], T.cb[:, SL * lo:SL * hi:2],
+                                                T.cb[:, SL * lo + 1:SL * hi:2], 0.0, A.add, A.add))
+
+        def steps(k):
+            lo, hi = CHUNKS[k]
+            o, n = CST * k, 9 * (hi - lo)
+            w("v", "ck%d" % k)
+            ev("df0" if k < 3 else "df1" if k < 5 else "df2",
+               V.tensor_tensor_scan(T.tin[:, 16 + lo:16 + hi], T.co[:, o + 9:o + n + 1:9], T.co[:, o:o + n:9], 0.0, A.max, A.subtract))
+
+        def turn(s):
+            lo, hi, lo2, hi2 = STAGES[s]
+            w("v", "df%d" % s)
+            ev("tr%d" % s, V.transpose(T.t1[:, lo:hi], T.tin[:, 16 + lo:16 + hi]))
+            ev("tr%d" % s, V.transpose(T.t2[:, lo2:hi2], T.tin[:, lo2:hi2]))
+
+        def sums(s):
+            lo, hi, lo2, hi2 = STAGES[s]
+            w("v", "tr%d" % s)
+            ev("us", V.tensor_tensor_scan(T.u1[:, lo:hi], T.k0[:, lo:hi], T.t1[:, lo:hi], 0.0, A.mult, A.add))
+            ev("us", V.tensor_tensor_scan(T.u2[:, lo2:hi2], T.k0[:, lo2:hi2], T.t2[:, lo2:hi2], 0.0, A.mult, A.add))
+
+        chunk(0)
+        w("v", "dsc")
+        ev("dns", V.tensor_tensor(T.dn[:], T.ds[:, 15:C:16], T.nn[:], A.add))
+        chunk(1)
+        steps(0)
+        chunk(2)
+        steps(1)
+        steps(2)
+        turn(0)
+        sums(0)
+        chunk(3)
+        chunk(4)
+        steps(3)
+        steps(4)
+        turn(1)
+        chunk(5)
+        sums(1)
+        steps(5)
+        w("v", "dns", "rsc")
+        ev("b1s", V.tensor_tensor(T.b1[:], T.dn[:], T.a2[:], A.add))
+        turn(2)
+        w("v", "b1s")
+        ev("la1", V.tensor_tensor(T.x3[:, 0:3 * nr:3], T.b1[:, 0:nr], T.ro[:, 127:128 * nr:128], A.add))
+        sums(2)
+        w("v", "acr")
+        ev("la1", V.tensor_tensor(T.x3[:, 3 * nr:96:3], T.b1[:, nr:32], T.a1[:, nr:32], A.add))
+        w("v", "us")
+        even, odd = T.pf[:, 4:5], T.pf[:, 5:6]
+        ev("la1", V.tensor_scalar(T.x3[:, 1:96:6], T.u1[:, 15:C:32], even, None, A.mult))
+        ev("la1", V.tensor_scalar(T.x3[:, 4:96:6], T.u2[:, 47:C + 32:32], even, None, A.mult))
+        ev("la1", V.tensor_scalar(T.x3[:, 2:96:6], T.u2[:, 31:C:32], odd, None, A.mult))
+        ev("la1", V.tensor_scalar(T.x3[:, 5:96:6], T.u1[:, 31:C:32], odd, None, A.mult))
+
+        w("v", "la1")
+        ev("l1", V.tensor_tensor_scan(T.p3[:], T.k3[:], T.x3[:], 0.0, A.mult, A.add))
+        pos = T.p3[:, 2:96:3]
+        w("v", "l1")
+        ev("l2", V.tensor_scalar(T.z2[:, 1:64:2], pos, K - 0.5, None, A.is_gt))
+        ev("l2", V.tensor_scalar(T.d2[:, 1:64:2], pos, float(K), 4.0, A.min, A.mult))
+        ev("l2r", V.tensor_copy(T.roff[:], pos))
+        w("v", "l2")
+        ev("l3", V.tensor_tensor_scan(T.i2[:], T.z2[:], T.d2[:], 0.0, A.mult, A.max))
+        w("v", "l3")
+        for e in range(4):
+            ev("l4%d" % e, V.tensor_scalar(T.soff[:, 32 * e:32 * e + 32], T.i2[:, 1:64:2], float(e), None, A.add))
+        w("s", "ee")
+        w("v", "ee")
+
+        if t < R - 1:
+            gather_half(t, 1, "s", range(4 - GV1))
+            gather_half(t, 0, "s", range(4 - GV0))
+            gather_half(t, 1, "v", range(4 - GV1, 4))
+            w("v", "gb")
+            quant_half(t + 1, 1)
+            w("p", "qb")
+            scores(t + 1, T.psa[:, 0:H2], H2, C, "sa")
+            gather_half(t, 0, "v", range(4 - GV0, 4))
+            w("v", "ga")
+            quant_half(t + 1, 0)
+        else:
+            gather_half(t, 0, "s", range(4))
+            gather_half(t, 1, "v", range(4))
+            xq, xs = T["xq%d" % R], T["xs%d" % R]
+            for h, ps in ((1, T.ps1), (0, T.psa)):
+                lo, hi = h * H2, (h + 1) * H2
+                qn, yn, cn = ("qb", "yb", "ycb") if h else ("qa", "ya", "yca")
+                w("v", "gb" if h else "ga")
+                quant_half(R, h)
+                w("p", qn, "qv")
+                ev(yn, PE.matmul_mx(ps[:, 0:H2], T.vq[:], T.vs[:], xq[:, lo:hi], xs[:, lo:hi], True, True))
+                w("y", qn)
+                ev("st1", SY.dma_start(T.oc[:, 4 * lo:4 * hi], xq[:, lo:hi].bitcast(dt.uint8)), 16)
+                w("s", yn)
+                ev(cn, S.activation(T.ysb[:, lo:hi], ps[:, 0:H2], F.Copy))
+            for k in range(4):
+                ev("st1", SY.dma_start(T.osc[4 * k:4 * k + 4, :], xs[32 * k:32 * k + 4, :]), 16)
+            for h in (1, 0):
+                lo, hi = h * H2, (h + 1) * H2
+                w("s", "ycb" if h else "yca")
+                ev("st2", S.dma_start(T.y[:, lo:hi], T.ysb[:, lo:hi]), 16)
+            listing()
+            w("y", "sct")
+            ev("st1", SY.dma_start(T.ol[:], T.lst[0:128:16, 0:K]), 16)
+
+    for name in sorted(cnt):
+        if max([v for (q, n), v in seen.items() if n == name] + [0]) < cnt[name]:
+            w("g", name)

@@ -1,10 +1,10 @@
 from concourse.mybir import dt, AluOpType, ActivationFunctionType
 
 C, K, R, NR = 512, 160, 3, 4
-NV = 15
-RS = 4
+NV = 16
+RS = 5
 GV1, GV0 = 3, 0
-VG, QP = 9, 8
+VG, QP = 12, 8
 EW = 4 * K
 H2 = C // 2
 SL = 18
@@ -100,10 +100,12 @@ def rank_program(g, core, T, topo):
         ev("qb" if h else "qa", V.quantize_mx(T["xq%d" % t][:, h * H2:(h + 1) * H2], T["xs%d" % t][:, h * H2:(h + 1) * H2],
                                               buf[:, o + 4 * h * H2:o + 4 * (h + 1) * H2]))
 
-    def own_scores(h, src, wait):
+    def own_scores(h, src, wait, between=None):
         lo, hi = h * H2, (h + 1) * H2
         w("v", wait)
         ev("mkb" if h else "mka", V.tensor_tensor(T.msk[:, lo:hi], src, T.mt[:], A.min))
+        if between:
+            between()
         w("v", "mkb" if h else "mka")
         ev("hb" if h else "ha", V.tensor_tensor_scan(T.hh[:, lo:hi], T.kt[:], T.msk[:, lo:hi], 0.0, A.min, A.max))
 
@@ -122,11 +124,20 @@ def rank_program(g, core, T, topo):
         w("v", "l2r", "io4")
         ev("sct", V.tensor_copy(T.lst[:, 0:C].indirect(T.roff[:, 0:32]), T.places[:]))
 
+    def marks():
+        w("v", "sct")
+        ev("lms", V.tensor_tensor_scan(T.lm[:], T.lst[:, 0:K], T.m4[:], 0.0, A.max, A.mult))
+
     def slot(c, lo, hi):
         return T.cb[:, SL * lo + c % 16:SL * hi:SL]
 
     def own(c):
         return T.hh[:, 16 * c + 15:16 * c + 16]
+
+    def compare(c):
+        lo, hi = 16 * c + 16, 16 * c + 16 + H2
+        w("v", "ha", "hb", "c0")
+        ev("cma", V.tensor_scalar(slot(c, lo, hi), T.ps1[:, lo:hi], own(c), None, A.is_lt))
 
     ev("lu", SY.dma_start(T.ub[:], T.u[:]), 16)
     ev("lxb", S.dma_start(T.win0[:, EW + 4 * H2:EW + 4 * C], T.x[:, 4 * H2:4 * C]), 16)
@@ -202,13 +213,13 @@ def rank_program(g, core, T, topo):
             ev("c6", V.tensor_scalar(T.d2[:, 0:64:2], T.jb[:], T.pf[:, 0:1], 4.0, A.add, A.mult))
             ev("c6", V.tensor_scalar(T.nn[:], T.nb[:], T.pf[:, 0:1], None, A.add))
             ev("c6", V.tensor_scalar(T.k3[:], T.i3[:], 1.0, None, A.min))
-        own_scores(0, T.ps1[:, 0:H2], "s1")
-        if t > 0:
+            own_scores(0, T.ps1[:, 0:H2], "s1")
+        else:
             listing()
-            w("v", "sct")
-            ev("lms", V.tensor_tensor_scan(T.lm[:], T.lst[:, 0:K], T.m4[:], 0.0, A.max, A.mult))
+            own_scores(0, T.ps1[:, 0:H2], "s1", marks)
             w("v", "lms")
             ev("lzs", V.tensor_tensor_scan(T.lz[:], T.k4[:], T.lm[:], 0.0, A.mult, A.add))
+            compare(0)
             w("v", "lzs")
             ev("vo", V.tensor_scalar(T.voff[:], T.lz[:, 3:K:4], 4.0, T.pf[:, 1:2], A.mult, A.add))
 
@@ -233,8 +244,8 @@ def rank_program(g, core, T, topo):
                 w("s", "vo")
                 ev("vg", S.activation(T["vic%d" % (t - 1)][:],
                                       T["win%d" % (t - 1)][:, EW:EW + 4 * C].indirect(T.voff[:, 0:40]), F.Copy))
-        w("s", "ha")
         for c in range(NV, 16):
+            w("s", "ha")
             signs(c, "sga")
         signs(31, "sgb")
         w("s", "sga", "c0")
@@ -244,10 +255,8 @@ def rank_program(g, core, T, topo):
         for c in range(31, 16, -1):
             below(c, "ac3" if c >= 25 else "ac4" if c >= 19 else "ac5")
 
-        w("v", "ha", "hb", "c0")
-        for c in range(NV):
-            lo, hi = 16 * c + 16, 16 * c + 16 + H2
-            ev("cma", V.tensor_scalar(slot(c, lo, hi), T.ps1[:, lo:hi], own(c), None, A.is_lt))
+        for c in range(1 if t else 0, NV):
+            compare(c)
             if t > 0 and c == QP:
                 w("v", "vg")
                 pq, ps = T["pq%d" % (t - 1)], T["ps%dc" % (t - 1)]
@@ -277,11 +286,17 @@ def rank_program(g, core, T, topo):
         w("s", "rr")
         for b in range(4):
             ev("ee", S.activation(win[:, b:EW:4], T["pr%d" % b][:, 0:K], F.Relu, scale=0.03125))
-        w("v", "cma")
-        for c in range(nr):
-            lo = 16 * c + 16
-            ev("rsc", V.tensor_tensor_scan(T.ro[:, 128 * c:128 * c + 128], slot(c, lo, lo + 128), slot(c, lo + 128, lo + H2),
-                                           0.0, A.add, A.add))
+        left = list(range(nr))
+
+        def rows(n):
+            w("v", "cma")
+            for _ in range(n):
+                c = left.pop()
+                lo = 16 * c + 16
+                ev("rsc", V.tensor_tensor_scan(T.ro[:, 128 * c:128 * c + 128], slot(c, lo, lo + 128), slot(c, lo + 128, lo + H2),
+                                               0.0, A.add, A.add))
+
+        rows(nr - 5)
         w("v", "dd", "c6")
         ev("dsc", V.tensor_tensor_scan(T.ds[:], T.k0[:, 0:C], T.cb[:, 16:SL * C:SL], 0.0, A.mult, A.add))
 
@@ -317,24 +332,27 @@ def rank_program(g, core, T, topo):
         steps(0)
         chunk(2)
         steps(1)
+        rows(1)
         steps(2)
-        turn(0)
-        sums(0)
         chunk(3)
-        chunk(4)
+        turn(0)
         steps(3)
+        rows(1)
+        sums(0)
+        chunk(4)
+        rows(2)
         steps(4)
-        turn(1)
         chunk(5)
-        sums(1)
+        turn(1)
         steps(5)
-        w("v", "dns", "rsc")
-        ev("b1s", V.tensor_tensor(T.b1[:], T.dn[:], T.a2[:], A.add))
+        rows(1)
+        sums(1)
         turn(2)
-        w("v", "b1s")
-        ev("la1", V.tensor_tensor(T.x3[:, 0:3 * nr:3], T.b1[:, 0:nr], T.ro[:, 127:128 * nr:128], A.add))
+        w("v", "dns")
+        ev("b1s", V.tensor_tensor(T.b1[:], T.dn[:], T.a2[:], A.add))
         sums(2)
-        w("v", "acr")
+        w("v", "b1s", "rsc", "acr")
+        ev("la1", V.tensor_tensor(T.x3[:, 0:3 * nr:3], T.b1[:, 0:nr], T.ro[:, 127:128 * nr:128], A.add))
         ev("la1", V.tensor_tensor(T.x3[:, 3 * nr:96:3], T.b1[:, nr:32], T.a1[:, nr:32], A.add))
         w("v", "us")
         even, odd = T.pf[:, 4:5], T.pf[:, 5:6]

@@ -3,15 +3,15 @@ from concourse.mybir import dt, AluOpType, ActivationFunctionType
 C, K, R, NR = 512, 160, 3, 4
 NV = 16
 RS = 5
-GV1, GV0 = 3, 0
-VG, QP = 12, 8
+GV = (1, 1, 2)
+VG, QP = 6, 5
 EW = 4 * K
 H2 = C // 2
 SL = 18
 BIG = 2e29
-CHUNKS = ((240, 352), (352, 464), (464, 512), (128, 240), (32, 128), (0, 32))
-CST = 1088
-STAGES = ((256, 512, 256, 544), (32, 256, 64, 256), (0, 32, 0, 64))
+CHUNKS = ((240, 352), (352, 464), (464, 512), (128, 240), (0, 128))
+CST = 1160
+STAGES = ((256, 512, 256, 544), (0, 256, 0, 256))
 Q8 = "float8_e4m3fn_x4"
 
 SCRATCH = {
@@ -24,20 +24,20 @@ SCRATCH = {
     "pcol": ("sbuf", [128, 1], "int32"), "pint": ("sbuf", [128, 4], "int32"), "pf": ("sbuf", [128, 6], "float32"),
     "uoi": ("sbuf", [128, 8], "int32"), "uoff": ("sbuf", [128, 8], "uint16"),
     "i16": ("sbuf", [128, C + 32], "bfloat16"), "i4": ("sbuf", [128, K], "bfloat16"), "places": ("sbuf", [128, C], "float32"),
-    "jb": ("sbuf", [128, 32], "float32"), "i3": ("sbuf", [128, 96], "float32"), "k3": ("sbuf", [128, 96], "float32"),
+    "jb": ("sbuf", [128, 32], "float32"), "i3": ("sbuf", [128, 48], "float32"), "k3": ("sbuf", [128, 48], "float32"),
     "nb": ("sbuf", [128, 32], "float32"), "nn": ("sbuf", [128, 32], "float32"),
     "mh": ("sbuf", [128, H2], "bfloat16"), "mt": ("sbuf", [128, H2], "bfloat16"), "kt": ("sbuf", [128, H2], "bfloat16"),
     "k0": ("sbuf", [128, C + 32], "bfloat16"),
     "m4": ("sbuf", [128, K], "bfloat16"), "k4": ("sbuf", [128, K], "bfloat16"),
     "msk": ("sbuf", [128, C], "float32"), "hh": ("sbuf", [128, C], "float32"),
-    "cb": ("sbuf", [128, SL * C], "bfloat16"), "sg": ("sbuf", [128, 20 * H2], "bfloat16"),
-    "jk": ("sbuf", [128, 8 * H2], "bfloat16"),
+    "cb": ("sbuf", [128, SL * C], "bfloat16"), "sg": ("sbuf", [128, 16 * H2], "bfloat16"),
+    "jk": ("sbuf", [128, RS * H2], "bfloat16"),
     "ro": ("sbuf", [128, 16 * 128], "float16"), "ds": ("sbuf", [128, C], "float16"),
     "co": ("sbuf", [128, CST * len(CHUNKS)], "float16"), "tin": ("sbuf", [128, C + 32], "bfloat16"),
     "t1": ("sbuf", [128, C], "bfloat16"), "t2": ("sbuf", [128, C + 32], "bfloat16"),
     "u1": ("sbuf", [128, C], "float16"), "u2": ("sbuf", [128, C + 32], "float16"),
     "a1": ("sbuf", [128, 32], "float32"), "a2": ("sbuf", [128, 32], "float32"),
-    "dn": ("sbuf", [128, 32], "float32"), "b1": ("sbuf", [128, 32], "float32"),
+    "dn": ("sbuf", [128, 32], "float32"), "b1": ("sbuf", [128, 16], "float32"),
     "x3": ("sbuf", [128, 96], "float32"), "p3": ("sbuf", [128, 96], "float32"),
     "z2": ("sbuf", [128, 64], "float32"), "d2": ("sbuf", [128, 64], "float32"), "i2": ("sbuf", [128, 64], "float32"),
     "soff": ("sbuf", [128, 128], "uint16"), "roff": ("sbuf", [128, 32], "uint16"), "voff": ("sbuf", [128, 40], "uint16"),
@@ -61,9 +61,9 @@ for _t in range(R - 1):
 
 SEMAPHORES = ["lu", "lxa", "lxb", "la", "lw", "lv", "io1", "io2", "io3", "io4", "c0", "c1", "c2", "c3", "c3a", "c4", "c5", "c6",
               "qa", "qb", "qin", "qv", "sa", "s1", "s2", "s2w", "rr", "mka", "mkb", "ha", "hb", "dd", "dsc", "dns",
-              "cma", "rsc", "sga", "sgb", "ac0", "ac1", "ac2", "ac3", "ac4", "ac5", "acr", "ee",
-              "ck0", "ck1", "ck2", "ck3", "ck4", "ck5", "df0", "df1", "df2", "tr0", "tr1", "tr2",
-              "us", "b1s", "la1", "l1", "l2", "l2r", "l3", "l40", "l41", "l42", "l43",
+              "cma", "rsc", "sga", "sgb", "ac0", "ac1", "ac2", "ac3", "ac4", "acr", "ee",
+              "ck0", "ck1", "ck2", "ck3", "ck4", "df0", "df1", "tr0", "tr1",
+              "us", "b1s", "la1", "l1", "l2", "ra", "rb", "l3", "l40", "l41", "l42", "l43", "l50", "l51", "l52", "l53",
               "ga", "gb", "sct", "lms", "lzs", "vo", "vg", "qp", "arr1", "arr2", "sent",
               "ya", "yb", "yca", "ycb", "st1", "st2"]
 
@@ -100,33 +100,35 @@ def rank_program(g, core, T, topo):
         ev("qb" if h else "qa", V.quantize_mx(T["xq%d" % t][:, h * H2:(h + 1) * H2], T["xs%d" % t][:, h * H2:(h + 1) * H2],
                                               buf[:, o + 4 * h * H2:o + 4 * (h + 1) * H2]))
 
-    def own_scores(h, src, wait, between=None):
+    def own_mask(h):
+        w("v", "sa" if h else "s1")
+        ev("mkb" if h else "mka", V.tensor_tensor(T.msk[:, h * H2:(h + 1) * H2], (T.psa if h else T.ps1)[:, 0:H2], T.mt[:], A.min))
+
+    def own_scan(h):
         lo, hi = h * H2, (h + 1) * H2
-        w("v", wait)
-        ev("mkb" if h else "mka", V.tensor_tensor(T.msk[:, lo:hi], src, T.mt[:], A.min))
-        if between:
-            between()
         w("v", "mkb" if h else "mka")
         ev("hb" if h else "ha", V.tensor_tensor_scan(T.hh[:, lo:hi], T.kt[:], T.msk[:, lo:hi], 0.0, A.min, A.max))
 
     def scores(t, out, lo, hi, name):
         ev(name, PE.matmul_mx(out, T.urq[:], T.urs[:], T["xq%d" % t][:, lo:hi], T["xs%d" % t][:, lo:hi], True, True))
 
+    def all_scores(t):
+        w("p", "qa")
+        scores(t, T.ps2[:, 0:C], 0, C, "s2")
+        scores(t, T.ps1[:, 0:C], 0, C, "s1")
+        scores(t, T.ps2[:, C:C + H2], 0, H2, "s2w")
+
     def gather_half(t, h, q, es):
         buf, o = state(t + 1)
         for e in es:
-            w(q, "l4%d" % e)
+            w(q, "ee", "l%d%d" % (4 + h, e))
             out = buf[:, o + 4 * h * H2 + e:o + 4 * (h + 1) * H2:4]
             src = T["win%d" % t][:, 0:EW + 4 * C].indirect(T.soff[:, 32 * e + 16 * h:32 * e + 16 * h + 16])
             ev("gb" if h else "ga", S.activation(out, src, F.Copy) if q == "s" else V.tensor_copy(out, src))
 
-    def listing():
-        w("v", "l2r", "io4")
-        ev("sct", V.tensor_copy(T.lst[:, 0:C].indirect(T.roff[:, 0:32]), T.places[:]))
-
-    def marks():
-        w("v", "sct")
-        ev("lms", V.tensor_tensor_scan(T.lm[:], T.lst[:, 0:K], T.m4[:], 0.0, A.max, A.mult))
+    def listing(lo, hi):
+        w("v", "rb" if lo >= 16 else "ra", "io4", "sct")
+        ev("sct", V.tensor_copy(T.lst[:, 0:C].indirect(T.roff[:, lo:hi]), T.places[:, 16 * lo:16 * hi]))
 
     def slot(c, lo, hi):
         return T.cb[:, SL * lo + c % 16:SL * hi:SL]
@@ -157,7 +159,7 @@ def rank_program(g, core, T, topo):
     count_up("io3", T.nb[:], [[16, 2], [0, 16]], 240)
     count_up("io3", T.i4[:], [[0, K // 4], [1, 4]], 0)
     count_up("io3", T.jb[:], [[16, 32]], K)
-    count_up("io3", T.i3[:], [[0, 32], [1, 3]], 0)
+    count_up("io3", T.i3[:], [[0, 16], [1, 3]], 0)
     count_up("io4", T.places[:], [[1, C]], 0)
     for q in range(8):
         ev("c0", V.memset(slot(q, 16 * q, 16 * q + 16), 0.0))
@@ -180,12 +182,13 @@ def rank_program(g, core, T, topo):
     w("v", "c2", "io2")
     ev("c3a", V.tensor_scalar(T.mh[:], T.i16[:, 0:H2], T.pf[:, 0:1], 0.5, A.is_equal, A.subtract))
     ev("c3", V.tensor_scalar(T.kt[:], T.i16[:, 0:H2], 0.5, BIG / 16, A.subtract, A.mult))
-    w("v", "c3a")
-    ev("c3", V.tensor_scalar(T.mt[:], T.mh[:], BIG, None, A.mult))
+    ev("c6", V.tensor_scalar(T.k0[:], T.i16[:], 1.0, None, A.min))
+    ev("c3", (w("v", "c3a"), V.tensor_scalar(T.mt[:], T.mh[:], BIG, None, A.mult))[1])
     w("v", "lu")
     ev("c4", V.quantize_mx(T.uq[:], T.us[:], T.ub[:]))
     ev("c6", V.tensor_scalar(T.pf[:, 4:5], T.pf[:, 3:4], 1.0, None, A.subtract))
     ev("c6", V.tensor_scalar(T.pf[:, 5:6], T.pf[:, 3:4], -1.0, None, A.mult))
+    ev("c6", V.tensor_scalar(T.co[:, 0:CST * len(CHUNKS):CST], T.i16[:, 0:len(CHUNKS)], 0.0, None, A.mult))
     w("v", "c4")
     ev("c5", V.tensor_copy(T.urq[:].bitcast(dt.uint32), T.uq[:].bitcast(dt.uint32).indirect(T.uoff[:, 0:8])))
     ev("c5", V.tensor_copy(T.urs[:], T.us[:].indirect(T.uoff[:, 0:8])))
@@ -195,41 +198,29 @@ def rank_program(g, core, T, topo):
     scores(0, T.psa[:, 0:H2], H2, C, "sa")
     w("v", "lxa")
     quant_half(0, 0)
+    all_scores(0)
     w("v", "c3")
+    own_mask(1)
+    w("v", "io3")
+    ev("c6", V.tensor_scalar(T.m4[:], T.i4[:], T.pf[:, 2:3], None, A.is_equal))
+    ev("c6", V.tensor_scalar(T.k4[:], T.i4[:], T.pf[:, 2:3], None, A.not_equal))
+    own_scan(1)
+    own_mask(0)
+    ev("c6", V.tensor_scalar(T.d2[:, 0:64:2], T.jb[:], T.pf[:, 0:1], 4.0, A.add, A.mult))
+    ev("c6", V.tensor_scalar(T.nn[:], T.nb[:], T.pf[:, 0:1], None, A.add))
+    own_scan(0)
+    ev("c6", V.tensor_scalar(T.k3[:], T.i3[:], 1.0, None, A.min))
 
     for t in range(R):
         win = T["win%d" % t]
-        w("p", "qa")
-        scores(t, T.ps2[:, 0:C], 0, C, "s2")
-        scores(t, T.ps1[:, 0:C], 0, C, "s1")
-        scores(t, T.ps2[:, C:C + H2], 0, H2, "s2w")
-        own_scores(1, T.psa[:, 0:H2], "sa")
-        if t == 0:
-            w("v", "io3")
-            ev("c6", V.tensor_scalar(T.k0[:], T.i16[:], 1.0, None, A.min))
-            ev("c6", V.tensor_scalar(T.co[:, 0:CST * len(CHUNKS):CST], T.i16[:, 0:len(CHUNKS)], 0.0, None, A.mult))
-            ev("c6", V.tensor_scalar(T.m4[:], T.i4[:], T.pf[:, 2:3], None, A.is_equal))
-            ev("c6", V.tensor_scalar(T.k4[:], T.i4[:], T.pf[:, 2:3], None, A.not_equal))
-            ev("c6", V.tensor_scalar(T.d2[:, 0:64:2], T.jb[:], T.pf[:, 0:1], 4.0, A.add, A.mult))
-            ev("c6", V.tensor_scalar(T.nn[:], T.nb[:], T.pf[:, 0:1], None, A.add))
-            ev("c6", V.tensor_scalar(T.k3[:], T.i3[:], 1.0, None, A.min))
-            own_scores(0, T.ps1[:, 0:H2], "s1")
-        else:
-            listing()
-            own_scores(0, T.ps1[:, 0:H2], "s1", marks)
-            w("v", "lms")
-            ev("lzs", V.tensor_tensor_scan(T.lz[:], T.k4[:], T.lm[:], 0.0, A.mult, A.add))
-            compare(0)
-            w("v", "lzs")
-            ev("vo", V.tensor_scalar(T.voff[:], T.lz[:, 3:K:4], 4.0, T.pf[:, 1:2], A.mult, A.add))
 
         def signs(c, name):
-            o, n = H2 * (c - NV), (H2 if c < 16 else 240)
-            ev(name, S.activation(T.sg[:, o:o + n], T.ps2[:, 16 * c + 16:16 * c + 16 + n], F.Sign, bias=own(c), scale=-1.0))
+            o = H2 * (c - NV)
+            ev(name, S.activation(T.sg[:, o:o + 240], T.ps2[:, 16 * c + 16:16 * c + 256], F.Sign, bias=own(c), scale=-1.0))
 
         def above(c, name):
-            o, lo, hi = H2 * (c - NV), 16 * c + 16, min(16 * c + 16 + H2, C)
-            ev(name, S.activation(slot(c, lo, hi), T.sg[:, o:o + hi - lo], F.Relu, accum_out=T.a1[:, c:c + 1]))
+            o, lo = H2 * (c - NV), 16 * c + 16
+            ev(name, S.activation(slot(c, lo, C), T.sg[:, o:o + C - lo], F.Relu, accum_out=T.a1[:, c:c + 1]))
 
         def below(c, name):
             o, n = H2 * (c - NV) + C - 16 * c - 16, 16 * (c - 16)
@@ -244,16 +235,13 @@ def rank_program(g, core, T, topo):
                 w("s", "vo")
                 ev("vg", S.activation(T["vic%d" % (t - 1)][:],
                                       T["win%d" % (t - 1)][:, EW:EW + 4 * C].indirect(T.voff[:, 0:40]), F.Copy))
-        for c in range(NV, 16):
-            w("s", "ha")
-            signs(c, "sga")
         signs(31, "sgb")
         w("s", "sga", "c0")
         for c in range(NV, 31):
             above(c, "ac0" if c <= 20 else "ac1" if c <= 27 else "ac2")
         w("s", "sgb")
         for c in range(31, 16, -1):
-            below(c, "ac3" if c >= 25 else "ac4" if c >= 19 else "ac5")
+            below(c, "ac3" if c >= 25 else "ac4")
 
         for c in range(1 if t else 0, NV):
             compare(c)
@@ -296,7 +284,7 @@ def rank_program(g, core, T, topo):
                 ev("rsc", V.tensor_tensor_scan(T.ro[:, 128 * c:128 * c + 128], slot(c, lo, lo + 128), slot(c, lo + 128, lo + H2),
                                                0.0, A.add, A.add))
 
-        rows(nr - 5)
+        rows(nr - 7)
         w("v", "dd", "c6")
         ev("dsc", V.tensor_tensor_scan(T.ds[:], T.k0[:, 0:C], T.cb[:, 16:SL * C:SL], 0.0, A.mult, A.add))
 
@@ -310,7 +298,7 @@ def rank_program(g, core, T, topo):
             lo, hi = CHUNKS[k]
             o, n = CST * k, 9 * (hi - lo)
             w("v", "ck%d" % k)
-            ev("df0" if k < 3 else "df1" if k < 5 else "df2",
+            ev("df0" if k < 3 else "df1",
                V.tensor_tensor_scan(T.tin[:, 16 + lo:16 + hi], T.co[:, o + 9:o + n + 1:9], T.co[:, o:o + n:9], 0.0, A.max, A.subtract))
 
         def turn(s):
@@ -325,6 +313,39 @@ def rank_program(g, core, T, topo):
             ev("us", V.tensor_tensor_scan(T.u1[:, lo:hi], T.k0[:, lo:hi], T.t1[:, lo:hi], 0.0, A.mult, A.add))
             ev("us", V.tensor_tensor_scan(T.u2[:, lo2:hi2], T.k0[:, lo2:hi2], T.t2[:, lo2:hi2], 0.0, A.mult, A.add))
 
+        even, odd = T.pf[:, 4:5], T.pf[:, 5:6]
+
+        def terms(h):
+            o, x = H2 * h, 48 * h
+            w("v", "us")
+            ev("la1", V.tensor_scalar(T.x3[:, x + 1:x + 48:6], T.u1[:, o + 15:o + H2:32], even, None, A.mult))
+            ev("la1", V.tensor_scalar(T.x3[:, x + 4:x + 48:6], T.u2[:, o + 47:o + H2 + 32:32], even, None, A.mult))
+            ev("la1", V.tensor_scalar(T.x3[:, x + 2:x + 48:6], T.u2[:, o + 31:o + H2:32], odd, None, A.mult))
+            ev("la1", V.tensor_scalar(T.x3[:, x + 5:x + 48:6], T.u1[:, o + 31:o + H2:32], odd, None, A.mult))
+
+        def positions(h):
+            x = 48 * h
+            w("v", "la1")
+            ev("l1", V.tensor_tensor_scan(T.p3[:, x:x + 48], T.k3[:], T.x3[:, x:x + 48], 0.0, A.mult, A.add))
+
+        def chosen(h):
+            pos, y = T.p3[:, 48 * h + 2:48 * h + 48:3], 32 * h
+            w("v", "l1")
+            ev("l2", V.tensor_scalar(T.z2[:, y + 1:y + 32:2], pos, K - 0.5, None, A.is_gt))
+            ev("l2", V.tensor_scalar(T.d2[:, y + 1:y + 32:2], pos, float(K), 4.0, A.min, A.mult))
+            ev("rb" if h else "ra", V.tensor_copy(T.roff[:, 16 * h:16 * h + 16], pos))
+
+        def sources(h):
+            y = 32 * h
+            w("v", "l2")
+            ev("l3", V.tensor_tensor_scan(T.i2[:, y:y + 32], T.z2[:, y:y + 32], T.d2[:, y:y + 32], 0.0, A.mult, A.max))
+
+        def offsets(h):
+            w("v", "l3")
+            for e in range(4):
+                ev("l%d%d" % (4 + h, e), V.tensor_scalar(T.soff[:, 32 * e + 16 * h:32 * e + 16 * h + 16],
+                                                         T.i2[:, 32 * h + 1:32 * h + 32:2], float(e), None, A.add))
+
         chunk(0)
         w("v", "dsc")
         ev("dns", V.tensor_tensor(T.dn[:], T.ds[:, 15:C:16], T.nn[:], A.add))
@@ -332,64 +353,68 @@ def rank_program(g, core, T, topo):
         steps(0)
         chunk(2)
         steps(1)
-        rows(1)
+        rows(2)
         steps(2)
-        chunk(3)
+        rows(1)
         turn(0)
+        chunk(3)
+        sums(0)
         steps(3)
         rows(1)
-        sums(0)
+        w("v", "dns", "ac4")
+        ev("b1s", V.tensor_tensor(T.b1[:], T.dn[:, 16:32], T.a2[:, 16:32], A.add))
         chunk(4)
-        rows(2)
+        w("v", "b1s")
+        ev("la1", V.tensor_tensor(T.x3[:, 48:96:3], T.b1[:], T.a1[:, 16:32], A.add))
+        terms(1)
         steps(4)
-        chunk(5)
+        rows(2)
+        positions(1)
         turn(1)
-        steps(5)
         rows(1)
+        chosen(1)
         sums(1)
-        turn(2)
-        w("v", "dns")
-        ev("b1s", V.tensor_tensor(T.b1[:], T.dn[:], T.a2[:], A.add))
-        sums(2)
-        w("v", "b1s", "rsc", "acr")
-        ev("la1", V.tensor_tensor(T.x3[:, 0:3 * nr:3], T.b1[:, 0:nr], T.ro[:, 127:128 * nr:128], A.add))
-        ev("la1", V.tensor_tensor(T.x3[:, 3 * nr:96:3], T.b1[:, nr:32], T.a1[:, nr:32], A.add))
-        w("v", "us")
-        even, odd = T.pf[:, 4:5], T.pf[:, 5:6]
-        ev("la1", V.tensor_scalar(T.x3[:, 1:96:6], T.u1[:, 15:C:32], even, None, A.mult))
-        ev("la1", V.tensor_scalar(T.x3[:, 4:96:6], T.u2[:, 47:C + 32:32], even, None, A.mult))
-        ev("la1", V.tensor_scalar(T.x3[:, 2:96:6], T.u2[:, 31:C:32], odd, None, A.mult))
-        ev("la1", V.tensor_scalar(T.x3[:, 5:96:6], T.u1[:, 31:C:32], odd, None, A.mult))
-
-        w("v", "la1")
-        ev("l1", V.tensor_tensor_scan(T.p3[:], T.k3[:], T.x3[:], 0.0, A.mult, A.add))
-        pos = T.p3[:, 2:96:3]
-        w("v", "l1")
-        ev("l2", V.tensor_scalar(T.z2[:, 1:64:2], pos, K - 0.5, None, A.is_gt))
-        ev("l2", V.tensor_scalar(T.d2[:, 1:64:2], pos, float(K), 4.0, A.min, A.mult))
-        ev("l2r", V.tensor_copy(T.roff[:], pos))
-        w("v", "l2")
-        ev("l3", V.tensor_tensor_scan(T.i2[:], T.z2[:], T.d2[:], 0.0, A.mult, A.max))
-        w("v", "l3")
-        for e in range(4):
-            ev("l4%d" % e, V.tensor_scalar(T.soff[:, 32 * e:32 * e + 32], T.i2[:, 1:64:2], float(e), None, A.add))
-        w("s", "ee")
-        w("v", "ee")
+        sources(1)
+        w("v", "rsc", "acr")
+        ev("la1", V.tensor_tensor(T.x3[:, 0:3 * nr:3], T.dn[:, 0:nr], T.ro[:, 127:128 * nr:128], A.add))
+        ev("la1", V.tensor_tensor(T.x3[:, 3 * nr:48:3], T.dn[:, nr:16], T.a1[:, nr:16], A.add))
+        offsets(1)
+        gather_half(t, 1, "s", range(4))
+        terms(0)
+        listing(16, 20)
+        positions(0)
+        listing(20, 24)
+        chosen(0)
+        listing(24, 28)
+        sources(0)
+        listing(28, 32)
+        offsets(0)
+        gather_half(t, 0, "s", range(4 - GV[t]))
+        gather_half(t, 0, "v", range(4 - GV[t], 4))
 
         if t < R - 1:
-            gather_half(t, 1, "s", range(4 - GV1))
-            gather_half(t, 0, "s", range(4 - GV0))
-            gather_half(t, 1, "v", range(4 - GV1, 4))
             w("v", "gb")
             quant_half(t + 1, 1)
             w("p", "qb")
             scores(t + 1, T.psa[:, 0:H2], H2, C, "sa")
-            gather_half(t, 0, "v", range(4 - GV0, 4))
+            listing(0, 8)
             w("v", "ga")
             quant_half(t + 1, 0)
+            all_scores(t + 1)
+            own_mask(1)
+            listing(8, 12)
+            own_scan(1)
+            listing(12, 16)
+            own_mask(0)
+            w("v", "sct")
+            ev("lms", V.tensor_tensor_scan(T.lm[:], T.lst[:, 0:K], T.m4[:], 0.0, A.max, A.mult))
+            own_scan(0)
+            w("v", "lms")
+            ev("lzs", V.tensor_tensor_scan(T.lz[:], T.k4[:], T.lm[:], 0.0, A.mult, A.add))
+            compare(0)
+            w("v", "lzs")
+            ev("vo", V.tensor_scalar(T.voff[:], T.lz[:, 3:K:4], 4.0, T.pf[:, 1:2], A.mult, A.add))
         else:
-            gather_half(t, 0, "s", range(4))
-            gather_half(t, 1, "v", range(4))
             xq, xs = T["xq%d" % R], T["xs%d" % R]
             for h, ps in ((1, T.ps1), (0, T.psa)):
                 lo, hi = h * H2, (h + 1) * H2
@@ -402,13 +427,13 @@ def rank_program(g, core, T, topo):
                 ev("st1", SY.dma_start(T.oc[:, 4 * lo:4 * hi], xq[:, lo:hi].bitcast(dt.uint8)), 16)
                 w("s", yn)
                 ev(cn, S.activation(T.ysb[:, lo:hi], ps[:, 0:H2], F.Copy))
+            listing(0, 16)
             for k in range(4):
                 ev("st1", SY.dma_start(T.osc[4 * k:4 * k + 4, :], xs[32 * k:32 * k + 4, :]), 16)
             for h in (1, 0):
                 lo, hi = h * H2, (h + 1) * H2
                 w("s", "ycb" if h else "yca")
                 ev("st2", S.dma_start(T.y[:, lo:hi], T.ysb[:, lo:hi]), 16)
-            listing()
             w("y", "sct")
             ev("st1", SY.dma_start(T.ol[:], T.lst[0:128:16, 0:K]), 16)
 

@@ -1,71 +1,114 @@
 from concourse.mybir import dt, AluOpType, ActivationFunctionType
 
 C, K, R, NR = 512, 160, 3, 4
-NV = 16
-RS = 5
-GV = (1, 1, 2)
-VG, QP = 6, 5
-EW = 4 * K
+NS = 2
+NV = 18
+WH = 28
+UG = 22
+WG = 24
+NC = 2
+CHUNKS = ((240, 352), (352, 464), (464, 512), (128, 240), (48, 128), (0, 48))
+PIECES = ((16, 20), (20, 24), (24, 28), (28, 32), (0, 8), (8, 16))
+M = 4 // NC
+HW = M * K
 H2 = C // 2
 SL = 18
+XS = 6
 BIG = 2e29
-CHUNKS = ((240, 352), (352, 464), (464, 512), (128, 240), (0, 128))
+FAR = 8192.0
 CST = 1160
-STAGES = ((256, 512, 256, 544), (0, 256, 0, 256))
 Q8 = "float8_e4m3fn_x4"
+
+ROUND = {
+    "v1": """c2 c3 c4 c5 c6 c7 c8 c9 c10 qp- c11 c12 c13 c14 c15 dd0 r2 k1 k0 k2 r3 ds0 r4 d1 d0 d2 r5 r6 r7 r8 pd0 tr1 r9 r10 r11 r12 r13 r14
+us1 k3 tm1 k4 ps1 k5 sr1 d4 d3 d5 of10 r15 rf1 tr0 pr0 ls0 us0 of11 ls1 tm0 ps0 ls2 sr0 rf0 of00 qb+ ls4 of01 mb+ ls5 hb+ ls3 qa+ dd1+ lm
+c16+ c17+ ma+ lz ds1+ r16+ r17+ ha+ pd1+ pr1+ vo""",
+    "v2": """c2 c3 c4 c5 c6 c7 c8 c9 c10 qp- c11 c12 c13 c14 c15 r2 dd0 k1 k0 r3 k2 ds0 r4 r5 d0 d2 d1 r6 r7 r8 r9 r10 tr1 k3 us1 r11 r12 d3
+r13 pd0 tm1 k4 ps1 k5 sr1 d4 r14 d5 of10 rf1 r15 tr0 ls0 us0 pr0 of11 tm0 ls1 ps0 sr0 ls3 rf0 of01 of00 qb+ ga3 ga2 ls2 qa+ ls4 yc0+ ls5""",
+    "s1": """s1 vg- s19 s18 s17 s29 s28 s25 s24 s0 s31 s30 a1 a0 s27 s26 a28 a29 a30 b28 b30 s21 s20 s23 s22 b31 b26 b27 b25 b29 b21 b20 b23 b24
+b22 b19 b18 b17 e0 e1 e2 e3 gb0 gb2 gb1 gb3 ga0 ga2 ga3 ga1 u19+ u22+ u23+ u20+ u18+ u21+ u24+ u25+ u26+ u27+ a19+ a20+ a22+ a23+ a18+
+a26+ a27+ a21+ a24+ a25+""",
+    "s2": """s0 vg- s25 s24 s1 s29 s28 a0 s31 s30 a1 s27 s26 b31 a28 a29 a30 b26 b28 b29 b30 b27 b25 s23 s22 s21 s20 s19 s18 s17 b24 b23 b21 b20
+b22 b19 b18 b17 e0 e1 e2 e3 gb2 gb0 gb3 gb1 ga1 ga0 yc1+ yd1+ yd0+""",
+}
+OPENING = ("qa+", "qb+", "ma+", "mb+", "ha+", "hb+")
+
+
+def spell(q):
+    out = [x[:-1] + ".0" for x in ROUND[q + "1"].split() if x[-1] == "+" and x not in OPENING]
+    for t in range(R):
+        for x in ROUND[q + ("2" if t == R - 1 else "1")].split():
+            if x[-1] == "+":
+                out.append("%s.%d" % (x[:-1], t + 1))
+            elif x[-1] != "-":
+                out.append("%s.%d" % (x, t))
+            elif t > 0:
+                out.append("%s.%d" % (x[:-1], t - 1))
+            elif x == "qp-":
+                out += ["qin.0", "qv.0"]
+    return " ".join(out)
+
+
+ORDER = {
+    "v": spell("v"),
+    "s": spell("s"),
+    "p": "rr.0 mu.1 m2.1 m1.1 m2w.1 m3.1 rr.1 mu.2 m2.2 m1.2 m2w.2 m3.2 rr.2 ym1.3 ym0.3",
+    "y": "cp1.1 cp0.1 cp1.2 cp0.2 oc1.3 oc0.3 osc.3 ol.3",
+    "g": "send.0 send.1",
+}
 
 SCRATCH = {
     "ub": ("sbuf", [128, 512], "bfloat16"), "uq": ("sbuf", [128, 128], Q8), "us": ("sbuf", [128, 128], "uint8"),
     "urq": ("sbuf", [128, 128], Q8), "urs": ("sbuf", [128, 128], "uint8"),
     "vb": ("sbuf", [128, 512], "bfloat16"), "vq": ("sbuf", [128, 128], Q8), "vs": ("sbuf", [128, 128], "uint8"),
-    "ab": ("sbuf", [128, EW], "bfloat16"),
+    "ab": ("sbuf", [128, 4 * K], "bfloat16"),
     "wq": ("sbuf", [128, 512], Q8), "wp": ("sbuf", [128, 512], "uint8"),
     "xfin": ("sbuf", [128, 4 * C], "bfloat16"),
-    "pcol": ("sbuf", [128, 1], "int32"), "pint": ("sbuf", [128, 4], "int32"), "pf": ("sbuf", [128, 6], "float32"),
+    "pcol": ("sbuf", [128, 1], "int32"), "pint": ("sbuf", [128, 4], "int32"), "pf": ("sbuf", [128, 4], "float32"),
     "uoi": ("sbuf", [128, 8], "int32"), "uoff": ("sbuf", [128, 8], "uint16"),
-    "i16": ("sbuf", [128, C + 32], "bfloat16"), "i4": ("sbuf", [128, K], "bfloat16"), "places": ("sbuf", [128, C], "float32"),
-    "jb": ("sbuf", [128, 32], "float32"), "i3": ("sbuf", [128, 48], "float32"), "k3": ("sbuf", [128, 48], "float32"),
-    "nb": ("sbuf", [128, 32], "float32"), "nn": ("sbuf", [128, 32], "float32"),
+    "i16": ("sbuf", [128, H2], "bfloat16"), "i4": ("sbuf", [128, K], "bfloat16"), "places": ("sbuf", [128, C], "float32"),
+    "jb": ("sbuf", [128, 32], "float32"),
     "mh": ("sbuf", [128, H2], "bfloat16"), "mt": ("sbuf", [128, H2], "bfloat16"), "kt": ("sbuf", [128, H2], "bfloat16"),
-    "k0": ("sbuf", [128, C + 32], "bfloat16"),
+    "k0": ("sbuf", [128, 544], "bfloat16"),
     "m4": ("sbuf", [128, K], "bfloat16"), "k4": ("sbuf", [128, K], "bfloat16"),
     "msk": ("sbuf", [128, C], "float32"), "hh": ("sbuf", [128, C], "float32"),
-    "cb": ("sbuf", [128, SL * C], "bfloat16"), "sg": ("sbuf", [128, 16 * H2], "bfloat16"),
-    "jk": ("sbuf", [128, RS * H2], "bfloat16"),
-    "ro": ("sbuf", [128, 16 * 128], "float16"), "ds": ("sbuf", [128, C], "float16"),
+    "cb": ("sbuf", [128, SL * C], "bfloat16"), "sg": ("sbuf", [128, (16 + NS) * H2], "bfloat16"),
+    "ro": ("sbuf", [128, NV * 128], "float16"), "ds": ("sbuf", [128, C], "float16"),
     "co": ("sbuf", [128, CST * len(CHUNKS)], "float16"), "tin": ("sbuf", [128, C + 32], "bfloat16"),
-    "t1": ("sbuf", [128, C], "bfloat16"), "t2": ("sbuf", [128, C + 32], "bfloat16"),
-    "u1": ("sbuf", [128, C], "float16"), "u2": ("sbuf", [128, C + 32], "float16"),
-    "a1": ("sbuf", [128, 32], "float32"), "a2": ("sbuf", [128, 32], "float32"),
-    "dn": ("sbuf", [128, 32], "float32"), "b1": ("sbuf", [128, 16], "float32"),
-    "x3": ("sbuf", [128, 96], "float32"), "p3": ("sbuf", [128, 96], "float32"),
-    "z2": ("sbuf", [128, 64], "float32"), "d2": ("sbuf", [128, 64], "float32"), "i2": ("sbuf", [128, 64], "float32"),
-    "soff": ("sbuf", [128, 128], "uint16"), "roff": ("sbuf", [128, 32], "uint16"), "voff": ("sbuf", [128, 40], "uint16"),
-    "lst": ("sbuf", [128, C], "float32"), "lm": ("sbuf", [128, K], "float32"), "lz": ("sbuf", [128, K], "float32"),
+    "t3": ("sbuf", [128, 1056], "bfloat16"), "u3": ("sbuf", [128, 1056], "float16"),
+    "i2": ("sbuf", [128, 16], "float32"), "m1": ("sbuf", [128, 16], "float32"), "m2": ("sbuf", [128, 16], "float32"),
+    "nb": ("sbuf", [128, 32], "float32"), "nn": ("sbuf", [128, 32], "float32"),
+    "xt": ("sbuf", [128, 32 * XS], "float32"), "px": ("sbuf", [128, 32 * XS], "float32"), "kx": ("sbuf", [128, 16 * XS], "float32"),
+    "cap": ("sbuf", [128, 32 * XS], "float32"), "sx": ("sbuf", [128, 32 * XS], "float32"),
+    "soff": ("sbuf", [128, 32 * M], "uint16"), "roff": ("sbuf", [128, 32], "uint16"), "voff": ("sbuf", [128, 40], "uint16"),
+    "lst": ("sbuf", [128, C], "float32"), "lm": ("sbuf", [128, K], "float16"), "lz": ("sbuf", [128, K], "float16"),
     "ysb": ("sbuf", [128, C], "float32"),
     "ps1": ("psum", [128, 512], "float32"), "ps2": ("psum", [128, 1024], "float32"), "psa": ("psum", [128, 512], "float32"),
 }
 for _b in range(4):
     SCRATCH["pr%d" % _b] = ("psum", [128, 512], "float32")
 for _t in range(R):
-    SCRATCH["win%d" % _t] = ("sbuf", [128, EW + 4 * C], "bfloat16")
+    for _j in range(NC):
+        SCRATCH["win%d%d" % (_t, _j)] = ("sbuf", [128, HW + 4 * C], "bfloat16")
     SCRATCH["inq%d" % _t] = ("sbuf", [128, K], Q8)
     SCRATCH["ins%d" % _t] = ("sbuf", [128, K], "uint8")
-for _t in range(R + 1):
+for _t in (0, R):
     SCRATCH["xq%d" % _t] = ("sbuf", [128, C], Q8)
     SCRATCH["xs%d" % _t] = ("sbuf", [128, C], "uint8")
 for _t in range(R - 1):
-    SCRATCH["vic%d" % _t] = ("sbuf", [128, EW], "bfloat16")
+    SCRATCH["vic%d" % _t] = ("sbuf", [128, 4 * K], "bfloat16")
     SCRATCH["pq%d" % _t] = ("sbuf", [128, K], Q8)
     SCRATCH["ps%dc" % _t] = ("sbuf", [128, K], "uint8")
 
-SEMAPHORES = ["lu", "lxa", "lxb", "la", "lw", "lv", "io1", "io2", "io3", "io4", "c0", "c1", "c2", "c3", "c3a", "c4", "c5", "c6",
-              "qa", "qb", "qin", "qv", "sa", "s1", "s2", "s2w", "rr", "mka", "mkb", "ha", "hb", "dd", "dsc", "dns",
-              "cma", "rsc", "sga", "sgb", "ac0", "ac1", "ac2", "ac3", "ac4", "acr", "ee",
-              "ck0", "ck1", "ck2", "ck3", "ck4", "df0", "df1", "tr0", "tr1",
-              "us", "b1s", "la1", "l1", "l2", "ra", "rb", "l3", "l40", "l41", "l42", "l43", "l50", "l51", "l52", "l53",
-              "ga", "gb", "sct", "lms", "lzs", "vo", "vg", "qp", "arr1", "arr2", "sent",
-              "ya", "yb", "yca", "ycb", "st1", "st2"]
+SEMAPHORES = ["lu", "lxa", "lxb", "la", "lw", "lv", "cp0", "cp1", "cp2", "io1", "io2", "io3", "io4", "io5",
+              "c0", "c1", "c2", "c3", "c3a", "c4", "c5", "c6", "c7",
+              "qa", "qb", "qin", "qv", "mu", "m1", "m2", "m2w", "m3", "rr", "ma", "mb", "ha", "hb",
+              "dd0", "dd1", "ds0", "ds1", "pd0", "pd1", "pr0", "pr1",
+              "cma", "cmb", "cmu", "rs0", "rs1", "su0", "su1", "sg0", "sg1", "sg2", "sg3", "acl", "ee0", "ee1", "ee2", "ee3",
+              "df0", "df1", "tr0", "tr1", "us0", "us1", "tm0", "tm1", "ps0", "ps1", "sr0", "sr1", "rf0", "rf1",
+              "of00", "of01", "of02", "of03", "of10", "of11", "of12", "of13",
+              "ga", "gb", "ls", "lm", "lz", "vo", "vg", "qp", "arr1", "arr2", "sent",
+              "ym0", "ym1", "yc0", "yc1", "st1", "st2"] + [x % k for x in ("ac%d", "k%d") for k in range(len(CHUNKS))]
 
 
 def rank_program(g, core, T, topo):
@@ -92,43 +135,25 @@ def rank_program(g, core, T, topo):
                 queues[q].wait_ge(T.sem[name], cnt[name])
                 seen[(q, name)] = cnt[name]
 
+    def win(t, j=0):
+        return T["win%d%d" % (t, j)]
+
     def state(t):
-        return (T["win%d" % t], EW) if t < R else (T.xfin, 0)
+        return (win(t), HW) if t < R else (T.xfin, 0)
 
     def quant_half(t, h):
         buf, o = state(t)
-        ev("qb" if h else "qa", V.quantize_mx(T["xq%d" % t][:, h * H2:(h + 1) * H2], T["xs%d" % t][:, h * H2:(h + 1) * H2],
-                                              buf[:, o + 4 * h * H2:o + 4 * (h + 1) * H2]))
+        xq, xs = T["xq%d" % (t // R * R)], T["xs%d" % (t // R * R)]
+        return V.quantize_mx(xq[:, h * H2:(h + 1) * H2], xs[:, h * H2:(h + 1) * H2], buf[:, o + 4 * h * H2:o + 4 * (h + 1) * H2])
 
     def own_mask(h):
-        w("v", "sa" if h else "s1")
-        ev("mkb" if h else "mka", V.tensor_tensor(T.msk[:, h * H2:(h + 1) * H2], (T.psa if h else T.ps1)[:, 0:H2], T.mt[:], A.min))
+        return V.tensor_tensor(T.msk[:, h * H2:(h + 1) * H2], (T.psa if h else T.ps1)[:, 0:H2], T.mt[:], A.min)
 
     def own_scan(h):
-        lo, hi = h * H2, (h + 1) * H2
-        w("v", "mkb" if h else "mka")
-        ev("hb" if h else "ha", V.tensor_tensor_scan(T.hh[:, lo:hi], T.kt[:], T.msk[:, lo:hi], 0.0, A.min, A.max))
+        return V.tensor_tensor_scan(T.hh[:, h * H2:(h + 1) * H2], T.kt[:], T.msk[:, h * H2:(h + 1) * H2], 0.0, A.min, A.max)
 
-    def scores(t, out, lo, hi, name):
-        ev(name, PE.matmul_mx(out, T.urq[:], T.urs[:], T["xq%d" % t][:, lo:hi], T["xs%d" % t][:, lo:hi], True, True))
-
-    def all_scores(t):
-        w("p", "qa")
-        scores(t, T.ps2[:, 0:C], 0, C, "s2")
-        scores(t, T.ps1[:, 0:C], 0, C, "s1")
-        scores(t, T.ps2[:, C:C + H2], 0, H2, "s2w")
-
-    def gather_half(t, h, q, es):
-        buf, o = state(t + 1)
-        for e in es:
-            w(q, "ee", "l%d%d" % (4 + h, e))
-            out = buf[:, o + 4 * h * H2 + e:o + 4 * (h + 1) * H2:4]
-            src = T["win%d" % t][:, 0:EW + 4 * C].indirect(T.soff[:, 32 * e + 16 * h:32 * e + 16 * h + 16])
-            ev("gb" if h else "ga", S.activation(out, src, F.Copy) if q == "s" else V.tensor_copy(out, src))
-
-    def listing(lo, hi):
-        w("v", "rb" if lo >= 16 else "ra", "io4", "sct")
-        ev("sct", V.tensor_copy(T.lst[:, 0:C].indirect(T.roff[:, lo:hi]), T.places[:, 16 * lo:16 * hi]))
+    def scores(out, lo, hi):
+        return PE.matmul_mx(out, T.urq[:], T.urs[:], T.xq0[:, lo:hi], T.xs0[:, lo:hi], True, True)
 
     def slot(c, lo, hi):
         return T.cb[:, SL * lo + c % 16:SL * hi:SL]
@@ -136,306 +161,267 @@ def rank_program(g, core, T, topo):
     def own(c):
         return T.hh[:, 16 * c + 15:16 * c + 16]
 
-    def compare(c):
-        lo, hi = 16 * c + 16, 16 * c + 16 + H2
-        w("v", "ha", "hb", "c0")
-        ev("cma", V.tensor_scalar(slot(c, lo, hi), T.ps1[:, lo:hi], own(c), None, A.is_lt))
+    def term(c, k):
+        return T.xt[:, XS * c + k:XS * c + k + 1]
 
     ev("lu", SY.dma_start(T.ub[:], T.u[:]), 16)
-    ev("lxb", S.dma_start(T.win0[:, EW + 4 * H2:EW + 4 * C], T.x[:, 4 * H2:4 * C]), 16)
-    ev("lxa", SY.dma_start(T.win0[:, EW:EW + 4 * H2], T.x[:, 0:4 * H2]), 16)
+    ev("lxb", S.dma_start(win(0)[:, HW + 4 * H2:HW + 4 * C], T.x[:, 4 * H2:4 * C]), 16)
+    ev("lxa", SY.dma_start(win(0)[:, HW:HW + 4 * H2], T.x[:, 0:4 * H2]), 16)
     w("y", "lxa")
     ev("la", SY.dma_start(T.ab[:], T.a[:]), 16)
     ev("lw", SY.dma_start(T.wq[:].bitcast(dt.uint8), T.wc[:]), 16)
     ev("lw", SY.dma_start(T.wp[:], T.ws[:]), 16)
     ev("lv", SY.dma_start(T.vb[:], T.v[:]), 16)
+    for j in range(1, NC):
+        ev("cp0", SY.dma_start(win(0, j)[:, HW:HW + 4 * C - j * M], T.x[:, j * M:4 * C]), 16)
 
     def count_up(name, out, pattern, base):
         ev(name, g.iota(out, pattern, base, 0, allow_small_or_imprecise_dtypes=True))
 
+    def zero(out):
+        ev("c0", S.activation(out, T.i16[:, 0:16], F.Identity, scale=0.0))
+
     ev("io1", g.iota(T.pcol[:], [[0, 1]], 0, 1))
-    ev("io1", g.iota(T.uoi[:], [[16, 8]], 0, 0))
-    count_up("io2", T.i16[:], [[0, 34], [1, 16]], 0)
-    count_up("io3", T.nb[:], [[16, 2], [0, 16]], 240)
+    count_up("io2", T.i16[:], [[0, 16], [1, 16]], 0)
+    ev("io5", g.iota(T.uoi[:], [[16, 8]], 0, 0))
     count_up("io3", T.i4[:], [[0, K // 4], [1, 4]], 0)
-    count_up("io3", T.jb[:], [[16, 32]], K)
-    count_up("io3", T.i3[:], [[0, 16], [1, 3]], 0)
+    count_up("io3", T.jb[:], [[16, 32]], HW // 4)
+    count_up("io3", T.i2[:], [[0, 8], [1, 2]], 0)
+    count_up("io3", T.nb[:], [[16, 2], [0, 16]], 240)
     count_up("io4", T.places[:], [[1, C]], 0)
-    for q in range(8):
-        ev("c0", V.memset(slot(q, 16 * q, 16 * q + 16), 0.0))
+    ev("c7", V.memset(T.xt[:], 0.0))
+    ev("c7", V.memset(T.kx[:], 1.0))
+    ev("c7", V.memset(T.cap[:], 0.0))
     w("v", "io1")
-    ev("c1", V.tensor_copy(T.uoff[:], T.uoi[:]))
     ev("c1", V.tensor_scalar(T.pint[:, 0:1], T.pcol[:], 15, None, A.bitwise_and))
     ev("c1", V.tensor_scalar(T.pint[:, 1:2], T.pcol[:], 3, None, A.bitwise_and))
     ev("c1", V.tensor_scalar(T.pint[:, 2:3], T.pcol[:], 2, 3, A.arith_shift_right, A.bitwise_and))
     ev("c1", V.tensor_scalar(T.pint[:, 3:4], T.pcol[:], 4, 1, A.arith_shift_right, A.bitwise_and))
-    for q in range(8, 16):
-        ev("c0", V.memset(slot(q, 16 * q, 16 * q + 16), 0.0))
+    ev("c7", V.memset(T.k0[:], 1.0))
     w("v", "c1")
-    ev("c2", V.tensor_copy(T.pf[:, 0:4], T.pint[:]))
-    ev("c0", V.memset(T.a1[:], 0.0))
-    ev("c0", V.memset(T.a2[:], 0.0))
-    ev("c6", V.memset(T.tin[:, 0:16], 0.0))
-    ev("c6", V.memset(T.tin[:, 16 + C:32 + C], 0.0))
-    ev("c6", V.memset(T.z2[:, 0:64:2], 0.0))
-    ev("c0", V.memset(T.cb[:, SL - 1:SL * C:SL], 0.0))
+    ev("c2", V.tensor_copy(T.pf[:], T.pint[:]))
+    ev("c6", V.memset(T.cb[:, SL - 1:SL * C:SL], 0.0))
     w("v", "c2", "io2")
-    ev("c3a", V.tensor_scalar(T.mh[:], T.i16[:, 0:H2], T.pf[:, 0:1], 0.5, A.is_equal, A.subtract))
-    ev("c3", V.tensor_scalar(T.kt[:], T.i16[:, 0:H2], 0.5, BIG / 16, A.subtract, A.mult))
-    ev("c6", V.tensor_scalar(T.k0[:], T.i16[:], 1.0, None, A.min))
-    ev("c3", (w("v", "c3a"), V.tensor_scalar(T.mt[:], T.mh[:], BIG, None, A.mult))[1])
+    ev("c3a", V.tensor_scalar(T.mh[:], T.i16[:], T.pf[:, 0:1], 0.5, A.is_equal, A.subtract))
+    ev("c3", V.tensor_scalar(T.kt[:], T.i16[:], 0.5, BIG / 16, A.subtract, A.mult))
+    w("v", "io5", "c7")
+    ev("c1", V.tensor_copy(T.uoff[:], T.uoi[:]))
+    ev("c6", V.memset(T.k0[:, 0:544:16], 0.0))
+    ev("c6", V.memset(T.xt[:, XS - 1:32 * XS:XS], -(K - 0.5) * FAR))
+    w("v", "c3a")
+    ev("c3", V.tensor_scalar(T.mt[:], T.mh[:], BIG, None, A.mult))
+    w("s", "io2")
+    for q in range(16):
+        zero(slot(q, 16 * q, 16 * q + 16))
+    zero(T.tin[:, 0:16])
+    zero(T.tin[:, 16 + C:32 + C])
     w("v", "lu")
     ev("c4", V.quantize_mx(T.uq[:], T.us[:], T.ub[:]))
-    ev("c6", V.tensor_scalar(T.pf[:, 4:5], T.pf[:, 3:4], 1.0, None, A.subtract))
-    ev("c6", V.tensor_scalar(T.pf[:, 5:6], T.pf[:, 3:4], -1.0, None, A.mult))
-    ev("c6", V.tensor_scalar(T.co[:, 0:CST * len(CHUNKS):CST], T.i16[:, 0:len(CHUNKS)], 0.0, None, A.mult))
-    w("v", "c4")
+    w("s", "c4", "c1", "c7")
+    ev("c5", S.activation(T.urs[:], T.us[:].indirect(T.uoff[:, 0:8]), F.Copy))
+    ev("c6", V.memset(T.kx[:, 0:16 * XS:XS], 0.0))
+    ev("c6", V.memset(T.kx[:, 3:16 * XS:XS], float(M)))
+    ev("c6", V.memset(T.kx[:, XS - 1:16 * XS:XS], FAR / M))
+    ev("c6", V.memset(T.cap[:, XS - 2:32 * XS:XS], FAR))
+    w("v", "c4", "c1")
     ev("c5", V.tensor_copy(T.urq[:].bitcast(dt.uint32), T.uq[:].bitcast(dt.uint32).indirect(T.uoff[:, 0:8])))
-    ev("c5", V.tensor_copy(T.urs[:], T.us[:].indirect(T.uoff[:, 0:8])))
     w("v", "lxb")
-    quant_half(0, 1)
+    ev("qb", quant_half(0, 1))
     w("p", "c5", "qb")
-    scores(0, T.psa[:, 0:H2], H2, C, "sa")
+    ev("mu", scores(T.psa[:, 0:H2], H2, C))
     w("v", "lxa")
-    quant_half(0, 0)
-    all_scores(0)
-    w("v", "c3")
-    own_mask(1)
+    ev("qa", quant_half(0, 0))
+    w("p", "qa")
+    ev("m2", scores(T.ps2[:, 0:C], 0, C))
+    ev("m1", scores(T.ps1[:, 0:C], 0, C))
+    ev("m2w", scores(T.ps2[:, C:C + H2], 0, H2))
+    ev("m3", scores(T.pr0[:, 0:C], 0, C))
+    ev("c6", V.tensor_scalar(T.co[:, 0:CST * len(CHUNKS):CST], T.i16[:, 0:len(CHUNKS)], 0.0, None, A.mult))
+    w("v", "c3", "mu")
+    ev("mb", own_mask(1))
     w("v", "io3")
     ev("c6", V.tensor_scalar(T.m4[:], T.i4[:], T.pf[:, 2:3], None, A.is_equal))
     ev("c6", V.tensor_scalar(T.k4[:], T.i4[:], T.pf[:, 2:3], None, A.not_equal))
-    own_scan(1)
-    own_mask(0)
-    ev("c6", V.tensor_scalar(T.d2[:, 0:64:2], T.jb[:], T.pf[:, 0:1], 4.0, A.add, A.mult))
     ev("c6", V.tensor_scalar(T.nn[:], T.nb[:], T.pf[:, 0:1], None, A.add))
-    own_scan(0)
-    ev("c6", V.tensor_scalar(T.k3[:], T.i3[:], 1.0, None, A.min))
+    w("v", "mb")
+    ev("hb", own_scan(1))
+    w("v", "m1")
+    ev("ma", own_mask(0))
+    ev("c6", V.tensor_scalar(T.m1[:], T.i2[:], T.pf[:, 3:4], -float(M), A.is_equal, A.mult))
+    ev("c6", V.tensor_scalar(T.m2[:], T.i2[:], T.pf[:, 3:4], -float(M), A.not_equal, A.mult))
+    ev("c6", V.tensor_scalar(T.cap[:, XS - 1:32 * XS:XS], T.jb[:], T.pf[:, 0:1], 4.0, A.add, A.mult))
+    w("v", "ma")
+    ev("ha", own_scan(0))
 
-    for t in range(R):
-        win = T["win%d" % t]
+    ops = {}
 
-        def signs(c, name):
-            o = H2 * (c - NV)
-            ev(name, S.activation(T.sg[:, o:o + 240], T.ps2[:, 16 * c + 16:16 * c + 256], F.Sign, bias=own(c), scale=-1.0))
+    def op(name, t, sem, needs, call):
+        ops["%s.%d" % (name, t)] = ("%s.%d" % (sem, t), [n if "." in n else "%s.%d" % (n, t) for n in needs], call)
 
-        def above(c, name):
-            o, lo = H2 * (c - NV), 16 * c + 16
-            ev(name, S.activation(slot(c, lo, C), T.sg[:, o:o + C - lo], F.Relu, accum_out=T.a1[:, c:c + 1]))
+    def level(lo, hi):
+        return "ac%d" % min(k for k, (a, b) in enumerate(CHUNKS) if a < hi and lo < b)
 
-        def below(c, name):
-            o, n = H2 * (c - NV) + C - 16 * c - 16, 16 * (c - 16)
-            ev(name, S.activation(slot(c, 0, n), T.sg[:, o:o + n], F.Sign, bias=1.0, accum_out=T.a2[:, c:c + 1]))
+    def describe(t):
+        last, old = t == R - 1, ".%d" % (t - 1)
+        buf, first = state(t + 1)
 
-        w("s", "s2", "hb")
-        signs(16, "sga")
-        w("s", "s2w")
-        for c in range(17, 31):
-            signs(c, "sga")
-            if t > 0 and c == 16 + VG:
-                w("s", "vo")
-                ev("vg", S.activation(T["vic%d" % (t - 1)][:],
-                                      T["win%d" % (t - 1)][:, EW:EW + 4 * C].indirect(T.voff[:, 0:40]), F.Copy))
-        signs(31, "sgb")
-        w("s", "sga", "c0")
-        for c in range(NV, 31):
-            above(c, "ac0" if c <= 20 else "ac1" if c <= 27 else "ac2")
-        w("s", "sgb")
-        for c in range(31, 16, -1):
-            below(c, "ac3" if c >= 25 else "ac4")
+        def signs(name, c, sem, needs, o, src, n):
+            op(name, t, sem, needs, lambda q: [S.activation(T.sg[:, o:o + n], src, F.Sign, bias=own(c), scale=-1.0)])
 
-        for c in range(1 if t else 0, NV):
-            compare(c)
-            if t > 0 and c == QP:
-                w("v", "vg")
-                pq, ps = T["pq%d" % (t - 1)], T["ps%dc" % (t - 1)]
-                ev("qp", V.quantize_mx(pq[:], ps[:], T["vic%d" % (t - 1)][:]))
-                w("g", "qp")
-                arr = T.sem["arr%d" % t]
-                g.remote_dma(T["inq%d" % t][:].bitcast(dt.uint8), pq[:].bitcast(dt.uint8), arr, T.sem.sent, pid, rid, emask)
-                g.remote_dma(T["ins%d" % t][:], ps[:], arr, T.sem.sent, pid, rid, emask)
-                cnt["sent"] = cnt.get("sent", 0) + 2 * n_out
-                cnt["arr%d" % t] = 2 * n_in
-        ev("dd", V.tensor_tensor(T.cb[:, 16:SL * C:SL], T.ps1[:], T.hh[:], A.is_lt))
-        if t == 0:
-            w("v", "la", "lv")
-            ev("qin", V.quantize_mx(T.inq0[:], T.ins0[:], T.ab[:]))
-            ev("qv", V.quantize_mx(T.vq[:], T.vs[:], T.vb[:]))
-            w("p", "qin", "lw")
-        else:
-            w("p", "arr%d" % t)
-        for b in range(4):
-            ev("rr", PE.matmul_mx(T["pr%d" % b][:, 0:K], T.wq[:, 128 * b:128 * b + 128], T.wp[:, 128 * b:128 * b + 128],
-                                  T["inq%d" % t][:], T["ins%d" % t][:], True, True))
-        nr = NV - RS
-        w("s", "cma")
-        for c in range(nr, NV):
-            o = H2 * (c - nr)
-            ev("acr", S.activation(T.jk[:, o:o + H2], slot(c, 16 * c + 16, 16 * c + 16 + H2), F.Identity, accum_out=T.a1[:, c:c + 1]))
-        w("s", "rr")
-        for b in range(4):
-            ev("ee", S.activation(win[:, b:EW:4], T["pr%d" % b][:, 0:K], F.Relu, scale=0.03125))
-        left = list(range(nr))
+        def above(c, sem, need, o, lo, hi):
+            op("a%d" % c, t, sem, [need], lambda q: [S.activation(slot(c, lo, hi), T.sg[:, o:o + hi - lo], F.Relu, accum_out=term(c, 1))])
 
-        def rows(n):
-            w("v", "cma")
-            for _ in range(n):
-                c = left.pop()
-                lo = 16 * c + 16
-                ev("rsc", V.tensor_tensor_scan(T.ro[:, 128 * c:128 * c + 128], slot(c, lo, lo + 128), slot(c, lo + 128, lo + H2),
-                                               0.0, A.add, A.add))
+        def below(c, need, o, n):
+            op("b%d" % c, t, level(0, n), [need], lambda q: [
+                S.activation(slot(c, 0, n), T.sg[:, o:o + n], F.Sign, bias=1.0, accum_out=term(c, 2))])
 
-        rows(nr - 7)
-        w("v", "dd", "c6")
-        ev("dsc", V.tensor_tensor_scan(T.ds[:], T.k0[:, 0:C], T.cb[:, 16:SL * C:SL], 0.0, A.mult, A.add))
+        for c in range(NS):
+            o, lo = H2 * (16 + c), 16 * c + 16
+            signs("s%d" % c, c, "sg3", ["m3", "ha"], o, T.pr0[:, lo:lo + H2], H2)
+            above(c, "acl", "sg3", o, lo, lo + H2)
+        for c in range(16, 32):
+            o, lo = H2 * (c - 16), 16 * c + 16
+            up, low = ("su0" if c < UG else "su1") if c < WH else "sg0", "sg0" if c >= WH else "sg1" if c >= WG else "sg2"
+            if NV <= c < WH:
+                signs("u%d" % c, c, up, ["m2", "hb"], o, T.ps2[:, lo:C], C - lo)
+            if NV <= c < 31:
+                above(c, level(lo, C), up, o, lo, C)
+            if c > 16:
+                a = C if c < WH else lo
+                signs("s%d" % c, c, low, ["m2", "m2w", "hb"], o + a - lo, T.ps2[:, a:lo + 240], lo + 240 - a)
+                below(c, low, o + C - lo, lo + 240 - C)
 
-        def chunk(k):
-            lo, hi = CHUNKS[k]
-            w("v", "ac%d" % k)
-            ev("ck%d" % k, V.tensor_tensor_scan(T.co[:, CST * k + 1:CST * k + 1 + 9 * (hi - lo)], T.cb[:, SL * lo:SL * hi:2],
-                                                T.cb[:, SL * lo + 1:SL * hi:2], 0.0, A.add, A.add))
+        for c in range(NS, NV):
+            lo = 16 * c + 16
+            n = (min(lo + H2, C) - lo) // 2
+            sem, src = ("cma" if c <= 8 else "cmb", T.ps1[:, lo:lo + 2 * n]) if c < 16 else ("cmu", T.psa[:, lo - H2:H2])
+            op("c%d" % c, t, sem, ["ha", "m1"] if c < 16 else ["hb"], lambda q, c=c, lo=lo, n=n, src=src: [
+                V.tensor_scalar(slot(c, lo, lo + 2 * n), src, own(c), None, A.is_lt)])
+            op("r%d" % c, t, "rs%d" % (c // 16), [sem], lambda q, c=c, lo=lo, n=n: [
+                V.tensor_tensor_scan(T.ro[:, 128 * c + 128 - n:128 * c + 128], slot(c, lo, lo + n), slot(c, lo + n, lo + 2 * n), 0.0, A.add, A.add)])
 
-        def steps(k):
-            lo, hi = CHUNKS[k]
+        for k, (lo, hi) in enumerate(CHUNKS):
             o, n = CST * k, 9 * (hi - lo)
-            w("v", "ck%d" % k)
-            ev("df0" if k < 3 else "df1",
-               V.tensor_tensor_scan(T.tin[:, 16 + lo:16 + hi], T.co[:, o + 9:o + n + 1:9], T.co[:, o:o + n:9], 0.0, A.max, A.subtract))
-
-        def turn(s):
-            lo, hi, lo2, hi2 = STAGES[s]
-            w("v", "df%d" % s)
-            ev("tr%d" % s, V.transpose(T.t1[:, lo:hi], T.tin[:, 16 + lo:16 + hi]))
-            ev("tr%d" % s, V.transpose(T.t2[:, lo2:hi2], T.tin[:, lo2:hi2]))
-
-        def sums(s):
-            lo, hi, lo2, hi2 = STAGES[s]
-            w("v", "tr%d" % s)
-            ev("us", V.tensor_tensor_scan(T.u1[:, lo:hi], T.k0[:, lo:hi], T.t1[:, lo:hi], 0.0, A.mult, A.add))
-            ev("us", V.tensor_tensor_scan(T.u2[:, lo2:hi2], T.k0[:, lo2:hi2], T.t2[:, lo2:hi2], 0.0, A.mult, A.add))
-
-        even, odd = T.pf[:, 4:5], T.pf[:, 5:6]
-
-        def terms(h):
-            o, x = H2 * h, 48 * h
-            w("v", "us")
-            ev("la1", V.tensor_scalar(T.x3[:, x + 1:x + 48:6], T.u1[:, o + 15:o + H2:32], even, None, A.mult))
-            ev("la1", V.tensor_scalar(T.x3[:, x + 4:x + 48:6], T.u2[:, o + 47:o + H2 + 32:32], even, None, A.mult))
-            ev("la1", V.tensor_scalar(T.x3[:, x + 2:x + 48:6], T.u2[:, o + 31:o + H2:32], odd, None, A.mult))
-            ev("la1", V.tensor_scalar(T.x3[:, x + 5:x + 48:6], T.u1[:, o + 31:o + H2:32], odd, None, A.mult))
-
-        def positions(h):
-            x = 48 * h
-            w("v", "la1")
-            ev("l1", V.tensor_tensor_scan(T.p3[:, x:x + 48], T.k3[:], T.x3[:, x:x + 48], 0.0, A.mult, A.add))
-
-        def chosen(h):
-            pos, y = T.p3[:, 48 * h + 2:48 * h + 48:3], 32 * h
-            w("v", "l1")
-            ev("l2", V.tensor_scalar(T.z2[:, y + 1:y + 32:2], pos, K - 0.5, None, A.is_gt))
-            ev("l2", V.tensor_scalar(T.d2[:, y + 1:y + 32:2], pos, float(K), 4.0, A.min, A.mult))
-            ev("rb" if h else "ra", V.tensor_copy(T.roff[:, 16 * h:16 * h + 16], pos))
-
-        def sources(h):
-            y = 32 * h
-            w("v", "l2")
-            ev("l3", V.tensor_tensor_scan(T.i2[:, y:y + 32], T.z2[:, y:y + 32], T.d2[:, y:y + 32], 0.0, A.mult, A.max))
-
-        def offsets(h):
-            w("v", "l3")
+            rows = ["ac%d" % i for i in range(0 if k < 3 else 3, k + 1)] + ["cma", "c6.0", "c0.0"]
+            rows += ["cmb"] * (hi > 160) + ["acl"] * (lo < 16 * NS + H2) + ["dd0"] * (lo < H2) + ["dd1", "cmu"] * (hi > H2)
+            op("k%d" % k, t, "k%d" % k, rows, lambda q, lo=lo, hi=hi, o=o, n=n: [
+                V.tensor_tensor_scan(T.co[:, o + 1:o + 1 + n], T.cb[:, SL * lo:SL * hi:2], T.cb[:, SL * lo + 1:SL * hi:2], 0.0, A.add, A.add)])
+            op("d%d" % k, t, "df1" if k < 3 else "df0", ["k%d" % k], lambda q, lo=lo, hi=hi, o=o, n=n: [
+                V.tensor_tensor_scan(T.tin[:, 16 + lo:16 + hi], T.co[:, o + 9:o + n + 1:9], T.co[:, o:o + n:9], 0.0, A.max, A.subtract)])
+        for h in range(2):
+            lo, n2, x, n, y, ab = H2 * h, H2 + 32 * h, 16 * XS * h, 16 * XS, 800 * h, "ab"[h]
+            r0, r1 = (16, NV) if h else (NS, 16)
+            pair = T.cb[:, SL * lo + 16:SL * (lo + H2):SL]
+            op("dd%d" % h, t, "dd%d" % h, ["h" + ab], lambda q, h=h, lo=lo, pair=pair: [
+                V.tensor_tensor(pair, (T.psa if h else T.ps1)[:, 0:H2], T.hh[:, lo:lo + H2], A.is_lt)])
+            op("ds%d" % h, t, "ds%d" % h, ["dd%d" % h, "c6.0"], lambda q, lo=lo, pair=pair: [
+                V.tensor_tensor_scan(T.ds[:, lo:lo + H2], T.k0[:, 0:H2], pair, 0.0, A.mult, A.add)])
+            op("pd%d" % h, t, "pd%d" % h, ["ds%d" % h], lambda q, h=h, lo=lo, x=x, n=n: [
+                V.tensor_tensor(T.xt[:, x:x + n:XS], T.ds[:, lo + 15:lo + H2:16], T.nn[:, 16 * h:16 * h + 16], A.add)])
+            if r1 > r0:
+                op("pr%d" % h, t, "pr%d" % h, ["rs%d" % h], lambda q, r0=r0, r1=r1: [
+                    V.tensor_copy(T.xt[:, 1 + r0 * XS:r1 * XS:XS], T.ro[:, 127 + 128 * r0:128 * r1:128])])
+            op("tr%d" % h, t, "tr%d" % h, ["df1", "df%d" % h], lambda q, lo=lo, n2=n2, y=y: [
+                V.transpose(T.t3[:, y:y + H2], T.tin[:, 16 + lo:16 + lo + H2]),
+                V.transpose(T.t3[:, H2 + lo:H2 + lo + n2], T.tin[:, lo:lo + n2])])
+            op("us%d" % h, t, "us%d" % h, ["tr%d" % h], lambda q, h=h, n2=n2: [
+                V.tensor_tensor_scan(T.u3[:, C * h:C * h + H2 + n2], T.k0[:, 0:H2 + n2], T.t3[:, C * h:C * h + H2 + n2], 0.0, A.mult, A.add)])
+            op("tm%d" % h, t, "tm%d" % h, ["us1", "us%d" % h], lambda q, lo=lo, x=x, n=n, y=y: [
+                V.tensor_tensor(T.xt[:, x + 3:x + n:XS], T.u3[:, y + 15:y + H2:16], T.m1[:], A.mult),
+                V.tensor_tensor(T.xt[:, x + 4:x + n:XS], T.u3[:, H2 + lo + 31:H2 + lo + 31 + H2:16], T.m2[:], A.mult)])
+            sums = ["ac%d" % k for k in range(len(CHUNKS))] if h else ["acl"]
+            op("ps%d" % h, t, "ps%d" % h, ["tm%d" % h, "pd%d" % h, "pr%d" % h] + sums, lambda q, x=x, n=n: [
+                V.tensor_tensor_scan(T.px[:, x:x + n], T.kx[:], T.xt[:, x:x + n], 0.0, A.mult, A.add)])
+            op("sr%d" % h, t, "sr%d" % h, ["ps%d" % h], lambda q, x=x, n=n: [
+                V.tensor_tensor_scan(T.sx[:, x:x + n], T.px[:, x:x + n], T.cap[:, x:x + n], 0.0, A.max, A.min)])
+            op("rf%d" % h, t, "rf%d" % h, ["ps%d" % h], lambda q, h=h, x=x, n=n: [
+                V.tensor_scalar(T.roff[:, 16 * h:16 * h + 16], T.px[:, x + XS - 2:x + n:XS], 1.0 / M, None, A.mult)])
+            for d in range(M):
+                op("of%d%d" % (h, d), t, "of%d%d" % (h, d), ["sr%d" % h], lambda q, h=h, d=d, x=x, n=n: [
+                    V.tensor_scalar(T.soff[:, 32 * d + 16 * h:32 * d + 16 * h + 16], T.sx[:, x + XS - 1:x + n:XS], float(d), None, A.add)])
             for e in range(4):
-                ev("l%d%d" % (4 + h, e), V.tensor_scalar(T.soff[:, 32 * e + 16 * h:32 * e + 16 * h + 16],
-                                                         T.i2[:, 32 * h + 1:32 * h + 32:2], float(e), None, A.add))
+                j, d = e // M, e % M
+                out = buf[:, first + 4 * lo + e:first + 4 * (lo + H2):4]
+                src = win(t, j)[:, 0:HW + 4 * C - j * M].indirect(T.soff[:, 32 * d + 16 * h:32 * d + 16 * h + 16])
+                op("g%s%d" % (ab, e), t, "g" + ab, ["ee%d" % j, "of%d%d" % (h, d)] + (["cp%d" % t] if j else []),
+                   lambda q, out=out, src=src: [S.activation(out, src, F.Copy) if q == "s" else V.tensor_copy(out, src)])
+            op("q" + ab, t + 1, "q" + ab, ["g%s.%d" % (ab, t)] + ([] if h or last else ["m2"]), lambda q, h=h: [quant_half(t + 1, h)])
+        for i, (lo, hi) in enumerate(PIECES):
+            op("ls%d" % i, t, "ls", ["rf%d" % (lo // 16), "io4.0"], lambda q, lo=lo, hi=hi: [
+                (w(q, "ls"), V.tensor_copy(T.lst[:, 0:C].indirect(T.roff[:, lo:hi]), T.places[:, 16 * lo:16 * hi]))[1]])
 
-        chunk(0)
-        w("v", "dsc")
-        ev("dns", V.tensor_tensor(T.dn[:], T.ds[:, 15:C:16], T.nn[:], A.add))
-        chunk(1)
-        steps(0)
-        chunk(2)
-        steps(1)
-        rows(2)
-        steps(2)
-        rows(1)
-        turn(0)
-        chunk(3)
-        sums(0)
-        steps(3)
-        rows(1)
-        w("v", "dns", "ac4")
-        ev("b1s", V.tensor_tensor(T.b1[:], T.dn[:, 16:32], T.a2[:, 16:32], A.add))
-        chunk(4)
-        w("v", "b1s")
-        ev("la1", V.tensor_tensor(T.x3[:, 48:96:3], T.b1[:], T.a1[:, 16:32], A.add))
-        terms(1)
-        steps(4)
-        rows(2)
-        positions(1)
-        turn(1)
-        rows(1)
-        chosen(1)
-        sums(1)
-        sources(1)
-        w("v", "rsc", "acr")
-        ev("la1", V.tensor_tensor(T.x3[:, 0:3 * nr:3], T.dn[:, 0:nr], T.ro[:, 127:128 * nr:128], A.add))
-        ev("la1", V.tensor_tensor(T.x3[:, 3 * nr:48:3], T.dn[:, nr:16], T.a1[:, nr:16], A.add))
-        offsets(1)
-        gather_half(t, 1, "s", range(4))
-        terms(0)
-        listing(16, 20)
-        positions(0)
-        listing(20, 24)
-        chosen(0)
-        listing(24, 28)
-        sources(0)
-        listing(28, 32)
-        offsets(0)
-        gather_half(t, 0, "s", range(4 - GV[t]))
-        gather_half(t, 0, "v", range(4 - GV[t], 4))
+        if t == 0:
+            op("qin", t, "qin", ["la"], lambda q: [V.quantize_mx(T.inq0[:], T.ins0[:], T.ab[:])])
+            op("qv", t, "qv", ["lv"], lambda q: [V.quantize_mx(T.vq[:], T.vs[:], T.vb[:])])
+        op("rr", t, "rr", ["sg3", "m3"] + (["qin", "lw"] if t == 0 else ["arr%d%s" % (t, old)]), lambda q: [
+            PE.matmul_mx(T["pr%d" % b][:, 0:K], T.wq[:, 128 * b:128 * b + 128], T.wp[:, 128 * b:128 * b + 128],
+                         T["inq%d" % t][:], T["ins%d" % t][:], True, True) for b in range(4)])
+        for b in range(4):
+            out, src = win(t, b // M)[:, b % M:HW:M], T["pr%d" % b][:, 0:K]
+            op("e%d" % b, t, "ee%d" % (b // M), ["rr"], lambda q, out=out, src=src: [
+                S.activation(out, src, F.Relu, scale=0.03125) if q == "s" else V.tensor_scalar(out, src, 0.0, 0.03125, A.max, A.mult)])
 
-        if t < R - 1:
-            w("v", "gb")
-            quant_half(t + 1, 1)
-            w("p", "qb")
-            scores(t + 1, T.psa[:, 0:H2], H2, C, "sa")
-            listing(0, 8)
-            w("v", "ga")
-            quant_half(t + 1, 0)
-            all_scores(t + 1)
-            own_mask(1)
-            listing(8, 12)
-            own_scan(1)
-            listing(12, 16)
-            own_mask(0)
-            w("v", "sct")
-            ev("lms", V.tensor_tensor_scan(T.lm[:], T.lst[:, 0:K], T.m4[:], 0.0, A.max, A.mult))
-            own_scan(0)
-            w("v", "lms")
-            ev("lzs", V.tensor_tensor_scan(T.lz[:], T.k4[:], T.lm[:], 0.0, A.mult, A.add))
-            compare(0)
-            w("v", "lzs")
-            ev("vo", V.tensor_scalar(T.voff[:], T.lz[:, 3:K:4], 4.0, T.pf[:, 1:2], A.mult, A.add))
+        if not last:
+            u = t + 1
+            op("mu", u, "mu", ["qb"], lambda q: [scores(T.psa[:, 0:H2], H2, C)])
+            op("m2", u, "m2", ["qb"], lambda q: [scores(T.ps2[:, 0:C], 0, C)])
+            op("m2w", u, "m2w", ["qa"], lambda q: [scores(T.ps2[:, C:C + H2], 0, H2)])
+            op("m1", u, "m1", ["qa", "qb"], lambda q: [scores(T.ps1[:, 0:C], 0, C)])
+            op("m3", u, "m3", ["qa", "qb"], lambda q: [scores(T.pr0[:, 0:C], 0, C)])
+            for h in range(2):
+                op("m" + "ab"[h], u, "m" + "ab"[h], ["mu" if h else "m1"], lambda q, h=h: [own_mask(h)])
+                op("h" + "ab"[h], u, "h" + "ab"[h], ["m" + "ab"[h]], lambda q, h=h: [own_scan(h)])
+                op("cp%d" % h, u, "cp%d" % u, ["g%s.%d" % ("ab"[h], t)], lambda q, h=h: [
+                    SY.dma_start(win(u, j)[:, HW + max(4 * h * H2 - j * M, 0):HW + 4 * (h + 1) * H2 - j * M],
+                                 win(u)[:, HW + max(4 * h * H2, j * M):HW + 4 * (h + 1) * H2]) for j in range(1, NC)])
+            vic, pq, ps = T["vic%d" % t], T["pq%d" % t], T["ps%dc" % t]
+            gone = win(t)[:, HW:HW + 4 * C].indirect(T.voff[:, 0:40])
+            op("lm", t, "lm", ["ls"], lambda q: [V.tensor_tensor_scan(T.lm[:], T.lst[:, 0:K], T.m4[:], 0.0, A.max, A.mult)])
+            op("lz", t, "lz", ["lm"], lambda q: [V.tensor_tensor_scan(T.lz[:], T.k4[:], T.lm[:], 0.0, A.mult, A.add)])
+            op("vo", t, "vo", ["lz"], lambda q: [V.tensor_scalar(T.voff[:], T.lz[:, 3:K:4], 4.0, T.pf[:, 1:2], A.mult, A.add)])
+            op("vg", t, "vg", ["vo"], lambda q: [S.activation(vic[:], gone, F.Copy) if q == "s" else V.tensor_copy(vic[:], gone)])
+            op("qp", t, "qp", ["vg"], lambda q: [V.quantize_mx(pq[:], ps[:], vic[:])])
+
+            def send(q):
+                arr = T.sem["arr%d" % u]
+                g.remote_dma(T["inq%d" % u][:].bitcast(dt.uint8), pq[:].bitcast(dt.uint8), arr, T.sem.sent, pid, rid, emask)
+                g.remote_dma(T["ins%d" % u][:], ps[:], arr, T.sem.sent, pid, rid, emask)
+                cnt["sent"] = cnt.get("sent", 0) + 2 * n_out
+                cnt["arr%d" % u] = 2 * n_in
+                return []
+
+            op("send", t, "arr%d" % u, ["qp"], send)
         else:
             xq, xs = T["xq%d" % R], T["xs%d" % R]
-            for h, ps in ((1, T.ps1), (0, T.psa)):
-                lo, hi = h * H2, (h + 1) * H2
-                qn, yn, cn = ("qb", "yb", "ycb") if h else ("qa", "ya", "yca")
-                w("v", "gb" if h else "ga")
-                quant_half(R, h)
-                w("p", qn, "qv")
-                ev(yn, PE.matmul_mx(ps[:, 0:H2], T.vq[:], T.vs[:], xq[:, lo:hi], xs[:, lo:hi], True, True))
-                w("y", qn)
-                ev("st1", SY.dma_start(T.oc[:, 4 * lo:4 * hi], xq[:, lo:hi].bitcast(dt.uint8)), 16)
-                w("s", yn)
-                ev(cn, S.activation(T.ysb[:, lo:hi], ps[:, 0:H2], F.Copy))
-            listing(0, 16)
-            for k in range(4):
-                ev("st1", SY.dma_start(T.osc[4 * k:4 * k + 4, :], xs[32 * k:32 * k + 4, :]), 16)
-            for h in (1, 0):
-                lo, hi = h * H2, (h + 1) * H2
-                w("s", "ycb" if h else "yca")
-                ev("st2", S.dma_start(T.y[:, lo:hi], T.ysb[:, lo:hi]), 16)
-            w("y", "sct")
-            ev("st1", SY.dma_start(T.ol[:], T.lst[0:128:16, 0:K]), 16)
+            for h, ps in ((0, T.ps1), (1, T.psa)):
+                lo, hi, qn = h * H2, (h + 1) * H2, "q" + "ab"[h]
+                op("ym%d" % h, R, "ym%d" % h, [qn, "qv.0"], lambda q, ps=ps, lo=lo, hi=hi: [
+                    PE.matmul_mx(ps[:, 0:H2], T.vq[:], T.vs[:], xq[:, lo:hi], xs[:, lo:hi], True, True)])
+                op("yc%d" % h, R, "yc%d" % h, ["ym%d" % h], lambda q, ps=ps, lo=lo, hi=hi: [
+                    S.activation(T.ysb[:, lo:hi], ps[:, 0:H2], F.Copy) if q == "s" else V.tensor_copy(T.ysb[:, lo:hi], ps[:, 0:H2])])
+                op("yd%d" % h, R, "st2", ["yc%d" % h], lambda q, lo=lo, hi=hi: [queues[q].dma_start(T.y[:, lo:hi], T.ysb[:, lo:hi])])
+                op("oc%d" % h, R, "st1", [qn], lambda q, lo=lo, hi=hi: [
+                    queues[q].dma_start(T.oc[:, 4 * lo:4 * hi], xq[:, lo:hi].bitcast(dt.uint8))])
+            op("osc", R, "st1", ["qa", "qb"], lambda q: [
+                queues[q].dma_start(T.osc[4 * k:4 * k + 4, :], xs[32 * k:32 * k + 4, :]) for k in range(4)])
+            op("ol", R, "st1", ["ls.%d" % t], lambda q: [queues[q].dma_start(T.ol[:], T.lst[0:128:16, 0:K])])
+
+    for t in range(R):
+        describe(t)
+
+    todo = {q: ORDER[q].split() for q in ORDER}
+    left = {}
+    for name in ops:
+        left[ops[name][0]] = left.get(ops[name][0], 0) + 1
+    for _ in range(len(ops)):
+        for q in todo:
+            while todo[q] and not any(left.get(n, 0) for n in ops[todo[q][0]][1]):
+                sem, needs, call = ops[todo[q].pop(0)]
+                w(q, *[n.split(".")[0] for n in needs])
+                for ins in call(q):
+                    ev(sem.split(".")[0], ins, 16 if sem[:2] in ("cp", "st") else 1)
+                left[sem] -= 1
+    assert not any(left.values()), [(q, todo[q][0]) for q in todo if todo[q]]
 
     for name in sorted(cnt):
         if max([v for (q, n), v in seen.items() if n == name] + [0]) < cnt[name]:

@@ -1,17 +1,16 @@
 from concourse.mybir import dt, AluOpType, ActivationFunctionType
 
 C, K, R, NR = 512, 160, 3, 4
-NS = 2
-NV = 18
-WH = 28
-UG = 22
-WG = 24
-NC = 2
+NSR = (2, 3, 3)
+NVR = (18, 20, 20)
+RSR = (2, 2, 0)
+WH, UG, WG = 28, 22, 24
+NC = 4
 CHUNKS = ((240, 352), (352, 464), (464, 512), (128, 240), (48, 128), (0, 48))
 PIECES = ((16, 20), (20, 24), (24, 28), (28, 32), (0, 8), (8, 16))
 M = 4 // NC
 HW = M * K
-H2 = C // 2
+H2, Q3 = C // 2, 3 * C // 4
 SL = 18
 XS = 6
 BIG = 2e29
@@ -19,41 +18,39 @@ FAR = 8192.0
 CST = 1160
 Q8 = "float8_e4m3fn_x4"
 
-ROUND = {
-    "v1": """c2 c3 c4 c5 c6 c7 c8 c9 c10 qp- c11 c12 c13 c14 c15 dd0 r2 k1 k0 k2 r3 ds0 r4 d1 d0 d2 r5 r6 r7 r8 pd0 tr1 r9 r10 r11 r12 r13 r14
-us1 k3 tm1 k4 ps1 k5 sr1 d4 d3 d5 of10 r15 rf1 tr0 pr0 ls0 us0 of11 ls1 tm0 ps0 ls2 sr0 rf0 of00 qb+ ls4 of01 mb+ ls5 hb+ ls3 qa+ dd1+ lm
-c16+ c17+ ma+ lz ds1+ r16+ r17+ ha+ pd1+ pr1+ vo""",
-    "v2": """c2 c3 c4 c5 c6 c7 c8 c9 c10 qp- c11 c12 c13 c14 c15 r2 dd0 k1 k0 r3 k2 ds0 r4 r5 d0 d2 d1 r6 r7 r8 r9 r10 tr1 k3 us1 r11 r12 d3
-r13 pd0 tm1 k4 ps1 k5 sr1 d4 r14 d5 of10 rf1 r15 tr0 ls0 us0 pr0 of11 tm0 ls1 ps0 sr0 ls3 rf0 of01 of00 qb+ ga3 ga2 ls2 qa+ ls4 yc0+ ls5""",
-    "s1": """s1 vg- s19 s18 s17 s29 s28 s25 s24 s0 s31 s30 a1 a0 s27 s26 a28 a29 a30 b28 b30 s21 s20 s23 s22 b31 b26 b27 b25 b29 b21 b20 b23 b24
-b22 b19 b18 b17 e0 e1 e2 e3 gb0 gb2 gb1 gb3 ga0 ga2 ga3 ga1 u19+ u22+ u23+ u20+ u18+ u21+ u24+ u25+ u26+ u27+ a19+ a20+ a22+ a23+ a18+
-a26+ a27+ a21+ a24+ a25+""",
-    "s2": """s0 vg- s25 s24 s1 s29 s28 a0 s31 s30 a1 s27 s26 b31 a28 a29 a30 b26 b28 b29 b30 b27 b25 s23 s22 s21 s20 s19 s18 s17 b24 b23 b21 b20
-b22 b19 b18 b17 e0 e1 e2 e3 gb2 gb0 gb3 gb1 ga1 ga0 yc1+ yd1+ yd0+""",
-}
-OPENING = ("qa+", "qb+", "ma+", "mb+", "ha+", "hb+")
-
-
-def spell(q):
-    out = [x[:-1] + ".0" for x in ROUND[q + "1"].split() if x[-1] == "+" and x not in OPENING]
-    for t in range(R):
-        for x in ROUND[q + ("2" if t == R - 1 else "1")].split():
-            if x[-1] == "+":
-                out.append("%s.%d" % (x[:-1], t + 1))
-            elif x[-1] != "-":
-                out.append("%s.%d" % (x, t))
-            elif t > 0:
-                out.append("%s.%d" % (x[:-1], t - 1))
-            elif x == "qp-":
-                out += ["qin.0", "qv.0"]
-    return " ".join(out)
-
-
 ORDER = {
-    "v": spell("v"),
-    "s": spell("s"),
-    "p": "rr.0 mu.1 m2.1 m1.1 m2w.1 m3.1 rr.1 mu.2 m2.2 m1.2 m2w.2 m3.2 rr.2 ym1.3 ym0.3",
-    "y": "cp1.1 cp0.1 cp1.2 cp0.2 oc1.3 oc0.3 osc.3 ol.3",
+    "v": """
+qd.0 qb.0 x2.0 x0.0 x1.0 md.0 mb.0 qa.0 hb.0 hd.0 c16.0 ma.0 dd1.0 ha.0 ds1.0 c17.0 c14.0 c12.0 c15.0 c9.0 c10.0 c7.0 c8.0 c13.0 c11.0 qv.0
+c4.0 c5.0 c6.0 c2.0 c3.0 qin.0 dd0.0 k1.0 k2.0 k0.0 d1.0 pd1.0 r11.0 d2.0 r12.0 r16.0 d0.0 r17.0 r7.0 ds0.0 r13.0 r8.0 r14.0 pr1.0 tr1.0
+r5.0 r15.0 r10.0 r4.0 r9.0 pd0.0 r6.0 us1.0 k3.0 tm1.0 k4.0 ps1.0 k5.0 d3.0 sr1.0 d4.0 d5.0 pr0.0 of10.0 tr0.0 ls0.0 us0.0 ps0.0 ls1.0
+tm0.0 ls3.0 sr0.0 ls2.0 of00.0
+qb.1 ls4.0 mb.1 ls5.0 hb.1 lm.0 qa.1 lz.0 dd1.1 c19.1 vo.0 ma.1 c16.1 ha.1 c17.1 c18.1 c3.1 c9.1 c10.1 r16.1 c7.1 c8.1 qp.0 c4.1 c15.1
+c11.1 c12.1 c14.1 c13.1 c5.1 c6.1 r14.1 dd0.1 k1.1 r19.1 r18.1 r17.1 r8.1 k0.1 k2.1 ds1.1 r13.1 d0.1 d1.1 r5.1 d2.1 r9.1 ds0.1 r12.1
+r15.1 r11.1 tr1.1 pd0.1 pr1.1 r6.1 pd1.1 us1.1 k3.1 tm1.1 k4.1 ps1.1 k5.1 sr1.1 d3.1 d4.1 d5.1 r7.1 of10.1 r10.1 tr0.1 ls0.1 pr0.1 us0.1
+ps0.1 ls1.1 tm0.1 sr0.1 ls2.1 of00.1
+qb.2 ls4.1 mb.2 ls5.1 hb.2 ls3.1 c18.2 qa.2 lm.1 dd1.2 c17.2 lz.1 ma.2 vo.1 c19.2 ha.2 ds1.2 c16.2 c15.2 c7.2 c8.2 c13.2 c9.2 r18.2 r16.2
+c5.2 c6.2 qp.1 c12.2 c10.2 c14.2 c11.2 c3.2 c4.2 dd0.2 r14.2 r7.2 k1.2 ds0.2 k2.2 k0.2 d1.2 d2.2 r4.2 r6.2 r17.2 d0.2 r8.2 r5.2 r9.2 r3.2
+r12.2 tr1.2 pd1.2 r10.2 r15.2 r13.2 r19.2 us1.2 k3.2 tm1.2 k4.2 ps1.2 k5.2 sr1.2 r11.2 d4.2 d3.2 of10.2 d5.2 pd0.2 tre.2 tr0.2 ps0.2 use.2
+us0.2 ls0.2 tm0.2 ls1.2 sr0.2 of00.2 ls2.2 ga3.2 gc1.2 ls3.2 qb.3 ls4.2 qc.3 qa.3 ls5.2 oz.3
+""",
+    "s": """
+u18.0 u20.0 u24.0 u25.0 u19.0 u21.0 u26.0 u27.0 a20.0 s29.0 s28.0 s1.0 s31.0 s30.0 u22.0 u23.0 s25.0 s24.0 a25.0 a24.0 a19.0 a21.0 s0.0
+a22.0 a23.0 a26.0 a27.0 a1.0 a18.0 a28.0 a29.0 a30.0 a0.0 s27.0 s26.0 b28.0 b30.0 s23.0 s22.0 b29.0 s19.0 s18.0 s17.0 s21.0 s20.0 b26.0
+b31.0 b25.0 b27.0 b24.0 b22.0 b21.0 b20.0 b23.0 b19.0 b18.0 b17.0 e0.0 e2.0 e3.0 e1.0 r3.0 r2.0 gb3.0 gb0.0 gb2.0 gb1.0 ga1.0 ga2.0 ga3.0
+ga0.0
+u24.1 u25.1 u22.1 u23.1 u26.1 u27.1 u20.1 u21.1 a23.1 a22.1 a20.1 a27.1 vg.0 s31.1 s30.1 s19.1 s18.1 a25.1 s2.1 s29.1 s28.1 s0.1 a21.1
+a29.1 a30.1 s1.1 a28.1 a24.1 b29.1 s17.1 a26.1 a1.1 a0.1 a2.1 b30.1 s27.1 s26.1 s25.1 s24.1 s23.1 s22.1 b28.1 b27.1 s21.1 s20.1 b26.1
+b31.1 b25.1 b23.1 b24.1 b21.1 b20.1 b22.1 b17.1 b19.1 b18.1 e3.1 r4.1 e2.1 e1.1 e0.1 r3.1 gb3.1 gb0.1 gb1.1 gb2.1 ga1.1 ga3.1 ga0.1 ga2.1
+u22.2 u23.2 u26.2 u27.2 u24.2 u25.2 u21.2 u20.2 a27.2 a22.2 a25.2 a23.2 a24.2 a26.2 a20.2 vg.1 s28.2 s0.2 s31.2 s30.2 s2.2 s29.2 s17.2
+s27.2 s26.2 s1.2 s21.2 a28.2 s20.2 a21.2 a30.2 a2.2 a29.2 a0.2 a1.2 s25.2 s24.2 s19.2 s18.2 b28.2 b30.2 s23.2 s22.2 b25.2 b26.2 b27.2
+b31.2 b29.2 b22.2 b21.2 b20.2 b23.2 b24.2 pr1.2 b17.2 b19.2 b18.2 e2.2 e0.2 e3.2 e1.2 pr0.2 gb0.2 gb1.2 gb3.2 gb2.2 gc2.2 gc0.2 ga1.2
+gc3.2 ga0.2 ga2.2 yc1.3 yc2.3 yd1.3 yc0.3 yd2.3 yd0.3
+""",
+    "p": """
+mq.0 mu.0 mv.0 ml.0 m1.0 m2w.0 m2.0 m3.0 rr.0 mu.1 mv.1 ml.1 m1.1 m2w.1 m2.1 m3.1 rr.1 mu.2 mv.2 ml.2 m1.2 m2w.2 m2.2 m3.2 rr.2
+ym1.3 ym2.3 ym0.3
+""",
+    "y": "cp1.1 cp0.1 cp1.2 cp0.2 oc1.3 oc2.3 oc0.3 osc.3 ol.3",
     "g": "send.0 send.1",
 }
 
@@ -65,24 +62,26 @@ SCRATCH = {
     "wq": ("sbuf", [128, 512], Q8), "wp": ("sbuf", [128, 512], "uint8"),
     "xfin": ("sbuf", [128, 4 * C], "bfloat16"),
     "pcol": ("sbuf", [128, 1], "int32"), "pint": ("sbuf", [128, 4], "int32"), "pf": ("sbuf", [128, 4], "float32"),
+    "pc": ("sbuf", [128, 3 + M], "float32"),
     "uoi": ("sbuf", [128, 8], "int32"), "uoff": ("sbuf", [128, 8], "uint16"),
     "i16": ("sbuf", [128, H2], "bfloat16"), "i4": ("sbuf", [128, K], "bfloat16"), "places": ("sbuf", [128, C], "float32"),
-    "jb": ("sbuf", [128, 32], "float32"),
+    "jb": ("sbuf", [128, 32], "float32"), "zz": ("sbuf", [128, 272], "bfloat16"),
     "mh": ("sbuf", [128, H2], "bfloat16"), "mt": ("sbuf", [128, H2], "bfloat16"), "kt": ("sbuf", [128, H2], "bfloat16"),
     "k0": ("sbuf", [128, 544], "bfloat16"),
     "m4": ("sbuf", [128, K], "bfloat16"), "k4": ("sbuf", [128, K], "bfloat16"),
     "msk": ("sbuf", [128, C], "float32"), "hh": ("sbuf", [128, C], "float32"),
-    "cb": ("sbuf", [128, SL * C], "bfloat16"), "sg": ("sbuf", [128, (16 + NS) * H2], "bfloat16"),
-    "ro": ("sbuf", [128, NV * 128], "float16"), "ds": ("sbuf", [128, C], "float16"),
+    "cb": ("sbuf", [128, SL * C], "bfloat16"), "sg": ("sbuf", [128, (16 + max(NSR)) * H2], "bfloat16"),
+    "jk": ("sbuf", [128, max(RSR) * H2], "bfloat16"),
+    "ro": ("sbuf", [128, max(NVR) * 128], "bfloat16"), "ds": ("sbuf", [128, 2 * 130], "bfloat16"),
     "co": ("sbuf", [128, CST * len(CHUNKS)], "float16"), "tin": ("sbuf", [128, C + 32], "bfloat16"),
     "t3": ("sbuf", [128, 1056], "bfloat16"), "u3": ("sbuf", [128, 1056], "float16"),
     "i2": ("sbuf", [128, 16], "float32"), "m1": ("sbuf", [128, 16], "float32"), "m2": ("sbuf", [128, 16], "float32"),
-    "nb": ("sbuf", [128, 32], "float32"), "nn": ("sbuf", [128, 32], "float32"),
     "xt": ("sbuf", [128, 32 * XS], "float32"), "px": ("sbuf", [128, 32 * XS], "float32"), "kx": ("sbuf", [128, 16 * XS], "float32"),
     "cap": ("sbuf", [128, 32 * XS], "float32"), "sx": ("sbuf", [128, 32 * XS], "float32"),
-    "soff": ("sbuf", [128, 32 * M], "uint16"), "roff": ("sbuf", [128, 32], "uint16"), "voff": ("sbuf", [128, 40], "uint16"),
-    "lst": ("sbuf", [128, C], "float32"), "lm": ("sbuf", [128, K], "float16"), "lz": ("sbuf", [128, K], "float16"),
-    "ysb": ("sbuf", [128, C], "float32"),
+    "yb": ("sbuf", [128, 80], "float32"), "k5": ("sbuf", [128, 80], "float32"), "kl": ("sbuf", [128, 16 * XS], "float32"),
+    "soff": ("sbuf", [128, 32 * M], "uint16"), "voff": ("sbuf", [128, 40], "uint16"),
+    "lst": ("sbuf", [128, HW + 4 * C], "float32"), "lm": ("sbuf", [128, K], "float16"), "lz": ("sbuf", [128, K], "float16"),
+    "olb": ("sbuf", [128, K], "float32"), "ysb": ("sbuf", [128, C], "float32"),
     "ps1": ("psum", [128, 512], "float32"), "ps2": ("psum", [128, 1024], "float32"), "psa": ("psum", [128, 512], "float32"),
 }
 for _b in range(4):
@@ -100,15 +99,15 @@ for _t in range(R - 1):
     SCRATCH["pq%d" % _t] = ("sbuf", [128, K], Q8)
     SCRATCH["ps%dc" % _t] = ("sbuf", [128, K], "uint8")
 
-SEMAPHORES = ["lu", "lxa", "lxb", "la", "lw", "lv", "cp0", "cp1", "cp2", "io1", "io2", "io3", "io4", "io5",
-              "c0", "c1", "c2", "c3", "c3a", "c4", "c5", "c6", "c7",
-              "qa", "qb", "qin", "qv", "mu", "m1", "m2", "m2w", "m3", "rr", "ma", "mb", "ha", "hb",
+SEMAPHORES = ["lu", "lxa", "lxb", "lxd", "la", "lw", "lv", "cp0", "cp1", "cp2", "io1", "io2", "io3", "io4", "io5", "io6",
+              "c0", "c1", "c2", "c3", "c3a", "c3b", "c4", "c5", "c6", "c7", "c8", "c9", "kc", "oz",
+              "qa", "qb", "qc", "qd", "qin", "qv", "mq", "mu", "mv", "ml", "m1", "m2", "m2w", "m3", "rr", "ma", "mb", "md", "ha", "hb", "hd",
               "dd0", "dd1", "ds0", "ds1", "pd0", "pd1", "pr0", "pr1",
-              "cma", "cmb", "cmu", "rs0", "rs1", "su0", "su1", "sg0", "sg1", "sg2", "sg3", "acl", "ee0", "ee1", "ee2", "ee3",
-              "df0", "df1", "tr0", "tr1", "us0", "us1", "tm0", "tm1", "ps0", "ps1", "sr0", "sr1", "rf0", "rf1",
-              "of00", "of01", "of02", "of03", "of10", "of11", "of12", "of13",
-              "ga", "gb", "ls", "lm", "lz", "vo", "vg", "qp", "arr1", "arr2", "sent",
-              "ym0", "ym1", "yc0", "yc1", "st1", "st2"] + [x % k for x in ("ac%d", "k%d") for k in range(len(CHUNKS))]
+              "cma", "cmb", "cmu", "rs0", "rs1", "rss", "su0", "su1", "sg0", "sg1", "sg2", "sg3", "acl", "ee0", "ee1", "ee2", "ee3",
+              "df0", "df1", "df2", "tr0", "tr1", "tre", "us0", "us1", "use", "tm0", "tm1", "ps0", "ps1", "sr0", "sr1",
+              "of00", "of01", "of10", "of11",
+              "ga", "gb", "gc", "ls", "lm", "lz", "vo", "vg", "qp", "arr1", "arr2", "sent",
+              "ym0", "ym1", "ym2", "yc0", "yc1", "yc2", "st1", "st2"] + [x % k for x in ("ac%d", "k%d") for k in range(len(CHUNKS))]
 
 
 def rank_program(g, core, T, topo):
@@ -141,16 +140,12 @@ def rank_program(g, core, T, topo):
     def state(t):
         return (win(t), HW) if t < R else (T.xfin, 0)
 
-    def quant_half(t, h):
+    def quant(t, lo, hi):
         buf, o = state(t)
-        xq, xs = T["xq%d" % (t // R * R)], T["xs%d" % (t // R * R)]
-        return V.quantize_mx(xq[:, h * H2:(h + 1) * H2], xs[:, h * H2:(h + 1) * H2], buf[:, o + 4 * h * H2:o + 4 * (h + 1) * H2])
+        return V.quantize_mx(T["xq%d" % (t // R * R)][:, lo:hi], T["xs%d" % (t // R * R)][:, lo:hi], buf[:, o + 4 * lo:o + 4 * hi])
 
-    def own_mask(h):
-        return V.tensor_tensor(T.msk[:, h * H2:(h + 1) * H2], (T.psa if h else T.ps1)[:, 0:H2], T.mt[:], A.min)
-
-    def own_scan(h):
-        return V.tensor_tensor_scan(T.hh[:, h * H2:(h + 1) * H2], T.kt[:], T.msk[:, h * H2:(h + 1) * H2], 0.0, A.min, A.max)
+    def copy(q, out, src):
+        return S.activation(out, src, F.Copy) if q == "s" else V.tensor_copy(out, src)
 
     def scores(out, lo, hi):
         return PE.matmul_mx(out, T.urq[:], T.urs[:], T.xq0[:, lo:hi], T.xs0[:, lo:hi], True, True)
@@ -165,8 +160,9 @@ def rank_program(g, core, T, topo):
         return T.xt[:, XS * c + k:XS * c + k + 1]
 
     ev("lu", SY.dma_start(T.ub[:], T.u[:]), 16)
-    ev("lxb", S.dma_start(win(0)[:, HW + 4 * H2:HW + 4 * C], T.x[:, 4 * H2:4 * C]), 16)
-    ev("lxa", SY.dma_start(win(0)[:, HW:HW + 4 * H2], T.x[:, 0:4 * H2]), 16)
+    ev("lxd", S.dma_start(win(0)[:, HW + 4 * Q3:HW + 4 * C], T.x[:, 4 * Q3:4 * C]), 16)
+    ev("lxb", SY.dma_start(win(0)[:, HW + 4 * H2:HW + 4 * Q3], T.x[:, 4 * H2:4 * Q3]), 16)
+    ev("lxa", S.dma_start(win(0)[:, HW:HW + 4 * H2], T.x[:, 0:4 * H2]), 16)
     w("y", "lxa")
     ev("la", SY.dma_start(T.ab[:], T.a[:]), 16)
     ev("lw", SY.dma_start(T.wq[:].bitcast(dt.uint8), T.wc[:]), 16)
@@ -178,80 +174,75 @@ def rank_program(g, core, T, topo):
     def count_up(name, out, pattern, base):
         ev(name, g.iota(out, pattern, base, 0, allow_small_or_imprecise_dtypes=True))
 
-    def zero(out):
-        ev("c0", S.activation(out, T.i16[:, 0:16], F.Identity, scale=0.0))
+    def fill(name, out, n, value):
+        ev(name, S.activation(out, T.zz[:, 0:n], F.Identity, bias=value))
 
     ev("io1", g.iota(T.pcol[:], [[0, 1]], 0, 1))
-    count_up("io2", T.i16[:], [[0, 16], [1, 16]], 0)
     ev("io5", g.iota(T.uoi[:], [[16, 8]], 0, 0))
-    count_up("io3", T.i4[:], [[0, K // 4], [1, 4]], 0)
+    count_up("io2", T.i16[:], [[0, 16], [1, 16]], 0)
     count_up("io3", T.jb[:], [[16, 32]], HW // 4)
     count_up("io3", T.i2[:], [[0, 8], [1, 2]], 0)
-    count_up("io3", T.nb[:], [[16, 2], [0, 16]], 240)
+    count_up("io6", T.i4[:], [[0, K // 4], [1, 4]], 0)
+    for q in range(16):
+        count_up("c0", slot(q, 16 * q, 16 * q + 16), [[0, 16]], 0)
+    count_up("c0", T.cb[:, SL - 1:SL * C:SL], [[0, C]], 0)
+    count_up("c0", T.tin[:, 0:16], [[0, 16]], 0)
+    count_up("c0", T.tin[:, 16 + C:32 + C], [[0, 16]], 0)
     count_up("io4", T.places[:], [[1, C]], 0)
-    ev("c7", V.memset(T.xt[:], 0.0))
-    ev("c7", V.memset(T.kx[:], 1.0))
-    ev("c7", V.memset(T.cap[:], 0.0))
+    ev("c2", V.memset(T.zz[:], 0.0))
+    w("s", "c2")
+    fill("c7", T.xt[:], 32 * XS, 0.0)
+    fill("c7", T.cap[:], 32 * XS, -FAR)
+    fill("c7", T.kx[:], 16 * XS, 1.0)
+    fill("c7", T.kl[:], 16 * XS, 1.0)
+    fill("c7", T.k5[:], 80, 1.0)
+    fill("c7", T.k0[:, 0:272], 272, 1.0)
+    fill("c7", T.k0[:, 272:544], 272, 1.0)
     w("v", "io1")
     ev("c1", V.tensor_scalar(T.pint[:, 0:1], T.pcol[:], 15, None, A.bitwise_and))
     ev("c1", V.tensor_scalar(T.pint[:, 1:2], T.pcol[:], 3, None, A.bitwise_and))
     ev("c1", V.tensor_scalar(T.pint[:, 2:3], T.pcol[:], 2, 3, A.arith_shift_right, A.bitwise_and))
     ev("c1", V.tensor_scalar(T.pint[:, 3:4], T.pcol[:], 4, 1, A.arith_shift_right, A.bitwise_and))
-    ev("c7", V.memset(T.k0[:], 1.0))
+    w("v", "io5")
+    ev("c3b", V.tensor_copy(T.uoff[:], T.uoi[:]))
     w("v", "c1")
     ev("c2", V.tensor_copy(T.pf[:], T.pint[:]))
-    ev("c6", V.memset(T.cb[:, SL - 1:SL * C:SL], 0.0))
     w("v", "c2", "io2")
     ev("c3a", V.tensor_scalar(T.mh[:], T.i16[:], T.pf[:, 0:1], 0.5, A.is_equal, A.subtract))
     ev("c3", V.tensor_scalar(T.kt[:], T.i16[:], 0.5, BIG / 16, A.subtract, A.mult))
-    w("v", "io5", "c7")
-    ev("c1", V.tensor_copy(T.uoff[:], T.uoi[:]))
-    ev("c6", V.memset(T.k0[:, 0:544:16], 0.0))
-    ev("c6", V.memset(T.xt[:, XS - 1:32 * XS:XS], -(K - 0.5) * FAR))
-    w("v", "c3a")
-    ev("c3", V.tensor_scalar(T.mt[:], T.mh[:], BIG, None, A.mult))
-    w("s", "io2")
-    for q in range(16):
-        zero(slot(q, 16 * q, 16 * q + 16))
-    zero(T.tin[:, 0:16])
-    zero(T.tin[:, 16 + C:32 + C])
     w("v", "lu")
     ev("c4", V.quantize_mx(T.uq[:], T.us[:], T.ub[:]))
-    w("s", "c4", "c1", "c7")
-    ev("c5", S.activation(T.urs[:], T.us[:].indirect(T.uoff[:, 0:8]), F.Copy))
-    ev("c6", V.memset(T.kx[:, 0:16 * XS:XS], 0.0))
-    ev("c6", V.memset(T.kx[:, 3:16 * XS:XS], float(M)))
-    ev("c6", V.memset(T.kx[:, XS - 1:16 * XS:XS], FAR / M))
-    ev("c6", V.memset(T.cap[:, XS - 2:32 * XS:XS], FAR))
-    w("v", "c4", "c1")
+    w("v", "c3a")
+    ev("c3", V.tensor_scalar(T.mt[:], T.mh[:], BIG, None, A.mult))
+    w("v", "c4", "c3b")
     ev("c5", V.tensor_copy(T.urq[:].bitcast(dt.uint32), T.uq[:].bitcast(dt.uint32).indirect(T.uoff[:, 0:8])))
-    w("v", "lxb")
-    ev("qb", quant_half(0, 1))
-    w("p", "c5", "qb")
-    ev("mu", scores(T.psa[:, 0:H2], H2, C))
-    w("v", "lxa")
-    ev("qa", quant_half(0, 0))
-    w("p", "qa")
-    ev("m2", scores(T.ps2[:, 0:C], 0, C))
-    ev("m1", scores(T.ps1[:, 0:C], 0, C))
-    ev("m2w", scores(T.ps2[:, C:C + H2], 0, H2))
-    ev("m3", scores(T.pr0[:, 0:C], 0, C))
-    ev("c6", V.tensor_scalar(T.co[:, 0:CST * len(CHUNKS):CST], T.i16[:, 0:len(CHUNKS)], 0.0, None, A.mult))
-    w("v", "c3", "mu")
-    ev("mb", own_mask(1))
-    w("v", "io3")
-    ev("c6", V.tensor_scalar(T.m4[:], T.i4[:], T.pf[:, 2:3], None, A.is_equal))
-    ev("c6", V.tensor_scalar(T.k4[:], T.i4[:], T.pf[:, 2:3], None, A.not_equal))
-    ev("c6", V.tensor_scalar(T.nn[:], T.nb[:], T.pf[:, 0:1], None, A.add))
-    w("v", "mb")
-    ev("hb", own_scan(1))
-    w("v", "m1")
-    ev("ma", own_mask(0))
-    ev("c6", V.tensor_scalar(T.m1[:], T.i2[:], T.pf[:, 3:4], -float(M), A.is_equal, A.mult))
-    ev("c6", V.tensor_scalar(T.m2[:], T.i2[:], T.pf[:, 3:4], -float(M), A.not_equal, A.mult))
-    ev("c6", V.tensor_scalar(T.cap[:, XS - 1:32 * XS:XS], T.jb[:], T.pf[:, 0:1], 4.0, A.add, A.mult))
-    w("v", "ma")
-    ev("ha", own_scan(0))
+    w("s", "c4", "c3b")
+    ev("c5", S.activation(T.urs[:], T.us[:].indirect(T.uoff[:, 0:8]), F.Copy))
+    w("s", "c7", "io3", "c2")
+    ev("c8", S.activation(T.m1[:], T.i2[:], F.Abs, bias=T.pf[:, 3:4], scale=-1.0))
+    ev("c9", S.activation(T.cap[:, XS - 1:32 * XS:XS], T.jb[:], F.Identity, bias=T.pf[:, 0:1]))
+    fill("c6", T.k0[:, 0:544:16], 34, 0.0)
+    fill("c6", T.ds[:, 0:260:130], 2, 0.0)
+    for k, (scale, bias) in enumerate([(1.0, 240 - FAR / 2), (FAR, (H2 - K + 0.5) * FAR), (-float(M), -float(M * H2))]
+                                      + [(float(M), float(M * H2 + d)) for d in range(M)]):
+        ev("c9", S.activation(T.pc[:, k:k + 1], T.pf[:, 0:1], F.Identity, bias=bias, scale=scale))
+    fill("c6", T.kx[:, 0:16 * XS:XS], 16, 0.0)
+    fill("c6", T.kx[:, 3:16 * XS:XS], 16, float(M))
+    fill("c6", T.kx[:, XS - 1:16 * XS:XS], 16, FAR / M)
+    fill("c6", T.cap[:, XS - 2:32 * XS:XS], 32, FAR)
+    fill("c6", T.k5[:, 0:80:5], 16, 0.0)
+    fill("c6", T.k5[:, 2:80:5], 16, FAR / M)
+    fill("c6", T.k5[:, 4:80:5], 16, -float(M))
+    fill("c6", T.kl[:, 0:16 * XS:XS], 16, 0.0)
+    w("s", "c8")
+    ev("c9", S.activation(T.m1[:], T.m1[:], F.Identity, bias=-float(M), scale=float(M)))
+    w("s", "c9")
+    for out, src, scale, bias in ((T.xt[:, 2:16 * XS:XS], T.m1[:], -FAR / 2 / M, T.pc[:, 0:1]), (T.xt[:, 3:16 * XS:XS], T.m1[:], FAR / M, FAR / 2),
+                                  (T.xt[:, 4:16 * XS:XS], T.m1[:], -FAR / M, -FAR / 2 - K + 0.5), (T.xt[:, 5:16 * XS:XS], T.m1[:], FAR / M, FAR / 2),
+                                  (T.m2[:], T.m1[:], -1.0, -float(M)), (T.yb[:, 4:80:5], T.cap[:, XS - 1:16 * XS:XS], -4.0, 0.0),
+                                  (T.cap[:, 17 * XS - 1:32 * XS:XS], T.cap[:, 17 * XS - 1:32 * XS:XS], 4.0, T.pc[:, 2:3]),
+                                  (T.xt[:, 17 * XS - 1:32 * XS:XS], T.m1[:], 0.0, T.pc[:, 1:2])):
+        ev("c9", S.activation(out, src, F.Identity, bias=bias, scale=scale))
 
     ops = {}
 
@@ -264,6 +255,30 @@ def rank_program(g, core, T, topo):
     def describe(t):
         last, old = t == R - 1, ".%d" % (t - 1)
         buf, first = state(t + 1)
+        NS, NV, RS = NSR[t], NVR[t], RSR[t]
+
+        op("mu", t, "mu", ["qb", "qd", "c5.0"], lambda q: [scores(T.psa[:, 0:H2], H2, C)])
+        op("mv", t, "mv", ["qb", "qd"], lambda q: [scores(T.pr2[:, 0:H2], H2, C)])
+        op("ml", t, "ml", ["qa"], lambda q: [scores(T.pr1[:, 0:H2], 0, H2)])
+        op("m1", t, "m1", ["qa", "qb"], lambda q: [scores(T.ps1[:, 0:C], 0, C)])
+        op("m2", t, "m2", ["qa", "qb"], lambda q: [scores(T.ps2[:, 0:C], 0, C)])
+        op("m2w", t, "m2w", ["qa"], lambda q: [scores(T.ps2[:, C:C + H2], 0, H2)])
+        op("m3", t, "m3", ["qa", "qb"], lambda q: [scores(T.pr0[:, 0:C], 0, C)])
+        parts = [("a", 0, H2, "ml", T.pr1[:, 0:H2]), ("b", H2, C, "mu", T.psa[:, 0:H2])]
+        if t == 0:
+            op("mq", t, "mq", ["qd", "c5.0"], lambda q: [scores(T.pr3[:, 0:C - Q3], Q3, C)])
+            parts[1:] = [("b", H2, Q3, "mu", T.psa[:, 0:Q3 - H2]), ("d", Q3, C, "mq", T.pr3[:, 0:C - Q3])]
+        for z, lo, hi, need, src in parts:
+            op("m" + z, t, "m" + z, [need, "c3.0"], lambda q, lo=lo, hi=hi, src=src: [
+                V.tensor_tensor(T.msk[:, lo:hi], src, T.mt[:, 0:hi - lo], A.min)])
+            op("h" + z, t, "h" + z, ["m" + z], lambda q, lo=lo, hi=hi: [
+                V.tensor_tensor_scan(T.hh[:, lo:hi], T.kt[:, 0:hi - lo], T.msk[:, lo:hi], 0.0, A.min, A.max)])
+            if t == 0:
+                op("q" + z, t, "q" + z, ["lx" + z], lambda q, lo=lo, hi=hi: [quant(0, lo, hi)])
+        if t == 0:
+            op("x0", t, "kc", [], lambda q: [V.tensor_scalar(T.co[:, 0:CST * len(CHUNKS):CST], T.i16[:, 0:len(CHUNKS)], 0.0, None, A.mult)])
+            op("x1", t, "kc", ["io6"], lambda q: [V.tensor_scalar(T.m4[:], T.i4[:], T.pf[:, 2:3], None, A.is_equal)])
+            op("x2", t, "kc", ["io6"], lambda q: [V.tensor_scalar(T.k4[:], T.i4[:], T.pf[:, 2:3], None, A.not_equal)])
 
         def signs(name, c, sem, needs, o, src, n):
             op(name, t, sem, needs, lambda q: [S.activation(T.sg[:, o:o + n], src, F.Sign, bias=own(c), scale=-1.0)])
@@ -280,15 +295,15 @@ def rank_program(g, core, T, topo):
             signs("s%d" % c, c, "sg3", ["m3", "ha"], o, T.pr0[:, lo:lo + H2], H2)
             above(c, "acl", "sg3", o, lo, lo + H2)
         for c in range(16, 32):
-            o, lo = H2 * (c - 16), 16 * c + 16
+            o, lo, held = H2 * (c - 16), 16 * c + 16, "hd" if t == 0 and 16 * c >= Q3 else "hb"
             up, low = ("su0" if c < UG else "su1") if c < WH else "sg0", "sg0" if c >= WH else "sg1" if c >= WG else "sg2"
             if NV <= c < WH:
-                signs("u%d" % c, c, up, ["m2", "hb"], o, T.ps2[:, lo:C], C - lo)
+                signs("u%d" % c, c, up, ["mv", held], o, T.pr2[:, lo - H2:H2], C - lo)
             if NV <= c < 31:
                 above(c, level(lo, C), up, o, lo, C)
             if c > 16:
                 a = C if c < WH else lo
-                signs("s%d" % c, c, low, ["m2", "m2w", "hb"], o + a - lo, T.ps2[:, a:lo + 240], lo + 240 - a)
+                signs("s%d" % c, c, low, ["m2w", held] + ["m2"] * (c >= WH), o + a - lo, T.ps2[:, a:lo + 240], lo + 240 - a)
                 below(c, low, o + C - lo, lo + 240 - C)
 
         for c in range(NS, NV):
@@ -297,63 +312,88 @@ def rank_program(g, core, T, topo):
             sem, src = ("cma" if c <= 8 else "cmb", T.ps1[:, lo:lo + 2 * n]) if c < 16 else ("cmu", T.psa[:, lo - H2:H2])
             op("c%d" % c, t, sem, ["ha", "m1"] if c < 16 else ["hb"], lambda q, c=c, lo=lo, n=n, src=src: [
                 V.tensor_scalar(slot(c, lo, lo + 2 * n), src, own(c), None, A.is_lt)])
-            op("r%d" % c, t, "rs%d" % (c // 16), [sem], lambda q, c=c, lo=lo, n=n: [
-                V.tensor_tensor_scan(T.ro[:, 128 * c + 128 - n:128 * c + 128], slot(c, lo, lo + n), slot(c, lo + n, lo + 2 * n), 0.0, A.add, A.add)])
+            if c < NS + RS:
+                op("r%d" % c, t, "rss", [sem], lambda q, c=c, lo=lo, n=n: [
+                    S.activation(T.jk[:, H2 * (c - NS):H2 * (c - NS) + 2 * n], slot(c, lo, lo + 2 * n), F.Identity, accum_out=term(c, 1))])
+            else:
+                op("r%d" % c, t, "rs%d" % (c // 16), [sem], lambda q, c=c, lo=lo, n=n: [
+                    V.tensor_tensor_scan(T.ro[:, 128 * c + 128 - n:128 * c + 128], slot(c, lo, lo + n), slot(c, lo + n, lo + 2 * n), 0.0,
+                                         A.add, A.add)])
 
         for k, (lo, hi) in enumerate(CHUNKS):
             o, n = CST * k, 9 * (hi - lo)
-            rows = ["ac%d" % i for i in range(0 if k < 3 else 3, k + 1)] + ["cma", "c6.0", "c0.0"]
+            rows = ["ac%d" % i for i in range(0 if k < 3 else 3, k + 1)] + ["cma", "c6.0", "c0.0", "kc.0"]
             rows += ["cmb"] * (hi > 160) + ["acl"] * (lo < 16 * NS + H2) + ["dd0"] * (lo < H2) + ["dd1", "cmu"] * (hi > H2)
             op("k%d" % k, t, "k%d" % k, rows, lambda q, lo=lo, hi=hi, o=o, n=n: [
                 V.tensor_tensor_scan(T.co[:, o + 1:o + 1 + n], T.cb[:, SL * lo:SL * hi:2], T.cb[:, SL * lo + 1:SL * hi:2], 0.0, A.add, A.add)])
-            op("d%d" % k, t, "df1" if k < 3 else "df0", ["k%d" % k], lambda q, lo=lo, hi=hi, o=o, n=n: [
+            op("d%d" % k, t, "df1" if k < 3 else "df0" if lo < 48 else "df2", ["k%d" % k], lambda q, lo=lo, hi=hi, o=o, n=n: [
                 V.tensor_tensor_scan(T.tin[:, 16 + lo:16 + hi], T.co[:, o + 9:o + n + 1:9], T.co[:, o:o + n:9], 0.0, A.max, A.subtract)])
+
+        def add_up(a, b):
+            return V.tensor_tensor_scan(T.u3[:, a:b], T.k0[:, 0:b - a], T.t3[:, a:b], 0.0, A.mult, A.add)
+
         for h in range(2):
             lo, n2, x, n, y, ab = H2 * h, H2 + 32 * h, 16 * XS * h, 16 * XS, 800 * h, "ab"[h]
-            r0, r1 = (16, NV) if h else (NS, 16)
-            pair = T.cb[:, SL * lo + 16:SL * (lo + H2):SL]
-            op("dd%d" % h, t, "dd%d" % h, ["h" + ab], lambda q, h=h, lo=lo, pair=pair: [
-                V.tensor_tensor(pair, (T.psa if h else T.ps1)[:, 0:H2], T.hh[:, lo:lo + H2], A.is_lt)])
-            op("ds%d" % h, t, "ds%d" % h, ["dd%d" % h, "c6.0"], lambda q, lo=lo, pair=pair: [
-                V.tensor_tensor_scan(T.ds[:, lo:lo + H2], T.k0[:, 0:H2], pair, 0.0, A.mult, A.add)])
-            op("pd%d" % h, t, "pd%d" % h, ["ds%d" % h], lambda q, h=h, lo=lo, x=x, n=n: [
-                V.tensor_tensor(T.xt[:, x:x + n:XS], T.ds[:, lo + 15:lo + H2:16], T.nn[:, 16 * h:16 * h + 16], A.add)])
-            if r1 > r0:
-                op("pr%d" % h, t, "pr%d" % h, ["rs%d" % h], lambda q, r0=r0, r1=r1: [
-                    V.tensor_copy(T.xt[:, 1 + r0 * XS:r1 * XS:XS], T.ro[:, 127 + 128 * r0:128 * r1:128])])
-            op("tr%d" % h, t, "tr%d" % h, ["df1", "df%d" % h], lambda q, lo=lo, n2=n2, y=y: [
-                V.transpose(T.t3[:, y:y + H2], T.tin[:, 16 + lo:16 + lo + H2]),
-                V.transpose(T.t3[:, H2 + lo:H2 + lo + n2], T.tin[:, lo:lo + n2])])
-            op("us%d" % h, t, "us%d" % h, ["tr%d" % h], lambda q, h=h, n2=n2: [
-                V.tensor_tensor_scan(T.u3[:, C * h:C * h + H2 + n2], T.k0[:, 0:H2 + n2], T.t3[:, C * h:C * h + H2 + n2], 0.0, A.mult, A.add)])
-            op("tm%d" % h, t, "tm%d" % h, ["us1", "us%d" % h], lambda q, lo=lo, x=x, n=n, y=y: [
-                V.tensor_tensor(T.xt[:, x + 3:x + n:XS], T.u3[:, y + 15:y + H2:16], T.m1[:], A.mult),
-                V.tensor_tensor(T.xt[:, x + 4:x + n:XS], T.u3[:, H2 + lo + 31:H2 + lo + 31 + H2:16], T.m2[:], A.mult)])
-            sums = ["ac%d" % k for k in range(len(CHUNKS))] if h else ["acl"]
-            op("ps%d" % h, t, "ps%d" % h, ["tm%d" % h, "pd%d" % h, "pr%d" % h] + sums, lambda q, x=x, n=n: [
-                V.tensor_tensor_scan(T.px[:, x:x + n], T.kx[:], T.xt[:, x:x + n], 0.0, A.mult, A.add)])
-            op("sr%d" % h, t, "sr%d" % h, ["ps%d" % h], lambda q, x=x, n=n: [
-                V.tensor_tensor_scan(T.sx[:, x:x + n], T.px[:, x:x + n], T.cap[:, x:x + n], 0.0, A.max, A.min)])
-            op("rf%d" % h, t, "rf%d" % h, ["ps%d" % h], lambda q, h=h, x=x, n=n: [
-                V.tensor_scalar(T.roff[:, 16 * h:16 * h + 16], T.px[:, x + XS - 2:x + n:XS], 1.0 / M, None, A.mult)])
+            r0, r1 = (16, NV) if h else (NS + RS, 16)
+            op("dd%d" % h, t, "dd%d" % h, ["h" + ab] + (["hd"] if h else ["m1"]), lambda q, h=h, lo=lo: [
+                V.tensor_tensor(T.cb[:, SL * lo + 16:SL * (lo + H2):SL], (T.psa if h else T.ps1)[:, 0:H2], T.hh[:, lo:lo + H2], A.is_lt)])
+            op("ds%d" % h, t, "ds%d" % h, ["dd%d" % h], lambda q, h=h, lo=lo: [
+                V.tensor_tensor_scan(T.ds[:, 130 * h + 1:130 * h + 129], T.cb[:, SL * lo + 16:SL * (lo + H2):2 * SL],
+                                     T.cb[:, SL * lo + SL + 16:SL * (lo + H2):2 * SL], 0.0, A.add, A.add)])
+            op("pd%d" % h, t, "pd%d" % h, ["ds%d" % h, "c6.0"], lambda q, h=h, x=x, n=n: [
+                V.tensor_tensor(T.xt[:, x:x + n:XS], T.ds[:, 130 * h + 8:130 * h + 129:8], T.ds[:, 130 * h:130 * h + 128:8], A.subtract)])
+            op("pr%d" % h, t, "pr%d" % h, ["rs%d" % h], lambda q, r0=r0, r1=r1: [
+                copy(q, T.xt[:, 1 + r0 * XS:r1 * XS:XS], T.ro[:, 127 + 128 * r0:128 * r1:128])])
+
+            def turn(a, b, b2, y=y, lo=lo):
+                return [V.transpose(T.t3[:, y + a:y + b], T.tin[:, 16 + lo + a:16 + lo + b]),
+                        V.transpose(T.t3[:, H2 + lo + a:H2 + lo + b2], T.tin[:, lo + a:lo + b2])]
+
+            if last and not h:
+                op("tre", t, "tre", ["df1", "df2"], lambda q, turn=turn: turn(64, H2, H2))
+                op("use", t, "use", ["tre"], lambda q: [add_up(64, H2), add_up(H2 + 64, C)])
+                op("tr0", t, "tr0", ["df2", "df0"], lambda q, turn=turn: turn(0, 64, 64))
+                op("us0", t, "us0", ["tr0"], lambda q: [add_up(0, 64), add_up(H2, H2 + 64)])
+            else:
+                op("tr%d" % h, t, "tr%d" % h, ["df1"] + ([] if h else ["df2", "df0"]), lambda q, turn=turn, n2=n2: turn(0, H2, n2))
+                op("us%d" % h, t, "us%d" % h, ["tr%d" % h], lambda q, h=h, n2=n2: [add_up(C * h, C * h + H2 + n2)])
+
+            u1, u2 = T.u3[:, y + 15:y + H2:16], T.u3[:, H2 + lo + 31:H2 + lo + 31 + H2:16]
+            if h:
+                op("tm1", t, "tm1", ["us1", "c9.0"], lambda q, x=x, n=n, u1=u1, u2=u2: [
+                    V.tensor_tensor(T.xt[:, x + 3:x + n:XS], u1, T.m1[:], A.mult), V.tensor_tensor(T.xt[:, x + 4:x + n:XS], u2, T.m2[:], A.mult)])
+                op("ps1", t, "ps1", ["tm1", "pd1", "pr1"] + ["ac%d" % k for k in range(len(CHUNKS))], lambda q, x=x, n=n: [
+                    V.tensor_tensor_scan(T.px[:, x:x + n], T.kx[:], T.xt[:, x:x + n], 0.0, A.mult, A.add)])
+                op("sr1", t, "sr1", ["ps1"], lambda q, x=x, n=n: [
+                    V.tensor_tensor_scan(T.sx[:, x:x + n], T.px[:, x:x + n], T.cap[:, x:x + n], 0.0, A.max, A.min)])
+            else:
+                op("ps0", t, "ps0", ["pd0", "pr0", "acl", "rss", "c9.0"], lambda q, n=n: [
+                    V.tensor_tensor_scan(T.px[:, 0:n], T.kl[:], T.xt[:, 0:n], 0.0, A.mult, A.add)])
+                op("tm0", t, "tm0", ["us1", "us0", "use", "ps0"], lambda q, n=n, u1=u1, u2=u2: [
+                    V.tensor_tensor(T.yb[:, a:80:5], T.px[:, b:n:XS], uu, A.subtract) for a, b, uu in ((0, 4, u1), (1, 5, u2), (2, 2, u1), (3, 3, u2))])
+                op("sr0", t, "sr0", ["tm0"], lambda q: [V.tensor_tensor_scan(T.sx[:, 0:80], T.k5[:], T.yb[:], 0.0, A.mult, A.max)])
             for d in range(M):
-                op("of%d%d" % (h, d), t, "of%d%d" % (h, d), ["sr%d" % h], lambda q, h=h, d=d, x=x, n=n: [
-                    V.tensor_scalar(T.soff[:, 32 * d + 16 * h:32 * d + 16 * h + 16], T.sx[:, x + XS - 1:x + n:XS], float(d), None, A.add)])
-            for e in range(4):
-                j, d = e // M, e % M
-                out = buf[:, first + 4 * lo + e:first + 4 * (lo + H2):4]
-                src = win(t, j)[:, 0:HW + 4 * C - j * M].indirect(T.soff[:, 32 * d + 16 * h:32 * d + 16 * h + 16])
-                op("g%s%d" % (ab, e), t, "g" + ab, ["ee%d" % j, "of%d%d" % (h, d)] + (["cp%d" % t] if j else []),
-                   lambda q, out=out, src=src: [S.activation(out, src, F.Copy) if q == "s" else V.tensor_copy(out, src)])
-            op("q" + ab, t + 1, "q" + ab, ["g%s.%d" % (ab, t)] + ([] if h or last else ["m2"]), lambda q, h=h: [quant_half(t + 1, h)])
+                src = T.sx[:, x + XS - 1:x + n:XS] if h else T.sx[:, 4:80:5]
+                op("of%d%d" % (h, d), t, "of%d%d" % (h, d), ["sr%d" % h], lambda q, h=h, d=d, src=src: [
+                    V.tensor_scalar(T.soff[:, 32 * d + 16 * h:32 * d + 16 * h + 16], src, 1.0 if h else -1.0,
+                                    T.pc[:, 3 + d:4 + d] if h else float(d), A.mult, A.add)])
+            for z, b0, b1 in (("c", 8, 16), ("a", 0, 8)) if last and not h else ((ab, 16 * h, 16 * h + 16),):
+                for e in range(4):
+                    j, d = e // M, e % M
+                    out = buf[:, first + 64 * b0 + e:first + 64 * b1:4]
+                    src = win(t, j)[:, 0:HW + 4 * C - j * M].indirect(T.soff[:, 32 * d + b0:32 * d + b1])
+                    op("g%s%d" % (z, e), t, "g" + z, ["ee%d" % j, "of%d%d" % (h, d)] + (["cp%d" % t] if j else []),
+                       lambda q, out=out, src=src: [copy(q, out, src)])
+                op("q" + z, t + 1, "q" + z, ["g%s.%d" % (z, t)], lambda q, b0=b0, b1=b1: [quant(t + 1, 16 * b0, 16 * b1)])
         for i, (lo, hi) in enumerate(PIECES):
-            op("ls%d" % i, t, "ls", ["rf%d" % (lo // 16), "io4.0"], lambda q, lo=lo, hi=hi: [
-                (w(q, "ls"), V.tensor_copy(T.lst[:, 0:C].indirect(T.roff[:, lo:hi]), T.places[:, 16 * lo:16 * hi]))[1]])
+            op("ls%d" % i, t, "ls", ["of%d0" % (lo // 16), "io4.0"], lambda q, lo=lo, hi=hi: [
+                (w(q, "ls"), V.tensor_copy(T.lst[:].indirect(T.soff[:, lo:hi]), T.places[:, 16 * lo:16 * hi]))[1]])
 
         if t == 0:
             op("qin", t, "qin", ["la"], lambda q: [V.quantize_mx(T.inq0[:], T.ins0[:], T.ab[:])])
             op("qv", t, "qv", ["lv"], lambda q: [V.quantize_mx(T.vq[:], T.vs[:], T.vb[:])])
-        op("rr", t, "rr", ["sg3", "m3"] + (["qin", "lw"] if t == 0 else ["arr%d%s" % (t, old)]), lambda q: [
+        free = ["sg3", "m3", "ma", "su0", "su1", "mv", "md"]
+        op("rr", t, "rr", free + (["qin", "lw"] if t == 0 else ["arr%d%s" % (t, old)]), lambda q: [
             PE.matmul_mx(T["pr%d" % b][:, 0:K], T.wq[:, 128 * b:128 * b + 128], T.wp[:, 128 * b:128 * b + 128],
                          T["inq%d" % t][:], T["ins%d" % t][:], True, True) for b in range(4)])
         for b in range(4):
@@ -363,23 +403,15 @@ def rank_program(g, core, T, topo):
 
         if not last:
             u = t + 1
-            op("mu", u, "mu", ["qb"], lambda q: [scores(T.psa[:, 0:H2], H2, C)])
-            op("m2", u, "m2", ["qb"], lambda q: [scores(T.ps2[:, 0:C], 0, C)])
-            op("m2w", u, "m2w", ["qa"], lambda q: [scores(T.ps2[:, C:C + H2], 0, H2)])
-            op("m1", u, "m1", ["qa", "qb"], lambda q: [scores(T.ps1[:, 0:C], 0, C)])
-            op("m3", u, "m3", ["qa", "qb"], lambda q: [scores(T.pr0[:, 0:C], 0, C)])
             for h in range(2):
-                op("m" + "ab"[h], u, "m" + "ab"[h], ["mu" if h else "m1"], lambda q, h=h: [own_mask(h)])
-                op("h" + "ab"[h], u, "h" + "ab"[h], ["m" + "ab"[h]], lambda q, h=h: [own_scan(h)])
                 op("cp%d" % h, u, "cp%d" % u, ["g%s.%d" % ("ab"[h], t)], lambda q, h=h: [
                     SY.dma_start(win(u, j)[:, HW + max(4 * h * H2 - j * M, 0):HW + 4 * (h + 1) * H2 - j * M],
                                  win(u)[:, HW + max(4 * h * H2, j * M):HW + 4 * (h + 1) * H2]) for j in range(1, NC)])
             vic, pq, ps = T["vic%d" % t], T["pq%d" % t], T["ps%dc" % t]
-            gone = win(t)[:, HW:HW + 4 * C].indirect(T.voff[:, 0:40])
-            op("lm", t, "lm", ["ls"], lambda q: [V.tensor_tensor_scan(T.lm[:], T.lst[:, 0:K], T.m4[:], 0.0, A.max, A.mult)])
+            op("lm", t, "lm", ["ls"], lambda q: [V.tensor_tensor_scan(T.lm[:], T.lst[:, 0:HW:M], T.m4[:], 0.0, A.max, A.mult)])
             op("lz", t, "lz", ["lm"], lambda q: [V.tensor_tensor_scan(T.lz[:], T.k4[:], T.lm[:], 0.0, A.mult, A.add)])
             op("vo", t, "vo", ["lz"], lambda q: [V.tensor_scalar(T.voff[:], T.lz[:, 3:K:4], 4.0, T.pf[:, 1:2], A.mult, A.add)])
-            op("vg", t, "vg", ["vo"], lambda q: [S.activation(vic[:], gone, F.Copy) if q == "s" else V.tensor_copy(vic[:], gone)])
+            op("vg", t, "vg", ["vo"], lambda q: [copy(q, vic[:], win(t)[:, HW:HW + 4 * C].indirect(T.voff[:, 0:40]))])
             op("qp", t, "qp", ["vg"], lambda q: [V.quantize_mx(pq[:], ps[:], vic[:])])
 
             def send(q):
@@ -393,18 +425,18 @@ def rank_program(g, core, T, topo):
             op("send", t, "arr%d" % u, ["qp"], send)
         else:
             xq, xs = T["xq%d" % R], T["xs%d" % R]
-            for h, ps in ((0, T.ps1), (1, T.psa)):
-                lo, hi, qn = h * H2, (h + 1) * H2, "q" + "ab"[h]
+            for h, ps, lo, hi in ((0, T.ps1, 0, 128), (1, T.psa, H2, C), (2, T.ps2, 128, H2)):
+                qn = "q" + "abc"[h]
                 op("ym%d" % h, R, "ym%d" % h, [qn, "qv.0"], lambda q, ps=ps, lo=lo, hi=hi: [
-                    PE.matmul_mx(ps[:, 0:H2], T.vq[:], T.vs[:], xq[:, lo:hi], xs[:, lo:hi], True, True)])
-                op("yc%d" % h, R, "yc%d" % h, ["ym%d" % h], lambda q, ps=ps, lo=lo, hi=hi: [
-                    S.activation(T.ysb[:, lo:hi], ps[:, 0:H2], F.Copy) if q == "s" else V.tensor_copy(T.ysb[:, lo:hi], ps[:, 0:H2])])
+                    PE.matmul_mx(ps[:, 0:hi - lo], T.vq[:], T.vs[:], xq[:, lo:hi], xs[:, lo:hi], True, True)])
+                op("yc%d" % h, R, "yc%d" % h, ["ym%d" % h], lambda q, ps=ps, lo=lo, hi=hi: [copy(q, T.ysb[:, lo:hi], ps[:, 0:hi - lo])])
                 op("yd%d" % h, R, "st2", ["yc%d" % h], lambda q, lo=lo, hi=hi: [queues[q].dma_start(T.y[:, lo:hi], T.ysb[:, lo:hi])])
                 op("oc%d" % h, R, "st1", [qn], lambda q, lo=lo, hi=hi: [
                     queues[q].dma_start(T.oc[:, 4 * lo:4 * hi], xq[:, lo:hi].bitcast(dt.uint8))])
-            op("osc", R, "st1", ["qa", "qb"], lambda q: [
+            op("osc", R, "st1", ["qa", "qb", "qc"], lambda q: [
                 queues[q].dma_start(T.osc[4 * k:4 * k + 4, :], xs[32 * k:32 * k + 4, :]) for k in range(4)])
-            op("ol", R, "st1", ["ls.%d" % t], lambda q: [queues[q].dma_start(T.ol[:], T.lst[0:128:16, 0:K])])
+            op("oz", R, "oz", ["ls.%d" % t], lambda q: [copy(q, T.olb[:], T.lst[:, 0:HW:M])])
+            op("ol", R, "st1", ["oz"], lambda q: [queues[q].dma_start(T.ol[:], T.olb[0:128:16, :])])
 
     for t in range(R):
         describe(t)

from concourse.mybir import dt, AluOpType, ActivationFunctionType

C, K, R, NR = 512, 160, 3, 4
NSR = (2, 3, 3)
NVR = (18, 20, 20)
RSR = (2, 2, 0)
WH, UG, WG = 28, 22, 24
NC = 4
CHUNKS = ((240, 352), (352, 464), (464, 512), (128, 240), (48, 128), (0, 48))
PIECES = ((16, 20), (20, 24), (24, 28), (28, 32), (0, 8), (8, 16))
M = 4 // NC
HW = M * K
H2, Q3 = C // 2, 3 * C // 4
SL = 18
XS = 6
BIG = 2e29
FAR = 8192.0
CST = 1160
Q8 = "float8_e4m3fn_x4"

ORDER = {
    "v": """
qd.0 qb.0 x2.0 x0.0 x1.0 md.0 mb.0 qa.0 hb.0 hd.0 c16.0 ma.0 dd1.0 ha.0 ds1.0 c17.0 c14.0 c12.0 c15.0 c9.0 c10.0 c7.0 c8.0 c13.0 c11.0 qv.0
c4.0 c5.0 c6.0 c2.0 c3.0 qin.0 dd0.0 k1.0 k2.0 k0.0 d1.0 pd1.0 r11.0 d2.0 r12.0 r16.0 d0.0 r17.0 r7.0 ds0.0 r13.0 r8.0 r14.0 pr1.0 tr1.0
r5.0 r15.0 r10.0 r4.0 r9.0 pd0.0 r6.0 us1.0 k3.0 tm1.0 k4.0 ps1.0 k5.0 d3.0 sr1.0 d4.0 d5.0 pr0.0 of10.0 tr0.0 ls0.0 us0.0 ps0.0 ls1.0
tm0.0 ls3.0 sr0.0 ls2.0 of00.0
qb.1 ls4.0 mb.1 ls5.0 hb.1 lm.0 qa.1 lz.0 dd1.1 c19.1 vo.0 ma.1 c16.1 ha.1 c17.1 c18.1 c3.1 c9.1 c10.1 r16.1 c7.1 c8.1 qp.0 c4.1 c15.1
c11.1 c12.1 c14.1 c13.1 c5.1 c6.1 r14.1 dd0.1 k1.1 r19.1 r18.1 r17.1 r8.1 k0.1 k2.1 ds1.1 r13.1 d0.1 d1.1 r5.1 d2.1 r9.1 ds0.1 r12.1
r15.1 r11.1 tr1.1 pd0.1 pr1.1 r6.1 pd1.1 us1.1 k3.1 tm1.1 k4.1 ps1.1 k5.1 sr1.1 d3.1 d4.1 d5.1 r7.1 of10.1 r10.1 tr0.1 ls0.1 pr0.1 us0.1
ps0.1 ls1.1 tm0.1 sr0.1 ls2.1 of00.1
qb.2 ls4.1 mb.2 ls5.1 hb.2 ls3.1 c18.2 qa.2 lm.1 dd1.2 c17.2 lz.1 ma.2 vo.1 c19.2 ha.2 ds1.2 c16.2 c15.2 c7.2 c8.2 c13.2 c9.2 r18.2 r16.2
c5.2 c6.2 qp.1 c12.2 c10.2 c14.2 c11.2 c3.2 c4.2 dd0.2 r14.2 r7.2 k1.2 ds0.2 k2.2 k0.2 d1.2 d2.2 r4.2 r6.2 r17.2 d0.2 r8.2 r5.2 r9.2 r3.2
r12.2 tr1.2 pd1.2 r10.2 r15.2 r13.2 r19.2 us1.2 k3.2 tm1.2 k4.2 ps1.2 k5.2 sr1.2 r11.2 d4.2 d3.2 of10.2 d5.2 pd0.2 tre.2 tr0.2 ps0.2 use.2
us0.2 ls0.2 tm0.2 ls1.2 sr0.2 of00.2 ls2.2 ga3.2 gc1.2 ls3.2 qb.3 ls4.2 qc.3 qa.3 ls5.2 oz.3
""",
    "s": """
u18.0 u20.0 u24.0 u25.0 u19.0 u21.0 u26.0 u27.0 a20.0 s29.0 s28.0 s1.0 s31.0 s30.0 u22.0 u23.0 s25.0 s24.0 a25.0 a24.0 a19.0 a21.0 s0.0
a22.0 a23.0 a26.0 a27.0 a1.0 a18.0 a28.0 a29.0 a30.0 a0.0 s27.0 s26.0 b28.0 b30.0 s23.0 s22.0 b29.0 s19.0 s18.0 s17.0 s21.0 s20.0 b26.0
b31.0 b25.0 b27.0 b24.0 b22.0 b21.0 b20.0 b23.0 b19.0 b18.0 b17.0 e0.0 e2.0 e3.0 e1.0 r3.0 r2.0 gb3.0 gb0.0 gb2.0 gb1.0 ga1.0 ga2.0 ga3.0
ga0.0
u24.1 u25.1 u22.1 u23.1 u26.1 u27.1 u20.1 u21.1 a23.1 a22.1 a20.1 a27.1 vg.0 s31.1 s30.1 s19.1 s18.1 a25.1 s2.1 s29.1 s28.1 s0.1 a21.1
a29.1 a30.1 s1.1 a28.1 a24.1 b29.1 s17.1 a26.1 a1.1 a0.1 a2.1 b30.1 s27.1 s26.1 s25.1 s24.1 s23.1 s22.1 b28.1 b27.1 s21.1 s20.1 b26.1
b31.1 b25.1 b23.1 b24.1 b21.1 b20.1 b22.1 b17.1 b19.1 b18.1 e3.1 r4.1 e2.1 e1.1 e0.1 r3.1 gb3.1 gb0.1 gb1.1 gb2.1 ga1.1 ga3.1 ga0.1 ga2.1
u22.2 u23.2 u26.2 u27.2 u24.2 u25.2 u21.2 u20.2 a27.2 a22.2 a25.2 a23.2 a24.2 a26.2 a20.2 vg.1 s28.2 s0.2 s31.2 s30.2 s2.2 s29.2 s17.2
s27.2 s26.2 s1.2 s21.2 a28.2 s20.2 a21.2 a30.2 a2.2 a29.2 a0.2 a1.2 s25.2 s24.2 s19.2 s18.2 b28.2 b30.2 s23.2 s22.2 b25.2 b26.2 b27.2
b31.2 b29.2 b22.2 b21.2 b20.2 b23.2 b24.2 pr1.2 b17.2 b19.2 b18.2 e2.2 e0.2 e3.2 e1.2 pr0.2 gb0.2 gb1.2 gb3.2 gb2.2 gc2.2 gc0.2 ga1.2
gc3.2 ga0.2 ga2.2 yc1.3 yc2.3 yd1.3 yc0.3 yd2.3 yd0.3
""",
    "p": """
mq.0 mu.0 mv.0 ml.0 m1.0 m2w.0 m2.0 m3.0 rr.0 mu.1 mv.1 ml.1 m1.1 m2w.1 m2.1 m3.1 rr.1 mu.2 mv.2 ml.2 m1.2 m2w.2 m2.2 m3.2 rr.2
ym1.3 ym2.3 ym0.3
""",
    "y": "cp1.1 cp0.1 cp1.2 cp0.2 oc1.3 oc2.3 oc0.3 osc.3 ol.3",
    "g": "send.0 send.1",
}

SCRATCH = {
    "ub": ("sbuf", [128, 512], "bfloat16"), "uq": ("sbuf", [128, 128], Q8), "us": ("sbuf", [128, 128], "uint8"),
    "urq": ("sbuf", [128, 128], Q8), "urs": ("sbuf", [128, 128], "uint8"),
    "vb": ("sbuf", [128, 512], "bfloat16"), "vq": ("sbuf", [128, 128], Q8), "vs": ("sbuf", [128, 128], "uint8"),
    "ab": ("sbuf", [128, 4 * K], "bfloat16"),
    "wq": ("sbuf", [128, 512], Q8), "wp": ("sbuf", [128, 512], "uint8"),
    "xfin": ("sbuf", [128, 4 * C], "bfloat16"),
    "pcol": ("sbuf", [128, 1], "int32"), "pint": ("sbuf", [128, 4], "int32"), "pf": ("sbuf", [128, 4], "float32"),
    "pc": ("sbuf", [128, 3 + M], "float32"),
    "uoi": ("sbuf", [128, 8], "int32"), "uoff": ("sbuf", [128, 8], "uint16"),
    "i16": ("sbuf", [128, H2], "bfloat16"), "i4": ("sbuf", [128, K], "bfloat16"), "places": ("sbuf", [128, C], "float32"),
    "jb": ("sbuf", [128, 32], "float32"), "zz": ("sbuf", [128, 272], "bfloat16"),
    "mh": ("sbuf", [128, H2], "bfloat16"), "mt": ("sbuf", [128, H2], "bfloat16"), "kt": ("sbuf", [128, H2], "bfloat16"),
    "k0": ("sbuf", [128, 544], "bfloat16"),
    "m4": ("sbuf", [128, K], "bfloat16"), "k4": ("sbuf", [128, K], "bfloat16"),
    "msk": ("sbuf", [128, C], "float32"), "hh": ("sbuf", [128, C], "float32"),
    "cb": ("sbuf", [128, SL * C], "bfloat16"), "sg": ("sbuf", [128, (16 + max(NSR)) * H2], "bfloat16"),
    "jk": ("sbuf", [128, max(RSR) * H2], "bfloat16"),
    "ro": ("sbuf", [128, max(NVR) * 128], "bfloat16"), "ds": ("sbuf", [128, 2 * 130], "bfloat16"),
    "co": ("sbuf", [128, CST * len(CHUNKS)], "float16"), "tin": ("sbuf", [128, C + 32], "bfloat16"),
    "t3": ("sbuf", [128, 1056], "bfloat16"), "u3": ("sbuf", [128, 1056], "float16"),
    "i2": ("sbuf", [128, 16], "float32"), "m1": ("sbuf", [128, 16], "float32"), "m2": ("sbuf", [128, 16], "float32"),
    "xt": ("sbuf", [128, 32 * XS], "float32"), "px": ("sbuf", [128, 32 * XS], "float32"), "kx": ("sbuf", [128, 16 * XS], "float32"),
    "cap": ("sbuf", [128, 32 * XS], "float32"), "sx": ("sbuf", [128, 32 * XS], "float32"),
    "yb": ("sbuf", [128, 80], "float32"), "k5": ("sbuf", [128, 80], "float32"), "kl": ("sbuf", [128, 16 * XS], "float32"),
    "soff": ("sbuf", [128, 32 * M], "uint16"), "voff": ("sbuf", [128, 40], "uint16"),
    "lst": ("sbuf", [128, HW + 4 * C], "float32"), "lm": ("sbuf", [128, K], "float16"), "lz": ("sbuf", [128, K], "float16"),
    "olb": ("sbuf", [128, K], "float32"), "ysb": ("sbuf", [128, C], "float32"),
    "ps1": ("psum", [128, 512], "float32"), "ps2": ("psum", [128, 1024], "float32"), "psa": ("psum", [128, 512], "float32"),
}
for _b in range(4):
    SCRATCH["pr%d" % _b] = ("psum", [128, 512], "float32")
for _t in range(R):
    for _j in range(NC):
        SCRATCH["win%d%d" % (_t, _j)] = ("sbuf", [128, HW + 4 * C], "bfloat16")
    SCRATCH["inq%d" % _t] = ("sbuf", [128, K], Q8)
    SCRATCH["ins%d" % _t] = ("sbuf", [128, K], "uint8")
for _t in (0, R):
    SCRATCH["xq%d" % _t] = ("sbuf", [128, C], Q8)
    SCRATCH["xs%d" % _t] = ("sbuf", [128, C], "uint8")
for _t in range(R - 1):
    SCRATCH["vic%d" % _t] = ("sbuf", [128, 4 * K], "bfloat16")
    SCRATCH["pq%d" % _t] = ("sbuf", [128, K], Q8)
    SCRATCH["ps%dc" % _t] = ("sbuf", [128, K], "uint8")

SEMAPHORES = ["lu", "lxa", "lxb", "lxd", "la", "lw", "lv", "cp0", "cp1", "cp2", "io1", "io2", "io3", "io4", "io5", "io6",
              "c0", "c1", "c2", "c3", "c3a", "c3b", "c4", "c5", "c6", "c7", "c8", "c9", "kc", "oz",
              "qa", "qb", "qc", "qd", "qin", "qv", "mq", "mu", "mv", "ml", "m1", "m2", "m2w", "m3", "rr", "ma", "mb", "md", "ha", "hb", "hd",
              "dd0", "dd1", "ds0", "ds1", "pd0", "pd1", "pr0", "pr1",
              "cma", "cmb", "cmu", "rs0", "rs1", "rss", "su0", "su1", "sg0", "sg1", "sg2", "sg3", "acl", "ee0", "ee1", "ee2", "ee3",
              "df0", "df1", "df2", "tr0", "tr1", "tre", "us0", "us1", "use", "tm0", "tm1", "ps0", "ps1", "sr0", "sr1",
              "of00", "of01", "of10", "of11",
              "ga", "gb", "gc", "ls", "lm", "lz", "vo", "vg", "qp", "arr1", "arr2", "sent",
              "ym0", "ym1", "ym2", "yc0", "yc1", "yc2", "st1", "st2"] + [x % k for x in ("ac%d", "k%d") for k in range(len(CHUNKS))]


def rank_program(g, core, T, topo):
    rank = T.rank_of(core)
    if rank is None:
        return
    A, F = AluOpType, ActivationFunctionType
    V, S, PE, SY = g.vector, g.scalar, g.tensor, g.sync
    queues = {"g": g, "v": V, "s": S, "p": PE, "y": SY}
    nxt = T.cores[(rank + 1) % NR]
    prv = T.cores[(rank - 1) % NR]
    rid, pid, _se = topo.addr(nxt)
    emask = topo.mask(core, nxt)
    n_out, n_in = len(topo.engines(core, nxt)), len(topo.engines(prv, core))
    cnt, seen = {}, {}

    def ev(name, ins, n=1):
        ins.then_inc(T.sem[name], n)
        cnt[name] = cnt.get(name, 0) + n

    def w(q, *names):
        for name in names:
            if seen.get((q, name), 0) < cnt.get(name, 0):
                queues[q].wait_ge(T.sem[name], cnt[name])
                seen[(q, name)] = cnt[name]

    def win(t, j=0):
        return T["win%d%d" % (t, j)]

    def state(t):
        return (win(t), HW) if t < R else (T.xfin, 0)

    def quant(t, lo, hi):
        buf, o = state(t)
        return V.quantize_mx(T["xq%d" % (t // R * R)][:, lo:hi], T["xs%d" % (t // R * R)][:, lo:hi], buf[:, o + 4 * lo:o + 4 * hi])

    def copy(q, out, src):
        return S.activation(out, src, F.Copy) if q == "s" else V.tensor_copy(out, src)

    def scores(out, lo, hi):
        return PE.matmul_mx(out, T.urq[:], T.urs[:], T.xq0[:, lo:hi], T.xs0[:, lo:hi], True, True)

    def slot(c, lo, hi):
        return T.cb[:, SL * lo + c % 16:SL * hi:SL]

    def own(c):
        return T.hh[:, 16 * c + 15:16 * c + 16]

    def term(c, k):
        return T.xt[:, XS * c + k:XS * c + k + 1]

    ev("lu", SY.dma_start(T.ub[:], T.u[:]), 16)
    ev("lxd", S.dma_start(win(0)[:, HW + 4 * Q3:HW + 4 * C], T.x[:, 4 * Q3:4 * C]), 16)
    ev("lxb", SY.dma_start(win(0)[:, HW + 4 * H2:HW + 4 * Q3], T.x[:, 4 * H2:4 * Q3]), 16)
    ev("lxa", S.dma_start(win(0)[:, HW:HW + 4 * H2], T.x[:, 0:4 * H2]), 16)
    w("y", "lxa")
    ev("la", SY.dma_start(T.ab[:], T.a[:]), 16)
    ev("lw", SY.dma_start(T.wq[:].bitcast(dt.uint8), T.wc[:]), 16)
    ev("lw", SY.dma_start(T.wp[:], T.ws[:]), 16)
    ev("lv", SY.dma_start(T.vb[:], T.v[:]), 16)
    for j in range(1, NC):
        ev("cp0", SY.dma_start(win(0, j)[:, HW:HW + 4 * C - j * M], T.x[:, j * M:4 * C]), 16)

    def count_up(name, out, pattern, base):
        ev(name, g.iota(out, pattern, base, 0, allow_small_or_imprecise_dtypes=True))

    def fill(name, out, n, value):
        ev(name, S.activation(out, T.zz[:, 0:n], F.Identity, bias=value))

    ev("io1", g.iota(T.pcol[:], [[0, 1]], 0, 1))
    ev("io5", g.iota(T.uoi[:], [[16, 8]], 0, 0))
    count_up("io2", T.i16[:], [[0, 16], [1, 16]], 0)
    count_up("io3", T.jb[:], [[16, 32]], HW // 4)
    count_up("io3", T.i2[:], [[0, 8], [1, 2]], 0)
    count_up("io6", T.i4[:], [[0, K // 4], [1, 4]], 0)
    for q in range(16):
        count_up("c0", slot(q, 16 * q, 16 * q + 16), [[0, 16]], 0)
    count_up("c0", T.cb[:, SL - 1:SL * C:SL], [[0, C]], 0)
    count_up("c0", T.tin[:, 0:16], [[0, 16]], 0)
    count_up("c0", T.tin[:, 16 + C:32 + C], [[0, 16]], 0)
    count_up("io4", T.places[:], [[1, C]], 0)
    ev("c2", V.memset(T.zz[:], 0.0))
    w("s", "c2")
    fill("c7", T.xt[:], 32 * XS, 0.0)
    fill("c7", T.cap[:], 32 * XS, -FAR)
    fill("c7", T.kx[:], 16 * XS, 1.0)
    fill("c7", T.kl[:], 16 * XS, 1.0)
    fill("c7", T.k5[:], 80, 1.0)
    fill("c7", T.k0[:, 0:272], 272, 1.0)
    fill("c7", T.k0[:, 272:544], 272, 1.0)
    w("v", "io1")
    ev("c1", V.tensor_scalar(T.pint[:, 0:1], T.pcol[:], 15, None, A.bitwise_and))
    ev("c1", V.tensor_scalar(T.pint[:, 1:2], T.pcol[:], 3, None, A.bitwise_and))
    ev("c1", V.tensor_scalar(T.pint[:, 2:3], T.pcol[:], 2, 3, A.arith_shift_right, A.bitwise_and))
    ev("c1", V.tensor_scalar(T.pint[:, 3:4], T.pcol[:], 4, 1, A.arith_shift_right, A.bitwise_and))
    w("v", "io5")
    ev("c3b", V.tensor_copy(T.uoff[:], T.uoi[:]))
    w("v", "c1")
    ev("c2", V.tensor_copy(T.pf[:], T.pint[:]))
    w("v", "c2", "io2")
    ev("c3a", V.tensor_scalar(T.mh[:], T.i16[:], T.pf[:, 0:1], 0.5, A.is_equal, A.subtract))
    ev("c3", V.tensor_scalar(T.kt[:], T.i16[:], 0.5, BIG / 16, A.subtract, A.mult))
    w("v", "lu")
    ev("c4", V.quantize_mx(T.uq[:], T.us[:], T.ub[:]))
    w("v", "c3a")
    ev("c3", V.tensor_scalar(T.mt[:], T.mh[:], BIG, None, A.mult))
    w("v", "c4", "c3b")
    ev("c5", V.tensor_copy(T.urq[:].bitcast(dt.uint32), T.uq[:].bitcast(dt.uint32).indirect(T.uoff[:, 0:8])))
    w("s", "c4", "c3b")
    ev("c5", S.activation(T.urs[:], T.us[:].indirect(T.uoff[:, 0:8]), F.Copy))
    w("s", "c7", "io3", "c2")
    ev("c8", S.activation(T.m1[:], T.i2[:], F.Abs, bias=T.pf[:, 3:4], scale=-1.0))
    ev("c9", S.activation(T.cap[:, XS - 1:32 * XS:XS], T.jb[:], F.Identity, bias=T.pf[:, 0:1]))
    fill("c6", T.k0[:, 0:544:16], 34, 0.0)
    fill("c6", T.ds[:, 0:260:130], 2, 0.0)
    for k, (scale, bias) in enumerate([(1.0, 240 - FAR / 2), (FAR, (H2 - K + 0.5) * FAR), (-float(M), -float(M * H2))]
                                      + [(float(M), float(M * H2 + d)) for d in range(M)]):
        ev("c9", S.activation(T.pc[:, k:k + 1], T.pf[:, 0:1], F.Identity, bias=bias, scale=scale))
    fill("c6", T.kx[:, 0:16 * XS:XS], 16, 0.0)
    fill("c6", T.kx[:, 3:16 * XS:XS], 16, float(M))
    fill("c6", T.kx[:, XS - 1:16 * XS:XS], 16, FAR / M)
    fill("c6", T.cap[:, XS - 2:32 * XS:XS], 32, FAR)
    fill("c6", T.k5[:, 0:80:5], 16, 0.0)
    fill("c6", T.k5[:, 2:80:5], 16, FAR / M)
    fill("c6", T.k5[:, 4:80:5], 16, -float(M))
    fill("c6", T.kl[:, 0:16 * XS:XS], 16, 0.0)
    w("s", "c8")
    ev("c9", S.activation(T.m1[:], T.m1[:], F.Identity, bias=-float(M), scale=float(M)))
    w("s", "c9")
    for out, src, scale, bias in ((T.xt[:, 2:16 * XS:XS], T.m1[:], -FAR / 2 / M, T.pc[:, 0:1]), (T.xt[:, 3:16 * XS:XS], T.m1[:], FAR / M, FAR / 2),
                                  (T.xt[:, 4:16 * XS:XS], T.m1[:], -FAR / M, -FAR / 2 - K + 0.5), (T.xt[:, 5:16 * XS:XS], T.m1[:], FAR / M, FAR / 2),
                                  (T.m2[:], T.m1[:], -1.0, -float(M)), (T.yb[:, 4:80:5], T.cap[:, XS - 1:16 * XS:XS], -4.0, 0.0),
                                  (T.cap[:, 17 * XS - 1:32 * XS:XS], T.cap[:, 17 * XS - 1:32 * XS:XS], 4.0, T.pc[:, 2:3]),
                                  (T.xt[:, 17 * XS - 1:32 * XS:XS], T.m1[:], 0.0, T.pc[:, 1:2])):
        ev("c9", S.activation(out, src, F.Identity, bias=bias, scale=scale))

    ops = {}

    def op(name, t, sem, needs, call):
        ops["%s.%d" % (name, t)] = ("%s.%d" % (sem, t), [n if "." in n else "%s.%d" % (n, t) for n in needs], call)

    def level(lo, hi):
        return "ac%d" % min(k for k, (a, b) in enumerate(CHUNKS) if a < hi and lo < b)

    def describe(t):
        last, old = t == R - 1, ".%d" % (t - 1)
        buf, first = state(t + 1)
        NS, NV, RS = NSR[t], NVR[t], RSR[t]

        op("mu", t, "mu", ["qb", "qd", "c5.0"], lambda q: [scores(T.psa[:, 0:H2], H2, C)])
        op("mv", t, "mv", ["qb", "qd"], lambda q: [scores(T.pr2[:, 0:H2], H2, C)])
        op("ml", t, "ml", ["qa"], lambda q: [scores(T.pr1[:, 0:H2], 0, H2)])
        op("m1", t, "m1", ["qa", "qb"], lambda q: [scores(T.ps1[:, 0:C], 0, C)])
        op("m2", t, "m2", ["qa", "qb"], lambda q: [scores(T.ps2[:, 0:C], 0, C)])
        op("m2w", t, "m2w", ["qa"], lambda q: [scores(T.ps2[:, C:C + H2], 0, H2)])
        op("m3", t, "m3", ["qa", "qb"], lambda q: [scores(T.pr0[:, 0:C], 0, C)])
        parts = [("a", 0, H2, "ml", T.pr1[:, 0:H2]), ("b", H2, C, "mu", T.psa[:, 0:H2])]
        if t == 0:
            op("mq", t, "mq", ["qd", "c5.0"], lambda q: [scores(T.pr3[:, 0:C - Q3], Q3, C)])
            parts[1:] = [("b", H2, Q3, "mu", T.psa[:, 0:Q3 - H2]), ("d", Q3, C, "mq", T.pr3[:, 0:C - Q3])]
        for z, lo, hi, need, src in parts:
            op("m" + z, t, "m" + z, [need, "c3.0"], lambda q, lo=lo, hi=hi, src=src: [
                V.tensor_tensor(T.msk[:, lo:hi], src, T.mt[:, 0:hi - lo], A.min)])
            op("h" + z, t, "h" + z, ["m" + z], lambda q, lo=lo, hi=hi: [
                V.tensor_tensor_scan(T.hh[:, lo:hi], T.kt[:, 0:hi - lo], T.msk[:, lo:hi], 0.0, A.min, A.max)])
            if t == 0:
                op("q" + z, t, "q" + z, ["lx" + z], lambda q, lo=lo, hi=hi: [quant(0, lo, hi)])
        if t == 0:
            op("x0", t, "kc", [], lambda q: [V.tensor_scalar(T.co[:, 0:CST * len(CHUNKS):CST], T.i16[:, 0:len(CHUNKS)], 0.0, None, A.mult)])
            op("x1", t, "kc", ["io6"], lambda q: [V.tensor_scalar(T.m4[:], T.i4[:], T.pf[:, 2:3], None, A.is_equal)])
            op("x2", t, "kc", ["io6"], lambda q: [V.tensor_scalar(T.k4[:], T.i4[:], T.pf[:, 2:3], None, A.not_equal)])

        def signs(name, c, sem, needs, o, src, n):
            op(name, t, sem, needs, lambda q: [S.activation(T.sg[:, o:o + n], src, F.Sign, bias=own(c), scale=-1.0)])

        def above(c, sem, need, o, lo, hi):
            op("a%d" % c, t, sem, [need], lambda q: [S.activation(slot(c, lo, hi), T.sg[:, o:o + hi - lo], F.Relu, accum_out=term(c, 1))])

        def below(c, need, o, n):
            op("b%d" % c, t, level(0, n), [need], lambda q: [
                S.activation(slot(c, 0, n), T.sg[:, o:o + n], F.Sign, bias=1.0, accum_out=term(c, 2))])

        for c in range(NS):
            o, lo = H2 * (16 + c), 16 * c + 16
            signs("s%d" % c, c, "sg3", ["m3", "ha"], o, T.pr0[:, lo:lo + H2], H2)
            above(c, "acl", "sg3", o, lo, lo + H2)
        for c in range(16, 32):
            o, lo, held = H2 * (c - 16), 16 * c + 16, "hd" if t == 0 and 16 * c >= Q3 else "hb"
            up, low = ("su0" if c < UG else "su1") if c < WH else "sg0", "sg0" if c >= WH else "sg1" if c >= WG else "sg2"
            if NV <= c < WH:
                signs("u%d" % c, c, up, ["mv", held], o, T.pr2[:, lo - H2:H2], C - lo)
            if NV <= c < 31:
                above(c, level(lo, C), up, o, lo, C)
            if c > 16:
                a = C if c < WH else lo
                signs("s%d" % c, c, low, ["m2w", held] + ["m2"] * (c >= WH), o + a - lo, T.ps2[:, a:lo + 240], lo + 240 - a)
                below(c, low, o + C - lo, lo + 240 - C)

        for c in range(NS, NV):
            lo = 16 * c + 16
            n = (min(lo + H2, C) - lo) // 2
            sem, src = ("cma" if c <= 8 else "cmb", T.ps1[:, lo:lo + 2 * n]) if c < 16 else ("cmu", T.psa[:, lo - H2:H2])
            op("c%d" % c, t, sem, ["ha", "m1"] if c < 16 else ["hb"], lambda q, c=c, lo=lo, n=n, src=src: [
                V.tensor_scalar(slot(c, lo, lo + 2 * n), src, own(c), None, A.is_lt)])
            if c < NS + RS:
                op("r%d" % c, t, "rss", [sem], lambda q, c=c, lo=lo, n=n: [
                    S.activation(T.jk[:, H2 * (c - NS):H2 * (c - NS) + 2 * n], slot(c, lo, lo + 2 * n), F.Identity, accum_out=term(c, 1))])
            else:
                op("r%d" % c, t, "rs%d" % (c // 16), [sem], lambda q, c=c, lo=lo, n=n: [
                    V.tensor_tensor_scan(T.ro[:, 128 * c + 128 - n:128 * c + 128], slot(c, lo, lo + n), slot(c, lo + n, lo + 2 * n), 0.0,
                                         A.add, A.add)])

        for k, (lo, hi) in enumerate(CHUNKS):
            o, n = CST * k, 9 * (hi - lo)
            rows = ["ac%d" % i for i in range(0 if k < 3 else 3, k + 1)] + ["cma", "c6.0", "c0.0", "kc.0"]
            rows += ["cmb"] * (hi > 160) + ["acl"] * (lo < 16 * NS + H2) + ["dd0"] * (lo < H2) + ["dd1", "cmu"] * (hi > H2)
            op("k%d" % k, t, "k%d" % k, rows, lambda q, lo=lo, hi=hi, o=o, n=n: [
                V.tensor_tensor_scan(T.co[:, o + 1:o + 1 + n], T.cb[:, SL * lo:SL * hi:2], T.cb[:, SL * lo + 1:SL * hi:2], 0.0, A.add, A.add)])
            op("d%d" % k, t, "df1" if k < 3 else "df0" if lo < 48 else "df2", ["k%d" % k], lambda q, lo=lo, hi=hi, o=o, n=n: [
                V.tensor_tensor_scan(T.tin[:, 16 + lo:16 + hi], T.co[:, o + 9:o + n + 1:9], T.co[:, o:o + n:9], 0.0, A.max, A.subtract)])

        def add_up(a, b):
            return V.tensor_tensor_scan(T.u3[:, a:b], T.k0[:, 0:b - a], T.t3[:, a:b], 0.0, A.mult, A.add)

        for h in range(2):
            lo, n2, x, n, y, ab = H2 * h, H2 + 32 * h, 16 * XS * h, 16 * XS, 800 * h, "ab"[h]
            r0, r1 = (16, NV) if h else (NS + RS, 16)
            op("dd%d" % h, t, "dd%d" % h, ["h" + ab] + (["hd"] if h else ["m1"]), lambda q, h=h, lo=lo: [
                V.tensor_tensor(T.cb[:, SL * lo + 16:SL * (lo + H2):SL], (T.psa if h else T.ps1)[:, 0:H2], T.hh[:, lo:lo + H2], A.is_lt)])
            op("ds%d" % h, t, "ds%d" % h, ["dd%d" % h], lambda q, h=h, lo=lo: [
                V.tensor_tensor_scan(T.ds[:, 130 * h + 1:130 * h + 129], T.cb[:, SL * lo + 16:SL * (lo + H2):2 * SL],
                                     T.cb[:, SL * lo + SL + 16:SL * (lo + H2):2 * SL], 0.0, A.add, A.add)])
            op("pd%d" % h, t, "pd%d" % h, ["ds%d" % h, "c6.0"], lambda q, h=h, x=x, n=n: [
                V.tensor_tensor(T.xt[:, x:x + n:XS], T.ds[:, 130 * h + 8:130 * h + 129:8], T.ds[:, 130 * h:130 * h + 128:8], A.subtract)])
            op("pr%d" % h, t, "pr%d" % h, ["rs%d" % h], lambda q, r0=r0, r1=r1: [
                copy(q, T.xt[:, 1 + r0 * XS:r1 * XS:XS], T.ro[:, 127 + 128 * r0:128 * r1:128])])

            def turn(a, b, b2, y=y, lo=lo):
                return [V.transpose(T.t3[:, y + a:y + b], T.tin[:, 16 + lo + a:16 + lo + b]),
                        V.transpose(T.t3[:, H2 + lo + a:H2 + lo + b2], T.tin[:, lo + a:lo + b2])]

            if last and not h:
                op("tre", t, "tre", ["df1", "df2"], lambda q, turn=turn: turn(64, H2, H2))
                op("use", t, "use", ["tre"], lambda q: [add_up(64, H2), add_up(H2 + 64, C)])
                op("tr0", t, "tr0", ["df2", "df0"], lambda q, turn=turn: turn(0, 64, 64))
                op("us0", t, "us0", ["tr0"], lambda q: [add_up(0, 64), add_up(H2, H2 + 64)])
            else:
                op("tr%d" % h, t, "tr%d" % h, ["df1"] + ([] if h else ["df2", "df0"]), lambda q, turn=turn, n2=n2: turn(0, H2, n2))
                op("us%d" % h, t, "us%d" % h, ["tr%d" % h], lambda q, h=h, n2=n2: [add_up(C * h, C * h + H2 + n2)])

            u1, u2 = T.u3[:, y + 15:y + H2:16], T.u3[:, H2 + lo + 31:H2 + lo + 31 + H2:16]
            if h:
                op("tm1", t, "tm1", ["us1", "c9.0"], lambda q, x=x, n=n, u1=u1, u2=u2: [
                    V.tensor_tensor(T.xt[:, x + 3:x + n:XS], u1, T.m1[:], A.mult), V.tensor_tensor(T.xt[:, x + 4:x + n:XS], u2, T.m2[:], A.mult)])
                op("ps1", t, "ps1", ["tm1", "pd1", "pr1"] + ["ac%d" % k for k in range(len(CHUNKS))], lambda q, x=x, n=n: [
                    V.tensor_tensor_scan(T.px[:, x:x + n], T.kx[:], T.xt[:, x:x + n], 0.0, A.mult, A.add)])
                op("sr1", t, "sr1", ["ps1"], lambda q, x=x, n=n: [
                    V.tensor_tensor_scan(T.sx[:, x:x + n], T.px[:, x:x + n], T.cap[:, x:x + n], 0.0, A.max, A.min)])
            else:
                op("ps0", t, "ps0", ["pd0", "pr0", "acl", "rss", "c9.0"], lambda q, n=n: [
                    V.tensor_tensor_scan(T.px[:, 0:n], T.kl[:], T.xt[:, 0:n], 0.0, A.mult, A.add)])
                op("tm0", t, "tm0", ["us1", "us0", "use", "ps0"], lambda q, n=n, u1=u1, u2=u2: [
                    V.tensor_tensor(T.yb[:, a:80:5], T.px[:, b:n:XS], uu, A.subtract) for a, b, uu in ((0, 4, u1), (1, 5, u2), (2, 2, u1), (3, 3, u2))])
                op("sr0", t, "sr0", ["tm0"], lambda q: [V.tensor_tensor_scan(T.sx[:, 0:80], T.k5[:], T.yb[:], 0.0, A.mult, A.max)])
            for d in range(M):
                src = T.sx[:, x + XS - 1:x + n:XS] if h else T.sx[:, 4:80:5]
                op("of%d%d" % (h, d), t, "of%d%d" % (h, d), ["sr%d" % h], lambda q, h=h, d=d, src=src: [
                    V.tensor_scalar(T.soff[:, 32 * d + 16 * h:32 * d + 16 * h + 16], src, 1.0 if h else -1.0,
                                    T.pc[:, 3 + d:4 + d] if h else float(d), A.mult, A.add)])
            for z, b0, b1 in (("c", 8, 16), ("a", 0, 8)) if last and not h else ((ab, 16 * h, 16 * h + 16),):
                for e in range(4):
                    j, d = e // M, e % M
                    out = buf[:, first + 64 * b0 + e:first + 64 * b1:4]
                    src = win(t, j)[:, 0:HW + 4 * C - j * M].indirect(T.soff[:, 32 * d + b0:32 * d + b1])
                    op("g%s%d" % (z, e), t, "g" + z, ["ee%d" % j, "of%d%d" % (h, d)] + (["cp%d" % t] if j else []),
                       lambda q, out=out, src=src: [copy(q, out, src)])
                op("q" + z, t + 1, "q" + z, ["g%s.%d" % (z, t)], lambda q, b0=b0, b1=b1: [quant(t + 1, 16 * b0, 16 * b1)])
        for i, (lo, hi) in enumerate(PIECES):
            op("ls%d" % i, t, "ls", ["of%d0" % (lo // 16), "io4.0"], lambda q, lo=lo, hi=hi: [
                (w(q, "ls"), V.tensor_copy(T.lst[:].indirect(T.soff[:, lo:hi]), T.places[:, 16 * lo:16 * hi]))[1]])

        if t == 0:
            op("qin", t, "qin", ["la"], lambda q: [V.quantize_mx(T.inq0[:], T.ins0[:], T.ab[:])])
            op("qv", t, "qv", ["lv"], lambda q: [V.quantize_mx(T.vq[:], T.vs[:], T.vb[:])])
        free = ["sg3", "m3", "ma", "su0", "su1", "mv", "md"]
        op("rr", t, "rr", free + (["qin", "lw"] if t == 0 else ["arr%d%s" % (t, old)]), lambda q: [
            PE.matmul_mx(T["pr%d" % b][:, 0:K], T.wq[:, 128 * b:128 * b + 128], T.wp[:, 128 * b:128 * b + 128],
                         T["inq%d" % t][:], T["ins%d" % t][:], True, True) for b in range(4)])
        for b in range(4):
            out, src = win(t, b // M)[:, b % M:HW:M], T["pr%d" % b][:, 0:K]
            op("e%d" % b, t, "ee%d" % (b // M), ["rr"], lambda q, out=out, src=src: [
                S.activation(out, src, F.Relu, scale=0.03125) if q == "s" else V.tensor_scalar(out, src, 0.0, 0.03125, A.max, A.mult)])

        if not last:
            u = t + 1
            for h in range(2):
                op("cp%d" % h, u, "cp%d" % u, ["g%s.%d" % ("ab"[h], t)], lambda q, h=h: [
                    SY.dma_start(win(u, j)[:, HW + max(4 * h * H2 - j * M, 0):HW + 4 * (h + 1) * H2 - j * M],
                                 win(u)[:, HW + max(4 * h * H2, j * M):HW + 4 * (h + 1) * H2]) for j in range(1, NC)])
            vic, pq, ps = T["vic%d" % t], T["pq%d" % t], T["ps%dc" % t]
            op("lm", t, "lm", ["ls"], lambda q: [V.tensor_tensor_scan(T.lm[:], T.lst[:, 0:HW:M], T.m4[:], 0.0, A.max, A.mult)])
            op("lz", t, "lz", ["lm"], lambda q: [V.tensor_tensor_scan(T.lz[:], T.k4[:], T.lm[:], 0.0, A.mult, A.add)])
            op("vo", t, "vo", ["lz"], lambda q: [V.tensor_scalar(T.voff[:], T.lz[:, 3:K:4], 4.0, T.pf[:, 1:2], A.mult, A.add)])
            op("vg", t, "vg", ["vo"], lambda q: [copy(q, vic[:], win(t)[:, HW:HW + 4 * C].indirect(T.voff[:, 0:40]))])
            op("qp", t, "qp", ["vg"], lambda q: [V.quantize_mx(pq[:], ps[:], vic[:])])

            def send(q):
                arr = T.sem["arr%d" % u]
                g.remote_dma(T["inq%d" % u][:].bitcast(dt.uint8), pq[:].bitcast(dt.uint8), arr, T.sem.sent, pid, rid, emask)
                g.remote_dma(T["ins%d" % u][:], ps[:], arr, T.sem.sent, pid, rid, emask)
                cnt["sent"] = cnt.get("sent", 0) + 2 * n_out
                cnt["arr%d" % u] = 2 * n_in
                return []

            op("send", t, "arr%d" % u, ["qp"], send)
        else:
            xq, xs = T["xq%d" % R], T["xs%d" % R]
            for h, ps, lo, hi in ((0, T.ps1, 0, 128), (1, T.psa, H2, C), (2, T.ps2, 128, H2)):
                qn = "q" + "abc"[h]
                op("ym%d" % h, R, "ym%d" % h, [qn, "qv.0"], lambda q, ps=ps, lo=lo, hi=hi: [
                    PE.matmul_mx(ps[:, 0:hi - lo], T.vq[:], T.vs[:], xq[:, lo:hi], xs[:, lo:hi], True, True)])
                op("yc%d" % h, R, "yc%d" % h, ["ym%d" % h], lambda q, ps=ps, lo=lo, hi=hi: [copy(q, T.ysb[:, lo:hi], ps[:, 0:hi - lo])])
                op("yd%d" % h, R, "st2", ["yc%d" % h], lambda q, lo=lo, hi=hi: [queues[q].dma_start(T.y[:, lo:hi], T.ysb[:, lo:hi])])
                op("oc%d" % h, R, "st1", [qn], lambda q, lo=lo, hi=hi: [
                    queues[q].dma_start(T.oc[:, 4 * lo:4 * hi], xq[:, lo:hi].bitcast(dt.uint8))])
            op("osc", R, "st1", ["qa", "qb", "qc"], lambda q: [
                queues[q].dma_start(T.osc[4 * k:4 * k + 4, :], xs[32 * k:32 * k + 4, :]) for k in range(4)])
            op("oz", R, "oz", ["ls.%d" % t], lambda q: [copy(q, T.olb[:], T.lst[:, 0:HW:M])])
            op("ol", R, "st1", ["oz"], lambda q: [queues[q].dma_start(T.ol[:], T.olb[0:128:16, :])])

    for t in range(R):
        describe(t)

    todo = {q: ORDER[q].split() for q in ORDER}
    left = {}
    for name in ops:
        left[ops[name][0]] = left.get(ops[name][0], 0) + 1
    for _ in range(len(ops)):
        for q in todo:
            while todo[q] and not any(left.get(n, 0) for n in ops[todo[q][0]][1]):
                sem, needs, call = ops[todo[q].pop(0)]
                w(q, *[n.split(".")[0] for n in needs])
                for ins in call(q):
                    ev(sem.split(".")[0], ins, 16 if sem[:2] in ("cp", "st") else 1)
                left[sem] -= 1
    assert not any(left.values()), [(q, todo[q][0]) for q in todo if todo[q]]

    for name in sorted(cnt):
        if max([v for (q, n), v in seen.items() if n == name] + [0]) < cnt[name]:
            w("g", name)
